import numpy as np
import ml_dtypes


def mxq(x, axis, fmt="e4m3"):
    dtype, down = {"e4m3": (ml_dtypes.float8_e4m3fn, 7), "e5m2": (ml_dtypes.float8_e5m2, 14)}[fmt]
    v = np.moveaxis(np.asarray(x, np.float32).astype(ml_dtypes.bfloat16).astype(np.float64), axis, -1)
    blocks = v.reshape(v.shape[:-1] + (-1, 32))
    amax = np.abs(blocks).max(-1, keepdims=True)
    byte = np.maximum(np.where(amax > 0, np.frexp(amax)[1] - 1 + 127, 0) - down, 1)
    scale = np.exp2(byte - 127.0)
    codes = (blocks / scale).astype(np.float32).astype(dtype).astype(np.float64)
    return np.moveaxis((codes * scale).reshape(v.shape), -1, axis)


WIDE = False


def mx_kscale(k):
    if not WIDE:
        return np.ones(k)
    levels = np.array([10, -10, 5, -5, 0])
    if k % 512:
        return np.exp2(np.random.permutation(np.resize(levels, k // 32))).repeat(32)
    a = np.empty((k // 512, 16))
    for p in range(k // 512):
        a[p, :8] = np.random.permutation(np.resize(levels, 8))
        for g in range(8):
            far = levels[np.abs(levels - a[p, g]) >= 10]
            a[p, g + 8] = far[np.random.randint(len(far))]
    return np.exp2(a.ravel()).repeat(32)


def f64(x):
    return np.asarray(x).astype(np.float64)


def striped(idx):
    return np.tile(idx.reshape(-1, 16).T, (8, 1)).astype(np.uint16)


def unstriped(offs):
    return offs[:16].T.reshape(-1).astype(np.int64)


E2M1 = np.array([0.0, 0.5, 1.0, 1.5, 2.0, 3.0, 4.0, 6.0, -0.0, -0.5, -1.0, -1.5, -2.0, -3.0, -4.0, -6.0])


def pack_weight(w, fmt):
    k, n = w.shape
    w = f64(np.asarray(w, np.float32).astype(ml_dtypes.bfloat16)).reshape(k // 32, 32, n)
    amax = np.abs(w).max(1)
    if fmt == "e4m3":
        byte = np.frexp(amax)[1] - 1 + 127 - 7
    else:
        mant, ex = np.frexp(amax / 6.0)
        byte = np.where(mant > 0.5, ex, ex - 1) + 127
    byte = np.clip(np.where(amax > 0, byte, 1), 1, 254)
    scaled = (w * np.exp2(127.0 - byte)[:, None, :]).reshape(k, n).astype(np.float32)
    by_word = np.ascontiguousarray(scaled.reshape(k // 512, 128, 4, n).transpose(0, 1, 3, 2))
    if fmt == "e4m3":
        words = by_word.astype(ml_dtypes.float8_e4m3fn).view(np.uint8)
    else:
        c = by_word.astype(ml_dtypes.float4_e2m1fn).view(np.uint8) & 0xF
        words = (c[..., 0::2] | (c[..., 1::2] << 4)).reshape(k // 512, 128, 2 * n)
    return np.ascontiguousarray(words), np.ascontiguousarray(byte.astype(np.uint8).reshape(k // 512, 16, n))


def unpack_weight(words, scales, fmt):
    g, _, n = scales.shape
    words = np.ascontiguousarray(words).reshape(g, 128, n, -1)
    if fmt == "e4m3":
        vals = words.view(ml_dtypes.float8_e4m3fn).astype(np.float64)
    else:
        nib = np.empty((g, 128, n, 4), np.uint8)
        nib[..., 0::2] = words & 0xF
        nib[..., 1::2] = words >> 4
        vals = E2M1[nib]
    vals = vals * np.repeat(np.exp2(scales.astype(np.float64) - 127.0), 8, axis=1)[..., None]
    return vals.transpose(0, 1, 3, 2).reshape(g * 512, n)


def gelu(v):
    return 0.5 * v * (1.0 + np.tanh(np.sqrt(2.0 / np.pi) * (v + 0.044715 * v**3)))


def bf(x):
    return np.asarray(x, np.float32).astype(ml_dtypes.bfloat16)


def planes(Y):
    n, m = Y.shape
    b = f64(bf(Y)).reshape(n // 32, 32, m)
    amax = np.abs(b).max(1)
    byte = np.clip(np.where(amax > 0, np.frexp(amax)[1] - 1 + 127 - 7, 1), 1, 254)
    codes = (b * np.exp2(127.0 - byte)[:, None, :]).reshape(n, m).astype(np.float32).astype(ml_dtypes.float8_e4m3fn).view(np.uint8)
    words = codes.reshape(n // 512, 128, 4, m).transpose(0, 1, 3, 2)
    return np.ascontiguousarray(words), np.ascontiguousarray(byte.astype(np.uint8).reshape(n // 512, 16, m))


K, K2, H, N, T, S, T2 = 1024, 512, 1024, 512, 4096, 1024, 2048

def setup_inputs():
    n = np.random.standard_normal
    s, s2, u = mx_kscale(K)[:, None], mx_kscale(K2)[:, None], mx_kscale(H)[:, None]
    tab_words, tab_scales = pack_weight(n((K, T)) * s, "e4m3")
    w4_words, w4_scales = pack_weight(n((K, H)) / np.sqrt(K) / s, "e2m1")
    w8_words, w8_scales = pack_weight(n((H, N)) / np.sqrt(H) / u, "e4m3")
    return {
        "tab_words": tab_words, "tab_scales": tab_scales,
        "offs": striped(np.random.permutation(T)[:S]),
        "w4_words": w4_words, "w4_scales": w4_scales,
        "wc": (n((K2, H)) / np.sqrt(K2) / s2).astype(np.float32),
        "scene": (n((K2, S)) * s2).astype(np.float32),
        "gain": (np.random.uniform(0.7, 1.5, H) * u[:, 0]).astype(np.float32),
        "page0": (n((H, T2)) * u).astype(np.float32),
        "offs2": striped(np.random.permutation(T2)[:S]),
        "wgs": np.exp(0.3 * n((128, S))).astype(np.float32),
        "w8_words": w8_words, "w8_scales": w8_scales,
        "bias": n((N, T2)).astype(np.float32),
    }

def reference(tab_words, tab_scales, offs, w4_words, w4_scales, wc, scene, gain, page0, offs2, wgs, w8_words, w8_scales, bias):
    v = unpack_weight(tab_words, tab_scales, "e4m3")[:, unstriped(offs)]
    w4 = unpack_weight(w4_words, w4_scales, "e2m1")
    a = w4.T @ v + mxq(f64(wc), 0, "e4m3").T @ mxq(f64(scene), 0, "e4m3")
    h = 0.5 * a * (1.0 + np.tanh(np.sqrt(2.0 / np.pi) * (a + 0.044715 * a * a * a))) * f64(gain)[:, None]
    page = f64(page0).copy()
    page[:, unstriped(offs2)] = np.tile(f64(wgs), (H // 128, 1)) * h
    w8 = unpack_weight(w8_words, w8_scales, "e4m3")
    y = (w8.T @ mxq(page, 0, "e4m3")) + f64(bias)
    words, scales = planes(page)
    return y, page, words, scales

@@ -1,0 +1,268 @@
+from contextlib import ExitStack
+
+import concourse.mybir as mybir
+from concourse.masks import make_identity
+
+F32 = mybir.dt.float32
+BF16 = mybir.dt.bfloat16
+I32 = mybir.dt.int32
+U32 = mybir.dt.uint32
+U16 = mybir.dt.uint16
+U8 = mybir.dt.uint8
+FP8X4 = mybir.dt.float8_e4m3fn_x4
+FP4X4 = mybir.dt.float4_e2m1fn_x4
+ACT = mybir.ActivationFunctionType
+ALU = mybir.AluOpType
+
+P = 128
+H, N, T, S, T2 = 1024, 512, 4096, 1024, 2048
+BANK = 512
+ROW_TILES = H // P
+CHUNKS = T2 // BANK
+EARLY_TILES = 4
+FLOPS = 5368709120
+
+
+def tile_list_narrator_prefix_cache_kernel(
+    tc, tab_words, tab_scales, offs, w4_words, w4_scales, wc, scene, gain, page0, offs2, wgs,
+    w8_words, w8_scales, bias, out_0, out_1, out_2, out_3,
+):
+    nc = tc.nc
+    with ExitStack() as ctx:
+        lists = ctx.enter_context(tc.tile_pool(name="lists", bufs=1))
+        keep = ctx.enter_context(tc.tile_pool(name="keep", bufs=1))
+        mx_banks = ctx.enter_context(tc.psum_pool(name="mx_banks", bufs=4))
+        turn_banks = ctx.enter_context(tc.psum_pool(name="turn_banks", bufs=2))
+        back_banks = ctx.enter_context(tc.psum_pool(name="back_banks", bufs=2))
+
+        wc_ranges = [(0, EARLY_TILES * P), (EARLY_TILES * P, H)]
+        halves = [slice(0, BANK), slice(BANK, S)]
+        list_halves = [slice(0, BANK // 16), slice(BANK // 16, S // 16)]
+
+        tab_scale_rows = keep.tile([P, 2, T], U8, tag="picking", align_bytes=64)
+        w4_scale = keep.tile([P, 2, H], U8, align_bytes=64)
+        w8_scale = keep.tile([P, 2, N], U8, align_bytes=64)
+        gain_rows = keep.tile([P, P], F32)
+        ident = keep.tile([P, P], F32)
+        nc.vector.memset(tab_scale_rows[:].bitcast(I32), 0)
+        nc.vector.memset(w4_scale[:].bitcast(I32), 0)
+        nc.vector.memset(w8_scale[:].bitcast(I32), 0)
+        for q in range(4):
+            nc.gpsimd.dma_start(out=tab_scale_rows[32 * q : 32 * q + 4, :, :].bitcast(I32),
+                                in_=tab_scales[:, 4 * q : 4 * q + 4, :].rearrange("a q t -> q a t").bitcast(I32))
+        for q in range(4):
+            nc.gpsimd.dma_start(out=w4_scale[32 * q : 32 * q + 4, :, :].bitcast(I32),
+                                in_=w4_scales[:, 4 * q : 4 * q + 4, :].rearrange("a q c -> q a c").bitcast(I32))
+        nc.gpsimd.memset(gain_rows[:], 0.0)
+        nc.scalar.dma_start(out=gain_rows[0:ROW_TILES, :], in_=gain.rearrange("(c p) -> c p", p=P))
+        make_identity(nc, ident[:])
+
+        picks = lists.tile([P, S // 16], U16)
+        slots = lists.tile([P, S // 16], U16)
+        scene_rows = scene.rearrange("(p j) s -> p j s", j=4)
+        wc_rows = wc.rearrange("(p j) c -> p j c", j=4)
+        scene_raw = [keep.tile([P, 4, BANK], F32, name=f"scene_raw{i}") for i in range(2)]
+        wc_raw = [keep.tile([P, 4, b - a], F32, name=f"wc_raw{i}") for i, (a, b) in enumerate(wc_ranges)]
+        tab = [keep.tile([P, T], I32, name=f"tab{a}", tag=f"big{a}") for a in range(2)]
+        w4 = keep.tile([P, 2, 2 * H], U8, align_bytes=64)
+        wgs_sb = keep.tile([P, S], F32)
+        page = [keep.tile([P, T2], F32, name=f"page{c}") for c in range(ROW_TILES)]
+        w8 = keep.tile([P, 2, N], I32, align_bytes=64)
+
+        def load_page(c):
+            nc.sync.dma_start(out=page[c][:], in_=page0[c * P : (c + 1) * P, :])
+
+        nc.sync.dma_start(picks[:], offs)
+        nc.sync.dma_start(slots[:], offs2)
+        nc.sync.dma_start(out=scene_raw[0][:], in_=scene_rows[:, :, halves[0]])
+        nc.sync.dma_start(out=wc_raw[0][:], in_=wc_rows[:, :, wc_ranges[0][0] : wc_ranges[0][1]])
+        for a in range(2):
+            nc.sync.dma_start(out=tab[a][:], in_=tab_words[a].rearrange("p t i -> p (t i)").bitcast(I32))
+        nc.sync.dma_start(out=w4[:].bitcast(I32), in_=w4_words.rearrange("a p c -> p a c").bitcast(I32))
+        nc.sync.dma_start(out=wgs_sb[:, halves[0]], in_=wgs[:, halves[0]])
+        load_page(0)
+        nc.sync.dma_start(out=scene_raw[1][:], in_=scene_rows[:, :, halves[1]])
+        for c in range(1, EARLY_TILES):
+            load_page(c)
+        nc.sync.dma_start(out=wc_raw[1][:], in_=wc_rows[:, :, wc_ranges[1][0] : wc_ranges[1][1]])
+        load_page(EARLY_TILES)
+        nc.sync.dma_start(out=wgs_sb[:, halves[1]], in_=wgs[:, halves[1]])
+        for c in range(EARLY_TILES + 1, ROW_TILES):
+            load_page(c)
+        nc.sync.dma_start(out=w8[:], in_=w8_words.rearrange("a p c i -> p a (c i)").bitcast(I32))
+        for q in range(4):
+            nc.sync.dma_start(out=w8_scale[32 * q : 32 * q + 4, :, :].bitcast(I32),
+                                in_=w8_scales[:, 4 * q : 4 * q + 4, :].rearrange("a q c -> q a c").bitcast(I32))
+
+        gain_bank = turn_banks.tile([P, 4, P], F32, name="turn_bank", tag="turn_bank")
+        nc.tensor.transpose(gain_bank[:, 0, :], gain_rows[:], ident[:])
+        gain_cols = keep.tile([P, ROW_TILES], F32)
+        nc.scalar.copy(gain_cols[:], gain_bank[:, 0, 0:ROW_TILES])
+
+        def quantise_operand(raw, width, name, tag):
+            woven = keep.tile([P, width, 4], BF16, name=name + "_woven", tag=tag, align_bytes=64)
+            nc.scalar.copy(woven[:].rearrange("p (c i) j -> p c j i", i=4),
+                           raw[:].rearrange("p j (c i) -> p c j i", i=4))
+            codes = keep.tile([P, width], U32, name=name + "_codes", align_bytes=64)
+            scale = keep.tile([P, width], U8, name=name + "_scale", align_bytes=64)
+            start = 0
+            while start < width:
+                step = max(w for w in (128, 256, 512) if w <= width - start)
+                cols = slice(start, start + step)
+                nc.vector.quantize_mx(out=codes[:, cols].bitcast(FP8X4), scales=scale[:, cols],
+                                      in_=woven[:, cols, :].rearrange("p c j -> p (c j)"))
+                start += step
+            return codes, scale
+
+        scene_q = [quantise_operand(scene_raw[0], BANK, "scene0", "ring0")]
+        wc_q = [quantise_operand(wc_raw[0], wc_ranges[0][1], "wc0", "ring1")]
+
+        picked_scale = [keep.tile([P, S], U8, name=f"picked_scale{a}", align_bytes=64) for a in range(2)]
+        for a in range(2):
+            nc.vector.tensor_copy(picked_scale[a][:], tab_scale_rows[:, a, :].indirect(picks[:]))
+        picked = keep.tile([P, 2, S], U32, tag="picking", align_bytes=64)
+        for a in range(2):
+            for i in range(2):
+                nc.vector.tensor_copy(picked[:, a, halves[i]], tab[a][:].bitcast(U32).indirect(picks[:, list_halves[i]]))
+
+        result_pairs = [keep.tile([P, 2, N // P, BANK], F32, name=f"result{i}", tag=f"big{i}") for i in range(2)]
+        result = [result_pairs[k // 2][:, k % 2, :, :] for k in range(CHUNKS)]
+        bias_rows = bias.rearrange("(n p) t -> p n t", p=P)
+        out_rows = out_0.rearrange("(n p) t -> p n t", p=P)
+        for k in range(CHUNKS):
+            nc.sync.dma_start(out=result[k], in_=bias_rows[:, :, k * BANK : (k + 1) * BANK])
+
+        hidden = {}
+
+        def first_stage(c, i):
+            if c not in hidden:
+                hidden.setdefault(c, keep.tile([P, S], F32, name=f"hidden{c}", tag=f"hidden{c % 5}", align_bytes=64))
+            part = 0 if c < EARLY_TILES else 1
+            wc_cols = slice(c * P - wc_ranges[part][0], (c + 1) * P - wc_ranges[part][0])
+            bank = mx_banks.tile([P, BANK], F32, name="mx_bank", tag="mx_bank")
+            nc.tensor.matmul_mx(out=bank[:], lhsT=wc_q[part][0][:, wc_cols].bitcast(FP8X4),
+                                lhsT_scale=wc_q[part][1][:, wc_cols],
+                                rhs=scene_q[i][0][:].bitcast(FP8X4), rhs_scale=scene_q[i][1][:],
+                                start=True, stop=False)
+            for a in range(2):
+                nc.tensor.matmul_mx(out=bank[:], lhsT=w4[:, a, 2 * c * P : 2 * (c + 1) * P].bitcast(FP4X4),
+                                    lhsT_scale=w4_scale[:, a, c * P : (c + 1) * P],
+                                    rhs=picked[:, a, halves[i]].bitcast(FP8X4), rhs_scale=picked_scale[a][:, halves[i]],
+                                    start=False, stop=(a == 1))
+            nc.scalar.activation(hidden[c][:, halves[i]], bank[:], ACT.Gelu_apprx_tanh)
+
+        def apply_gain(c, cols):
+            nc.scalar.activation(hidden[c][:, cols], hidden[c][:, cols], ACT.Copy, scale=gain_cols[:, c : c + 1])
+
+        def apply_gain_late(c):
+            gained = keep.tile([P, S], F32, name=f"gained{c}", tag=f"ring{c - 5}", align_bytes=64)
+            nc.scalar.activation(gained[:], hidden[c][:], ACT.Copy, scale=gain_cols[:, c : c + 1])
+            hidden.update({c: gained})
+
+        def scatter(c, cols, list_cols):
+            nc.vector.tensor_tensor(page[c][:].indirect(slots[:, list_cols]), hidden[c][:, cols], wgs_sb[:, cols], ALU.mult)
+
+        def scatter_whole(c):
+            scatter(c, slice(0, S), slice(0, S // 16))
+
+        def store_page(c):
+            nc.sync.dma_start(out=out_1[c * P : (c + 1) * P, :], in_=page[c][:])
+
+        turned = {}
+
+        def turn(c, k):
+            g, quarter = divmod(c, 4)
+            if (g, k) not in turned:
+                turned.setdefault((g, k), keep.tile([P, 4, 2, 2 * P], BF16, name=f"turned{g}{k}", tag=f"turned{k}"))
+            bank = turn_banks.tile([P, 4, P], F32, name="turn_bank", tag="turn_bank")
+            for b in range(4):
+                nc.tensor.transpose(bank[:, b, :], page[c][:, k * BANK + b * P : k * BANK + (b + 1) * P], ident[:])
+            nc.scalar.copy(
+                turned[(g, k)][:, :, :, 64 * quarter : 64 * (quarter + 1)].rearrange("s b u (p e) -> s b u p e", e=2),
+                bank[:].rearrange("s b (p u e) -> s b u p e", u=2, e=2))
+
+        page_codes = [keep.tile([P, T2], I32, name=f"page_codes{g}", align_bytes=64) for g in range(2)]
+        page_scale = [keep.tile([P, T2], U8, name=f"page_scale{g}", align_bytes=64) for g in range(2)]
+
+        def quantise_page(g, k):
+            pairs = turned[(g, k)][:].rearrange("s b u w -> s (b u w)").bitcast(F32)
+            woven = keep.tile([P, BANK, 4], BF16, name=f"woven{g}{k}", tag=("ring", "hidden")[g] + str(k), align_bytes=64)
+            woven_flat = woven[:].rearrange("p s j -> p (s j)")
+            woven_pairs = woven_flat.bitcast(F32)
+            for half in range(2):
+                bank = back_banks.tile([P, 2, 2, P], F32, name="back_bank", tag="back_bank")
+                for b in range(2):
+                    for u in range(2):
+                        at = ((2 * half + b) * 2 + u) * P
+                        nc.tensor.transpose(bank[:, b, u, :], pairs[:, at : at + P], ident[:])
+                nc.scalar.copy(
+                    woven_pairs[:, half * BANK : (half + 1) * BANK].rearrange("p (b s u) -> p b s u", b=2, u=2),
+                    bank[:].rearrange("p b u s -> p b s u"))
+            cols = slice(k * BANK, (k + 1) * BANK)
+            nc.vector.quantize_mx(out=page_codes[g][:, cols].bitcast(FP8X4), scales=page_scale[g][:, cols], in_=woven_flat)
+
+        def store_codes(g, cols):
+            nc.sync.dma_start(out=out_2[g].rearrange("p m t -> p (m t)").bitcast(I32)[:, cols], in_=page_codes[g][:, cols])
+
+        def store_scales(g):
+            for q in range(4):
+                nc.sync.dma_start(out=out_3[g, 4 * q : 4 * q + 4, :].bitcast(I32),
+                                  in_=page_scale[g][32 * q : 32 * q + 4, :].bitcast(I32))
+
+        def second_stage(k):
+            cols = slice(k * BANK, (k + 1) * BANK)
+            for n in range(N // P):
+                bank = mx_banks.tile([P, BANK], F32, name="mx_bank", tag="mx_bank")
+                for g in range(2):
+                    nc.tensor.matmul_mx(out=bank[:], lhsT=w8[:, g, n * P : (n + 1) * P].bitcast(FP8X4),
+                                        lhsT_scale=w8_scale[:, g, n * P : (n + 1) * P],
+                                        rhs=page_codes[g][:, cols].bitcast(FP8X4), rhs_scale=page_scale[g][:, cols],
+                                        start=(g == 0), stop=(g == 1))
+                nc.vector.tensor_tensor(result[k][:, n, :], bank[:], result[k][:, n, :], ALU.add)
+                if k == CHUNKS - 1:
+                    nc.sync.dma_start(out=out_rows[:, n, cols], in_=result[k][:, n, :])
+                elif n % 2 == 1:
+                    nc.sync.dma_start(out=out_rows[:, n - 1 : n + 1, cols], in_=result[k][:, n - 1 : n + 1, :])
+
+        for c in range(EARLY_TILES):
+            first_stage(c, 0)
+            apply_gain(c, halves[0])
+            scatter(c, halves[0], list_halves[0])
+        scene_q.append(quantise_operand(scene_raw[1], BANK, "scene1", "ring2"))
+        wc_q.append(quantise_operand(wc_raw[1], wc_ranges[1][1] - wc_ranges[1][0], "wc1", "ring3"))
+        for c in range(EARLY_TILES):
+            first_stage(c, 1)
+            apply_gain(c, halves[1])
+        first_stage(4, 0)
+        first_stage(4, 1)
+        apply_gain(4, slice(0, S))
+        for c in range(EARLY_TILES):
+            scatter(c, halves[1], list_halves[1])
+            store_page(c)
+            if c < 3:
+                first_stage(c + 5, 0)
+                first_stage(c + 5, 1)
+            for k in range(CHUNKS):
+                turn(c, k)
+                if c == 3:
+                    quantise_page(0, k)
+        for c in range(5, ROW_TILES):
+            apply_gain_late(c)
+        for c in range(4, 7):
+            scatter_whole(c)
+            store_page(c)
+            for k in range(CHUNKS):
+                turn(c, k)
+        store_codes(0, slice(0, T2))
+        store_scales(0)
+        scatter_whole(7)
+        store_page(7)
+        for k in range(CHUNKS + 1):
+            if k < CHUNKS:
+                turn(7, k)
+                quantise_page(1, k)
+                store_codes(1, slice(k * BANK, (k + 1) * BANK))
+            if k == CHUNKS - 1:
+                store_scales(1)
+            if k > 0:
+                second_stage(k - 1)

@@ -35,7 +35,7 @@ def tile_list_narrator_prefix_cache_kernel(
         turn_banks = ctx.enter_context(tc.psum_pool(name="turn_banks", bufs=2))
         back_banks = ctx.enter_context(tc.psum_pool(name="back_banks", bufs=2))
 
-        wc_ranges = [(0, EARLY_TILES * P), (EARLY_TILES * P, H)]
+        wc_ranges = [(0, 2 * P), (2 * P, 4 * P), (4 * P, H)]
         halves = [slice(0, BANK), slice(BANK, S)]
         list_halves = [slice(0, BANK // 16), slice(BANK // 16, S // 16)]
 
@@ -44,27 +44,26 @@ def tile_list_narrator_prefix_cache_kernel(
         w8_scale = keep.tile([P, 2, N], U8, align_bytes=64)
         gain_rows = keep.tile([P, P], F32)
         ident = keep.tile([P, P], F32)
-        nc.vector.memset(tab_scale_rows[:].bitcast(I32), 0)
+        nc.vector.memset(tab_scale_rows[:, 0, :].bitcast(I32), 0)
+        nc.gpsimd.memset(tab_scale_rows[:, 1, :].bitcast(I32), 0)
         nc.vector.memset(w4_scale[:].bitcast(I32), 0)
         nc.vector.memset(w8_scale[:].bitcast(I32), 0)
-        for q in range(4):
-            nc.gpsimd.dma_start(out=tab_scale_rows[32 * q : 32 * q + 4, :, :].bitcast(I32),
-                                in_=tab_scales[:, 4 * q : 4 * q + 4, :].rearrange("a q t -> q a t").bitcast(I32))
-        for q in range(4):
-            nc.gpsimd.dma_start(out=w4_scale[32 * q : 32 * q + 4, :, :].bitcast(I32),
-                                in_=w4_scales[:, 4 * q : 4 * q + 4, :].rearrange("a q c -> q a c").bitcast(I32))
         nc.gpsimd.memset(gain_rows[:], 0.0)
         nc.scalar.dma_start(out=gain_rows[0:ROW_TILES, :], in_=gain.rearrange("(c p) -> c p", p=P))
         make_identity(nc, ident[:])
+        warm = keep.tile([P, 1], F32)
+        nc.scalar.activation(warm[:], ident[:, 0:1], ACT.Gelu_apprx_tanh)
 
         picks = lists.tile([P, S // 16], U16)
         slots = lists.tile([P, S // 16], U16)
         scene_rows = scene.rearrange("(p j) s -> p j s", j=4)
         wc_rows = wc.rearrange("(p j) c -> p j c", j=4)
-        scene_raw = [keep.tile([P, 4, BANK], F32, name=f"scene_raw{i}") for i in range(2)]
-        wc_raw = [keep.tile([P, 4, b - a], F32, name=f"wc_raw{i}") for i, (a, b) in enumerate(wc_ranges)]
+        scene_first = [keep.tile([P, 4, BANK // 2], F32, name=f"scene_first{i}", tag=f"scene_first{i}", align_bytes=64)
+                       for i in range(2)]
+        scene_second = keep.tile([P, 4, BANK], F32, tag="scene_second", align_bytes=64)
+        wc_raw = [keep.tile([P, 4, b - a], F32, name=f"wc_raw{i}", tag=f"wc_raw{i}", align_bytes=64) for i, (a, b) in enumerate(wc_ranges)]
         tab = [keep.tile([P, T], I32, name=f"tab{a}", tag=f"big{a}") for a in range(2)]
-        w4 = keep.tile([P, 2, 2 * H], U8, align_bytes=64)
+        w4 = [keep.tile([P, 2, H], U8, name=f"w4_{i}", align_bytes=64) for i in range(2)]
         wgs_sb = keep.tile([P, S], F32)
         page = [keep.tile([P, T2], F32, name=f"page{c}") for c in range(ROW_TILES)]
         w8 = keep.tile([P, 2, N], I32, align_bytes=64)
@@ -72,22 +71,42 @@ def tile_list_narrator_prefix_cache_kernel(
         def load_page(c):
             nc.sync.dma_start(out=page[c][:], in_=page0[c * P : (c + 1) * P, :])
 
+        def load_table(a, cols):
+            nc.sync.dma_start(out=tab[a][:, cols], in_=tab_words[a].rearrange("p t i -> p (t i)").bitcast(I32)[:, cols])
+
+        def load_wc(part):
+            nc.sync.dma_start(out=wc_raw[part][:], in_=wc_rows[:, :, wc_ranges[part][0] : wc_ranges[part][1]])
+
+        def load_w4(i):
+            nc.sync.dma_start(out=w4[i][:].bitcast(I32),
+                              in_=w4_words.rearrange("a p c -> p a c")[:, :, i * H : (i + 1) * H].bitcast(I32))
+
         nc.sync.dma_start(picks[:], offs)
         nc.sync.dma_start(slots[:], offs2)
-        nc.sync.dma_start(out=scene_raw[0][:], in_=scene_rows[:, :, halves[0]])
-        nc.sync.dma_start(out=wc_raw[0][:], in_=wc_rows[:, :, wc_ranges[0][0] : wc_ranges[0][1]])
-        for a in range(2):
-            nc.sync.dma_start(out=tab[a][:], in_=tab_words[a].rearrange("p t i -> p (t i)").bitcast(I32))
-        nc.sync.dma_start(out=w4[:].bitcast(I32), in_=w4_words.rearrange("a p c -> p a c").bitcast(I32))
+        load_table(0, slice(0, T // 4))
+        for q in range(4):
+            nc.sync.dma_start(out=tab_scale_rows[32 * q : 32 * q + 4, :, :].bitcast(I32),
+                                in_=tab_scales[:, 4 * q : 4 * q + 4, :].rearrange("a q t -> q a t").bitcast(I32))
+        load_table(0, slice(T // 4, T))
+        load_table(1, slice(0, T))
+        for q in range(4):
+            nc.sync.dma_start(out=w4_scale[32 * q : 32 * q + 4, :, :].bitcast(I32),
+                                in_=w4_scales[:, 4 * q : 4 * q + 4, :].rearrange("a q c -> q a c").bitcast(I32))
+        load_w4(0)
+        load_wc(0)
+        for i in range(2):
+            nc.sync.dma_start(out=scene_first[i][:], in_=scene_rows[:, :, i * BANK // 2 : (i + 1) * BANK // 2])
         nc.sync.dma_start(out=wgs_sb[:, halves[0]], in_=wgs[:, halves[0]])
         load_page(0)
-        nc.sync.dma_start(out=scene_raw[1][:], in_=scene_rows[:, :, halves[1]])
-        for c in range(1, EARLY_TILES):
-            load_page(c)
-        nc.sync.dma_start(out=wc_raw[1][:], in_=wc_rows[:, :, wc_ranges[1][0] : wc_ranges[1][1]])
-        load_page(EARLY_TILES)
+        load_wc(1)
+        load_page(1)
+        nc.sync.dma_start(out=scene_second[:], in_=scene_rows[:, :, halves[1]])
+        load_page(2)
+        load_page(3)
         nc.sync.dma_start(out=wgs_sb[:, halves[1]], in_=wgs[:, halves[1]])
-        for c in range(EARLY_TILES + 1, ROW_TILES):
+        load_wc(2)
+        load_w4(1)
+        for c in range(EARLY_TILES, ROW_TILES):
             load_page(c)
         nc.sync.dma_start(out=w8[:], in_=w8_words.rearrange("a p c i -> p a (c i)").bitcast(I32))
         for q in range(4):
@@ -99,23 +118,19 @@ def tile_list_narrator_prefix_cache_kernel(
         gain_cols = keep.tile([P, ROW_TILES], F32)
         nc.scalar.copy(gain_cols[:], gain_bank[:, 0, 0:ROW_TILES])
 
-        def quantise_operand(raw, width, name, tag):
+        def quantise_operand(pieces, name, tag):
+            width = sum(raw.shape[2] for raw, copy in pieces)
             woven = keep.tile([P, width, 4], BF16, name=name + "_woven", tag=tag, align_bytes=64)
-            nc.scalar.copy(woven[:].rearrange("p (c i) j -> p c j i", i=4),
-                           raw[:].rearrange("p j (c i) -> p c j i", i=4))
             codes = keep.tile([P, width], U32, name=name + "_codes", align_bytes=64)
             scale = keep.tile([P, width], U8, name=name + "_scale", align_bytes=64)
             start = 0
-            while start < width:
-                step = max(w for w in (128, 256, 512) if w <= width - start)
-                cols = slice(start, start + step)
+            for raw, copy in pieces:
+                cols = slice(start, start + raw.shape[2])
+                copy(woven[:, cols, :].rearrange("p (c i) j -> p c j i", i=4), raw[:].rearrange("p j (c i) -> p c j i", i=4))
                 nc.vector.quantize_mx(out=codes[:, cols].bitcast(FP8X4), scales=scale[:, cols],
                                       in_=woven[:, cols, :].rearrange("p c j -> p (c j)"))
-                start += step
+                start += raw.shape[2]
             return codes, scale
-
-        scene_q = [quantise_operand(scene_raw[0], BANK, "scene0", "ring0")]
-        wc_q = [quantise_operand(wc_raw[0], wc_ranges[0][1], "wc0", "ring1")]
 
         picked_scale = [keep.tile([P, S], U8, name=f"picked_scale{a}", align_bytes=64) for a in range(2)]
         for a in range(2):
@@ -125,6 +140,9 @@ def tile_list_narrator_prefix_cache_kernel(
             for i in range(2):
                 nc.vector.tensor_copy(picked[:, a, halves[i]], tab[a][:].bitcast(U32).indirect(picks[:, list_halves[i]]))
 
+        wc_q = [quantise_operand([(wc_raw[0], nc.scalar.copy)], "wc0", "ring1")]
+        scene_q = [quantise_operand([(scene_first[0], nc.vector.tensor_copy), (scene_first[1], nc.scalar.copy)], "scene0", "ring0")]
+
         result_pairs = [keep.tile([P, 2, N // P, BANK], F32, name=f"result{i}", tag=f"big{i}") for i in range(2)]
         result = [result_pairs[k // 2][:, k % 2, :, :] for k in range(CHUNKS)]
         bias_rows = bias.rearrange("(n p) t -> p n t", p=P)
@@ -132,38 +150,43 @@ def tile_list_narrator_prefix_cache_kernel(
         for k in range(CHUNKS):
             nc.sync.dma_start(out=result[k], in_=bias_rows[:, :, k * BANK : (k + 1) * BANK])
 
+        half_tags = {(0, 0): "half0", (1, 0): "wc_raw1", (2, 0): "half1", (3, 0): "scene_second",
+                     (0, 1): "half0", (1, 1): "half1", (2, 1): "wc_raw2", (3, 1): "scene_first0"}
         hidden = {}
 
         def first_stage(c, i):
-            if c not in hidden:
-                hidden.setdefault(c, keep.tile([P, S], F32, name=f"hidden{c}", tag=f"hidden{c % 5}", align_bytes=64))
-            part = 0 if c < EARLY_TILES else 1
+            if c < EARLY_TILES:
+                hidden.update({(c, i): keep.tile([P, BANK], F32, name=f"hidden{c}{i}", tag=half_tags[(c, i)], align_bytes=64)[:]})
+            elif i == 0:
+                whole = keep.tile([P, S], F32, name=f"hidden{c}", tag=f"hidden{c - 4}", align_bytes=64)
+                hidden.update({c: whole[:], (c, 0): whole[:, halves[0]], (c, 1): whole[:, halves[1]]})
+            part = min(c // 2, 2)
             wc_cols = slice(c * P - wc_ranges[part][0], (c + 1) * P - wc_ranges[part][0])
             bank = mx_banks.tile([P, BANK], F32, name="mx_bank", tag="mx_bank")
+            for a in range(2):
+                nc.tensor.matmul_mx(out=bank[:], lhsT=w4[c // 4][:, a, 2 * (c % 4) * P : 2 * (c % 4 + 1) * P].bitcast(FP4X4),
+                                    lhsT_scale=w4_scale[:, a, c * P : (c + 1) * P],
+                                    rhs=picked[:, a, halves[i]].bitcast(FP8X4), rhs_scale=picked_scale[a][:, halves[i]],
+                                    start=(a == 0), stop=False)
             nc.tensor.matmul_mx(out=bank[:], lhsT=wc_q[part][0][:, wc_cols].bitcast(FP8X4),
                                 lhsT_scale=wc_q[part][1][:, wc_cols],
                                 rhs=scene_q[i][0][:].bitcast(FP8X4), rhs_scale=scene_q[i][1][:],
-                                start=True, stop=False)
-            for a in range(2):
-                nc.tensor.matmul_mx(out=bank[:], lhsT=w4[:, a, 2 * c * P : 2 * (c + 1) * P].bitcast(FP4X4),
-                                    lhsT_scale=w4_scale[:, a, c * P : (c + 1) * P],
-                                    rhs=picked[:, a, halves[i]].bitcast(FP8X4), rhs_scale=picked_scale[a][:, halves[i]],
-                                    start=False, stop=(a == 1))
-            nc.scalar.activation(hidden[c][:, halves[i]], bank[:], ACT.Gelu_apprx_tanh)
+                                start=False, stop=True)
+            nc.scalar.activation(hidden[(c, i)], bank[:], ACT.Gelu_apprx_tanh)
 
-        def apply_gain(c, cols):
-            nc.scalar.activation(hidden[c][:, cols], hidden[c][:, cols], ACT.Copy, scale=gain_cols[:, c : c + 1])
+        def apply_gain(c, key):
+            nc.scalar.activation(hidden[key], hidden[key], ACT.Copy, scale=gain_cols[:, c : c + 1])
 
         def apply_gain_late(c):
-            gained = keep.tile([P, S], F32, name=f"gained{c}", tag=f"ring{c - 5}", align_bytes=64)
-            nc.scalar.activation(gained[:], hidden[c][:], ACT.Copy, scale=gain_cols[:, c : c + 1])
-            hidden.update({c: gained})
+            gained = keep.tile([P, S], F32, name=f"gained{c}", tag="turned3", align_bytes=64)
+            nc.scalar.activation(gained[:], hidden[c], ACT.Copy, scale=gain_cols[:, c : c + 1])
+            hidden.update({c: gained[:]})
 
-        def scatter(c, cols, list_cols):
-            nc.vector.tensor_tensor(page[c][:].indirect(slots[:, list_cols]), hidden[c][:, cols], wgs_sb[:, cols], ALU.mult)
+        def scatter_half(c, i):
+            nc.vector.tensor_tensor(page[c][:].indirect(slots[:, list_halves[i]]), hidden[(c, i)], wgs_sb[:, halves[i]], ALU.mult)
 
         def scatter_whole(c):
-            scatter(c, slice(0, S), slice(0, S // 16))
+            nc.vector.tensor_tensor(page[c][:].indirect(slots[:]), hidden[c], wgs_sb[:], ALU.mult)
 
         def store_page(c):
             nc.sync.dma_start(out=out_1[c * P : (c + 1) * P, :], in_=page[c][:])
@@ -173,7 +196,8 @@ def tile_list_narrator_prefix_cache_kernel(
         def turn(c, k):
             g, quarter = divmod(c, 4)
             if (g, k) not in turned:
-                turned.setdefault((g, k), keep.tile([P, 4, 2, 2 * P], BF16, name=f"turned{g}{k}", tag=f"turned{k}"))
+                turned.setdefault((g, k), keep.tile([P, 4, 2, 2 * P], BF16, name=f"turned{g}{k}",
+                                                   tag="wc_raw0" if (g, k) == (1, 3) else f"turned{k}", align_bytes=64))
             bank = turn_banks.tile([P, 4, P], F32, name="turn_bank", tag="turn_bank")
             for b in range(4):
                 nc.tensor.transpose(bank[:, b, :], page[c][:, k * BANK + b * P : k * BANK + (b + 1) * P], ident[:])
@@ -186,7 +210,7 @@ def tile_list_narrator_prefix_cache_kernel(
 
         def quantise_page(g, k):
             pairs = turned[(g, k)][:].rearrange("s b u w -> s (b u w)").bitcast(F32)
-            woven = keep.tile([P, BANK, 4], BF16, name=f"woven{g}{k}", tag=("ring", "hidden")[g] + str(k), align_bytes=64)
+            woven = keep.tile([P, BANK, 4], BF16, name=f"woven{g}{k}", tag=f"ring{k}", align_bytes=64)
             woven_flat = woven[:].rearrange("p s j -> p (s j)")
             woven_pairs = woven_flat.bitcast(F32)
             for half in range(2):
@@ -226,28 +250,31 @@ def tile_list_narrator_prefix_cache_kernel(
 
         for c in range(EARLY_TILES):
             first_stage(c, 0)
-            apply_gain(c, halves[0])
-            scatter(c, halves[0], list_halves[0])
-        scene_q.append(quantise_operand(scene_raw[1], BANK, "scene1", "ring2"))
-        wc_q.append(quantise_operand(wc_raw[1], wc_ranges[1][1] - wc_ranges[1][0], "wc1", "ring3"))
+            apply_gain(c, (c, 0))
+            scatter_half(c, 0)
+            if c == 0:
+                wc_q.append(quantise_operand([(wc_raw[1], nc.scalar.copy)], "wc1", "ring2"))
+            if c == 2:
+                scene_q.append(quantise_operand([(scene_second, nc.scalar.copy)], "scene1", "ring3"))
         for c in range(EARLY_TILES):
             first_stage(c, 1)
-            apply_gain(c, halves[1])
-        first_stage(4, 0)
-        first_stage(4, 1)
-        apply_gain(4, slice(0, S))
+            apply_gain(c, (c, 1))
+            if c == 1:
+                wc_q.append(quantise_operand([(wc_raw[2], nc.scalar.copy)], "wc2", "ring0"))
         for c in range(EARLY_TILES):
-            scatter(c, halves[1], list_halves[1])
+            scatter_half(c, 1)
             store_page(c)
-            if c < 3:
-                first_stage(c + 5, 0)
-                first_stage(c + 5, 1)
             for k in range(CHUNKS):
                 turn(c, k)
-                if c == 3:
-                    quantise_page(0, k)
-        for c in range(5, ROW_TILES):
-            apply_gain_late(c)
+            if c < 3:
+                first_stage(c + 4, 0)
+                first_stage(c + 4, 1)
+                apply_gain(c + 4, c + 4)
+        first_stage(7, 0)
+        first_stage(7, 1)
+        for k in range(CHUNKS):
+            quantise_page(0, k)
+        apply_gain_late(7)
         for c in range(4, 7):
             scatter_whole(c)
             store_page(c)
@@ -257,12 +284,12 @@ def tile_list_narrator_prefix_cache_kernel(
         store_scales(0)
         scatter_whole(7)
         store_page(7)
-        for k in range(CHUNKS + 1):
-            if k < CHUNKS:
-                turn(7, k)
-                quantise_page(1, k)
-                store_codes(1, slice(k * BANK, (k + 1) * BANK))
-            if k == CHUNKS - 1:
-                store_scales(1)
-            if k > 0:
-                second_stage(k - 1)
+        turn(7, 0)
+        for k in range(CHUNKS):
+            if k + 1 < CHUNKS:
+                turn(7, k + 1)
+            quantise_page(1, k)
+            store_codes(1, slice(k * BANK, (k + 1) * BANK))
+        store_scales(1)
+        for k in range(CHUNKS):
+            second_stage(k)

@@ -16,11 +16,16 @@ ALU = mybir.AluOpType
 
 P = 128
 H, N, T, S, T2 = 1024, 512, 4096, 1024, 2048
+PACK = 4
+QUADRANTS = 4
+LIST_ROWS = 16
 BANK = 512
-ROW_TILES = H // P
+PAGE_TILES = H // P
+GROUP_TILES = 4
+LAST_TILE = PAGE_TILES - 1
 CHUNKS = T2 // BANK
-EARLY_TILES = 4
-FLOPS = 5368709120
+ALIGN = 64
+FLOPS = 2 * (1024 + 512) * H * S + 2 * H * N * T2
 
 
 def tile_list_narrator_prefix_cache_kernel(
@@ -35,38 +40,45 @@ def tile_list_narrator_prefix_cache_kernel(
         turn_banks = ctx.enter_context(tc.psum_pool(name="turn_banks", bufs=2))
         back_banks = ctx.enter_context(tc.psum_pool(name="back_banks", bufs=2))
 
-        wc_ranges = [(0, 2 * P), (2 * P, 4 * P), (4 * P, H)]
         halves = [slice(0, BANK), slice(BANK, S)]
-        list_halves = [slice(0, BANK // 16), slice(BANK // 16, S // 16)]
+        list_halves = [slice(0, BANK // LIST_ROWS), slice(BANK // LIST_ROWS, S // LIST_ROWS)]
 
-        tab_scale_rows = keep.tile([P, 2, T], U8, tag="picking", align_bytes=64)
-        w4_scale = keep.tile([P, 2, H], U8, align_bytes=64)
-        w8_scale = keep.tile([P, 2, N], U8, align_bytes=64)
+        def plane_rows(plane, q):
+            return plane[32 * q : 32 * q + 4].bitcast(I32)
+
+        def load_scale_planes(planes, scales):
+            for q in range(QUADRANTS):
+                nc.gpsimd.dma_start(out=plane_rows(planes, q),
+                                    in_=scales[:, 4 * q : 4 * q + 4, :].rearrange("a q c -> q a c").bitcast(I32))
+
+        tab_scale_rows = keep.tile([P, 2, T], U8, tag="picking", align_bytes=ALIGN)
+        picked_scale = keep.tile([P, 2, S], U8, align_bytes=ALIGN)
+        w4_scale = keep.tile([P, 2, H], U8, align_bytes=ALIGN)
+        w8_scale = keep.tile([P, 2, N], U8, align_bytes=ALIGN)
         gain_rows = keep.tile([P, P], F32)
         ident = keep.tile([P, P], F32)
         nc.vector.memset(tab_scale_rows[:, 0, :].bitcast(I32), 0)
         nc.gpsimd.memset(tab_scale_rows[:, 1, :].bitcast(I32), 0)
         nc.vector.memset(w4_scale[:].bitcast(I32), 0)
+        nc.vector.memset(picked_scale[:].bitcast(I32), 0)
         nc.vector.memset(w8_scale[:].bitcast(I32), 0)
+        load_scale_planes(w4_scale, w4_scales)
         nc.gpsimd.memset(gain_rows[:], 0.0)
-        nc.scalar.dma_start(out=gain_rows[0:ROW_TILES, :], in_=gain.rearrange("(c p) -> c p", p=P))
+        nc.scalar.dma_start(out=gain_rows[0:PAGE_TILES, :], in_=gain.rearrange("(c p) -> c p", p=P))
         make_identity(nc, ident[:])
-        warm = keep.tile([P, 1], F32)
-        nc.scalar.activation(warm[:], ident[:, 0:1], ACT.Gelu_apprx_tanh)
 
-        picks = lists.tile([P, S // 16], U16)
-        slots = lists.tile([P, S // 16], U16)
-        scene_rows = scene.rearrange("(p j) s -> p j s", j=4)
-        wc_rows = wc.rearrange("(p j) c -> p j c", j=4)
-        scene_first = [keep.tile([P, 4, BANK // 2], F32, name=f"scene_first{i}", tag=f"scene_first{i}", align_bytes=64)
-                       for i in range(2)]
-        scene_second = keep.tile([P, 4, BANK], F32, tag="scene_second", align_bytes=64)
-        wc_raw = [keep.tile([P, 4, b - a], F32, name=f"wc_raw{i}", tag=f"wc_raw{i}", align_bytes=64) for i, (a, b) in enumerate(wc_ranges)]
-        tab = [keep.tile([P, T], I32, name=f"tab{a}", tag=f"big{a}") for a in range(2)]
-        w4 = [keep.tile([P, 2, H], U8, name=f"w4_{i}", align_bytes=64) for i in range(2)]
+        picks = lists.tile([P, S // LIST_ROWS], U16)
+        slots = lists.tile([P, S // LIST_ROWS], U16)
+        scene_rows = scene.rearrange("(p j) s -> p j s", j=PACK)
+        wc_rows = wc.rearrange("(p j) c -> p j c", j=PACK)
+        scene_raw = [keep.tile([P, PACK, BANK], F32, name=f"scene_raw{i}", tag=f"scene_raw{i}", align_bytes=ALIGN)
+                     for i in range(2)]
+        wc_raw = [keep.tile([P, PACK, BANK], F32, name=f"wc_raw{g}", tag=f"wc_raw{g}", align_bytes=ALIGN) for g in range(2)]
+        tab = [keep.tile([P, T], I32, name=f"tab{a}", tag=f"table_then_result{a}") for a in range(2)]
+        w4 = [keep.tile([P, 2, 2 * BANK], U8, name=f"w4_{g}", align_bytes=ALIGN) for g in range(2)]
         wgs_sb = keep.tile([P, S], F32)
-        page = [keep.tile([P, T2], F32, name=f"page{c}") for c in range(ROW_TILES)]
-        w8 = keep.tile([P, 2, N], I32, align_bytes=64)
+        page = [keep.tile([P, T2], F32, name=f"page{c}") for c in range(PAGE_TILES)]
+        w8 = keep.tile([P, 2, N], I32, align_bytes=ALIGN)
 
         def load_page(c):
             nc.sync.dma_start(out=page[c][:], in_=page0[c * P : (c + 1) * P, :])
@@ -74,119 +86,108 @@ def tile_list_narrator_prefix_cache_kernel(
         def load_table(a, cols):
             nc.sync.dma_start(out=tab[a][:, cols], in_=tab_words[a].rearrange("p t i -> p (t i)").bitcast(I32)[:, cols])
 
-        def load_wc(part):
-            nc.sync.dma_start(out=wc_raw[part][:], in_=wc_rows[:, :, wc_ranges[part][0] : wc_ranges[part][1]])
+        def load_wc(g):
+            nc.sync.dma_start(out=wc_raw[g][:], in_=wc_rows[:, :, halves[g]])
 
-        def load_w4(i):
-            nc.sync.dma_start(out=w4[i][:].bitcast(I32),
-                              in_=w4_words.rearrange("a p c -> p a c")[:, :, i * H : (i + 1) * H].bitcast(I32))
+        def load_scene(i):
+            nc.sync.dma_start(out=scene_raw[i][:], in_=scene_rows[:, :, halves[i]])
+
+        def load_wgs(i):
+            nc.sync.dma_start(out=wgs_sb[:, halves[i]], in_=wgs[:, halves[i]])
+
+        def load_w4(g):
+            columns = w4_words.rearrange("a p c -> p a c")[:, :, 2 * g * BANK : 2 * (g + 1) * BANK]
+            nc.sync.dma_start(out=w4[g][:].bitcast(I32), in_=columns.bitcast(I32))
 
         nc.sync.dma_start(picks[:], offs)
         nc.sync.dma_start(slots[:], offs2)
         load_table(0, slice(0, T // 4))
-        for q in range(4):
-            nc.sync.dma_start(out=tab_scale_rows[32 * q : 32 * q + 4, :, :].bitcast(I32),
-                                in_=tab_scales[:, 4 * q : 4 * q + 4, :].rearrange("a q t -> q a t").bitcast(I32))
+        nc.sync.dma_start(out=tab_scale_rows[0:P:8, :, :].bitcast(I32), in_=tab_scales.rearrange("a q t -> q a t").bitcast(I32))
         load_table(0, slice(T // 4, T))
-        load_table(1, slice(0, T))
-        for q in range(4):
-            nc.sync.dma_start(out=w4_scale[32 * q : 32 * q + 4, :, :].bitcast(I32),
-                                in_=w4_scales[:, 4 * q : 4 * q + 4, :].rearrange("a q c -> q a c").bitcast(I32))
-        load_w4(0)
         load_wc(0)
-        for i in range(2):
-            nc.sync.dma_start(out=scene_first[i][:], in_=scene_rows[:, :, i * BANK // 2 : (i + 1) * BANK // 2])
-        nc.sync.dma_start(out=wgs_sb[:, halves[0]], in_=wgs[:, halves[0]])
+        load_scene(0)
+        load_w4(0)
+        load_table(1, slice(0, T))
+        load_wgs(0)
         load_page(0)
-        load_wc(1)
         load_page(1)
-        nc.sync.dma_start(out=scene_second[:], in_=scene_rows[:, :, halves[1]])
+        load_scene(1)
         load_page(2)
         load_page(3)
-        nc.sync.dma_start(out=wgs_sb[:, halves[1]], in_=wgs[:, halves[1]])
-        load_wc(2)
+        load_wgs(1)
+        load_wc(1)
         load_w4(1)
-        for c in range(EARLY_TILES, ROW_TILES):
+        for c in range(GROUP_TILES, PAGE_TILES):
             load_page(c)
         nc.sync.dma_start(out=w8[:], in_=w8_words.rearrange("a p c i -> p a (c i)").bitcast(I32))
-        for q in range(4):
-            nc.sync.dma_start(out=w8_scale[32 * q : 32 * q + 4, :, :].bitcast(I32),
-                                in_=w8_scales[:, 4 * q : 4 * q + 4, :].rearrange("a q c -> q a c").bitcast(I32))
+        load_scale_planes(w8_scale, w8_scales)
 
         gain_bank = turn_banks.tile([P, 4, P], F32, name="turn_bank", tag="turn_bank")
         nc.tensor.transpose(gain_bank[:, 0, :], gain_rows[:], ident[:])
-        gain_cols = keep.tile([P, ROW_TILES], F32)
-        nc.scalar.copy(gain_cols[:], gain_bank[:, 0, 0:ROW_TILES])
+        gain_cols = keep.tile([P, PAGE_TILES], F32)
+        nc.scalar.copy(gain_cols[:], gain_bank[:, 0, 0:PAGE_TILES])
 
-        def quantise_operand(pieces, name, tag):
-            width = sum(raw.shape[2] for raw, copy in pieces)
-            woven = keep.tile([P, width, 4], BF16, name=name + "_woven", tag=tag, align_bytes=64)
-            codes = keep.tile([P, width], U32, name=name + "_codes", align_bytes=64)
-            scale = keep.tile([P, width], U8, name=name + "_scale", align_bytes=64)
-            start = 0
-            for raw, copy in pieces:
-                cols = slice(start, start + raw.shape[2])
-                copy(woven[:, cols, :].rearrange("p (c i) j -> p c j i", i=4), raw[:].rearrange("p j (c i) -> p c j i", i=4))
-                nc.vector.quantize_mx(out=codes[:, cols].bitcast(FP8X4), scales=scale[:, cols],
-                                      in_=woven[:, cols, :].rearrange("p c j -> p (c j)"))
-                start += raw.shape[2]
+        def quantise_operand(raw, name, tag):
+            woven = keep.tile([P, BANK, PACK], BF16, name=name + "_woven", tag=tag, align_bytes=ALIGN)
+            codes = keep.tile([P, BANK], U32, name=name + "_codes", align_bytes=ALIGN)
+            scale = keep.tile([P, BANK], U8, name=name + "_scale", align_bytes=ALIGN)
+            nc.scalar.copy(woven[:].rearrange("p (c i) j -> p c j i", i=4), raw[:].rearrange("p j (c i) -> p c j i", i=4))
+            nc.vector.quantize_mx(out=codes[:].bitcast(FP8X4), scales=scale[:], in_=woven[:].rearrange("p c j -> p (c j)"))
             return codes, scale
 
-        picked_scale = [keep.tile([P, S], U8, name=f"picked_scale{a}", align_bytes=64) for a in range(2)]
+        picked_rows = keep.tile([P, 2, S], U8, align_bytes=ALIGN)
         for a in range(2):
-            nc.vector.tensor_copy(picked_scale[a][:], tab_scale_rows[:, a, :].indirect(picks[:]))
-        picked = keep.tile([P, 2, S], U32, tag="picking", align_bytes=64)
+            nc.vector.tensor_copy(picked_rows[:, a, :], tab_scale_rows[:, a, :].indirect(picks[:]))
+        for q in range(QUADRANTS):
+            nc.gpsimd.dma_start(out=plane_rows(picked_scale, q), in_=picked_rows[32 * q : 32 * q + 32 : 8, :, :].bitcast(I32))
+        picked = keep.tile([P, 2, S], U32, tag="picking", align_bytes=ALIGN)
         for a in range(2):
             for i in range(2):
                 nc.vector.tensor_copy(picked[:, a, halves[i]], tab[a][:].bitcast(U32).indirect(picks[:, list_halves[i]]))
 
-        wc_q = [quantise_operand([(wc_raw[0], nc.scalar.copy)], "wc0", "ring1")]
-        scene_q = [quantise_operand([(scene_first[0], nc.vector.tensor_copy), (scene_first[1], nc.scalar.copy)], "scene0", "ring0")]
+        wc_q = [quantise_operand(wc_raw[0], "wc0", "woven1")]
+        scene_q = [quantise_operand(scene_raw[0], "scene0", "woven0")]
 
-        result_pairs = [keep.tile([P, 2, N // P, BANK], F32, name=f"result{i}", tag=f"big{i}") for i in range(2)]
-        result = [result_pairs[k // 2][:, k % 2, :, :] for k in range(CHUNKS)]
+        result = [keep.tile([P, 2, T2], F32, name=f"result{a}", tag=f"table_then_result{a}") for a in range(2)]
         bias_rows = bias.rearrange("(n p) t -> p n t", p=P)
         out_rows = out_0.rearrange("(n p) t -> p n t", p=P)
-        for k in range(CHUNKS):
-            nc.sync.dma_start(out=result[k], in_=bias_rows[:, :, k * BANK : (k + 1) * BANK])
+        for a in range(2):
+            nc.sync.dma_start(out=result[a][:], in_=bias_rows[:, 2 * a : 2 * a + 2, :])
 
-        half_tags = {(0, 0): "half0", (1, 0): "wc_raw1", (2, 0): "half1", (3, 0): "scene_second",
-                     (0, 1): "half0", (1, 1): "half1", (2, 1): "wc_raw2", (3, 1): "scene_first0"}
+        half_tags = {(0, 0): "half0", (1, 0): "turned0", (2, 0): "half1", (3, 0): "scene_raw1",
+                     (0, 1): "half0", (1, 1): "half1", (2, 1): "wc_raw1", (3, 1): "scene_raw0"}
         hidden = {}
 
         def first_stage(c, i):
-            if c < EARLY_TILES:
-                hidden.update({(c, i): keep.tile([P, BANK], F32, name=f"hidden{c}{i}", tag=half_tags[(c, i)], align_bytes=64)[:]})
+            g, place = divmod(c, GROUP_TILES)
+            if g == 0:
+                half = keep.tile([P, BANK], F32, name=f"hidden{c}{i}", tag=half_tags[(c, i)], align_bytes=ALIGN)
+                hidden.update({(c, i): half[:]})
             elif i == 0:
-                whole = keep.tile([P, S], F32, name=f"hidden{c}", tag=f"hidden{c - 4}", align_bytes=64)
+                whole = keep.tile([P, S], F32, name=f"hidden{c}", align_bytes=ALIGN)
                 hidden.update({c: whole[:], (c, 0): whole[:, halves[0]], (c, 1): whole[:, halves[1]]})
-            part = min(c // 2, 2)
-            wc_cols = slice(c * P - wc_ranges[part][0], (c + 1) * P - wc_ranges[part][0])
+            wc_codes, wc_scale = wc_q[g]
+            scene_codes, scene_scale = scene_q[i]
+            rows = slice(place * P, (place + 1) * P)
             bank = mx_banks.tile([P, BANK], F32, name="mx_bank", tag="mx_bank")
+            nc.tensor.matmul_mx(out=bank[:], lhsT=wc_codes[:, rows].bitcast(FP8X4), lhsT_scale=wc_scale[:, rows],
+                                rhs=scene_codes[:].bitcast(FP8X4), rhs_scale=scene_scale[:], start=True, stop=False)
             for a in range(2):
-                nc.tensor.matmul_mx(out=bank[:], lhsT=w4[c // 4][:, a, 2 * (c % 4) * P : 2 * (c % 4 + 1) * P].bitcast(FP4X4),
+                nc.tensor.matmul_mx(out=bank[:], lhsT=w4[g][:, a, 2 * place * P : 2 * (place + 1) * P].bitcast(FP4X4),
                                     lhsT_scale=w4_scale[:, a, c * P : (c + 1) * P],
-                                    rhs=picked[:, a, halves[i]].bitcast(FP8X4), rhs_scale=picked_scale[a][:, halves[i]],
-                                    start=(a == 0), stop=False)
-            nc.tensor.matmul_mx(out=bank[:], lhsT=wc_q[part][0][:, wc_cols].bitcast(FP8X4),
-                                lhsT_scale=wc_q[part][1][:, wc_cols],
-                                rhs=scene_q[i][0][:].bitcast(FP8X4), rhs_scale=scene_q[i][1][:],
-                                start=False, stop=True)
+                                    rhs=picked[:, a, halves[i]].bitcast(FP8X4), rhs_scale=picked_scale[:, a, halves[i]],
+                                    start=False, stop=(a == 1))
             nc.scalar.activation(hidden[(c, i)], bank[:], ACT.Gelu_apprx_tanh)
 
-        def apply_gain(c, key):
-            nc.scalar.activation(hidden[key], hidden[key], ACT.Copy, scale=gain_cols[:, c : c + 1])
-
-        def apply_gain_late(c):
-            gained = keep.tile([P, S], F32, name=f"gained{c}", tag="turned3", align_bytes=64)
-            nc.scalar.activation(gained[:], hidden[c], ACT.Copy, scale=gain_cols[:, c : c + 1])
-            hidden.update({c: gained[:]})
+        def apply_gain(c, out, in_):
+            nc.scalar.activation(out, in_, ACT.Copy, scale=gain_cols[:, c : c + 1])
 
         def scatter_half(c, i):
-            nc.vector.tensor_tensor(page[c][:].indirect(slots[:, list_halves[i]]), hidden[(c, i)], wgs_sb[:, halves[i]], ALU.mult)
+            nc.vector.tensor_tensor(page[c][:].indirect(slots[:, list_halves[i]]), hidden[(c, i)], wgs_sb[:, halves[i]],
+                                    ALU.mult)
 
-        def scatter_whole(c):
-            nc.vector.tensor_tensor(page[c][:].indirect(slots[:]), hidden[c], wgs_sb[:], ALU.mult)
+        def scatter_whole(c, values):
+            nc.vector.tensor_tensor(page[c][:].indirect(slots[:]), values, wgs_sb[:], ALU.mult)
 
         def store_page(c):
             nc.sync.dma_start(out=out_1[c * P : (c + 1) * P, :], in_=page[c][:])
@@ -194,33 +195,33 @@ def tile_list_narrator_prefix_cache_kernel(
         turned = {}
 
         def turn(c, k):
-            g, quarter = divmod(c, 4)
-            if (g, k) not in turned:
-                turned.setdefault((g, k), keep.tile([P, 4, 2, 2 * P], BF16, name=f"turned{g}{k}",
-                                                   tag="wc_raw0" if (g, k) == (1, 3) else f"turned{k}", align_bytes=64))
+            g, place = divmod(c, GROUP_TILES)
+            if place == 0:
+                tag = "wc_raw0" if (g, k) == (1, CHUNKS - 1) else f"turned{k}"
+                turned.update({(g, k): keep.tile([P, 4, 2, 2 * P], BF16, name=f"turned{g}{k}", tag=tag, align_bytes=ALIGN)})
             bank = turn_banks.tile([P, 4, P], F32, name="turn_bank", tag="turn_bank")
             for b in range(4):
                 nc.tensor.transpose(bank[:, b, :], page[c][:, k * BANK + b * P : k * BANK + (b + 1) * P], ident[:])
             nc.scalar.copy(
-                turned[(g, k)][:, :, :, 64 * quarter : 64 * (quarter + 1)].rearrange("s b u (p e) -> s b u p e", e=2),
+                turned[(g, k)][:, :, :, 64 * place : 64 * (place + 1)].rearrange("s b u (p e) -> s b u p e", e=2),
                 bank[:].rearrange("s b (p u e) -> s b u p e", u=2, e=2))
 
-        page_codes = [keep.tile([P, T2], I32, name=f"page_codes{g}", align_bytes=64) for g in range(2)]
-        page_scale = [keep.tile([P, T2], U8, name=f"page_scale{g}", align_bytes=64) for g in range(2)]
+        page_codes = [keep.tile([P, T2], I32, name=f"page_codes{g}", align_bytes=ALIGN) for g in range(2)]
+        page_scale = [keep.tile([P, T2], U8, name=f"page_scale{g}", align_bytes=ALIGN) for g in range(2)]
 
         def quantise_page(g, k):
             pairs = turned[(g, k)][:].rearrange("s b u w -> s (b u w)").bitcast(F32)
-            woven = keep.tile([P, BANK, 4], BF16, name=f"woven{g}{k}", tag=f"ring{k}", align_bytes=64)
+            woven = keep.tile([P, BANK, PACK], BF16, name=f"woven{g}{k}", tag=f"woven{k}", align_bytes=ALIGN)
             woven_flat = woven[:].rearrange("p s j -> p (s j)")
             woven_pairs = woven_flat.bitcast(F32)
-            for half in range(2):
+            for two_blocks in range(2):
                 bank = back_banks.tile([P, 2, 2, P], F32, name="back_bank", tag="back_bank")
                 for b in range(2):
                     for u in range(2):
-                        at = ((2 * half + b) * 2 + u) * P
+                        at = ((2 * two_blocks + b) * 2 + u) * P
                         nc.tensor.transpose(bank[:, b, u, :], pairs[:, at : at + P], ident[:])
                 nc.scalar.copy(
-                    woven_pairs[:, half * BANK : (half + 1) * BANK].rearrange("p (b s u) -> p b s u", b=2, u=2),
+                    woven_pairs[:, two_blocks * BANK : (two_blocks + 1) * BANK].rearrange("p (b s u) -> p b s u", b=2, u=2),
                     bank[:].rearrange("p b u s -> p b s u"))
             cols = slice(k * BANK, (k + 1) * BANK)
             nc.vector.quantize_mx(out=page_codes[g][:, cols].bitcast(FP8X4), scales=page_scale[g][:, cols], in_=woven_flat)
@@ -229,9 +230,8 @@ def tile_list_narrator_prefix_cache_kernel(
             nc.sync.dma_start(out=out_2[g].rearrange("p m t -> p (m t)").bitcast(I32)[:, cols], in_=page_codes[g][:, cols])
 
         def store_scales(g):
-            for q in range(4):
-                nc.sync.dma_start(out=out_3[g, 4 * q : 4 * q + 4, :].bitcast(I32),
-                                  in_=page_scale[g][32 * q : 32 * q + 4, :].bitcast(I32))
+            for q in range(QUADRANTS):
+                nc.gpsimd.dma_start(out=out_3[g, 4 * q : 4 * q + 4, :].bitcast(I32), in_=plane_rows(page_scale[g], q))
 
         def second_stage(k):
             cols = slice(k * BANK, (k + 1) * BANK)
@@ -242,52 +242,51 @@ def tile_list_narrator_prefix_cache_kernel(
                                         lhsT_scale=w8_scale[:, g, n * P : (n + 1) * P],
                                         rhs=page_codes[g][:, cols].bitcast(FP8X4), rhs_scale=page_scale[g][:, cols],
                                         start=(g == 0), stop=(g == 1))
-                nc.vector.tensor_tensor(result[k][:, n, :], bank[:], result[k][:, n, :], ALU.add)
+                sums = result[n // 2][:, n % 2, cols]
+                nc.vector.tensor_tensor(sums, bank[:], sums, ALU.add)
                 if k == CHUNKS - 1:
-                    nc.sync.dma_start(out=out_rows[:, n, cols], in_=result[k][:, n, :])
+                    nc.sync.dma_start(out=out_rows[:, n, cols], in_=sums)
                 elif n % 2 == 1:
-                    nc.sync.dma_start(out=out_rows[:, n - 1 : n + 1, cols], in_=result[k][:, n - 1 : n + 1, :])
+                    nc.sync.dma_start(out=out_rows[:, n - 1 : n + 1, cols], in_=result[n // 2][:, :, cols])
 
-        for c in range(EARLY_TILES):
+        for c in range(GROUP_TILES):
+            if half_tags[(c, 0)] == "scene_raw1":
+                scene_q.append(quantise_operand(scene_raw[1], "scene1", "woven3"))
             first_stage(c, 0)
-            apply_gain(c, (c, 0))
+            apply_gain(c, hidden[(c, 0)], hidden[(c, 0)])
             scatter_half(c, 0)
-            if c == 0:
-                wc_q.append(quantise_operand([(wc_raw[1], nc.scalar.copy)], "wc1", "ring2"))
-            if c == 2:
-                scene_q.append(quantise_operand([(scene_second, nc.scalar.copy)], "scene1", "ring3"))
-        for c in range(EARLY_TILES):
+        for c in range(GROUP_TILES):
+            if half_tags[(c, 1)] == "wc_raw1":
+                wc_q.append(quantise_operand(wc_raw[1], "wc1", "woven2"))
             first_stage(c, 1)
-            apply_gain(c, (c, 1))
-            if c == 1:
-                wc_q.append(quantise_operand([(wc_raw[2], nc.scalar.copy)], "wc2", "ring0"))
-        for c in range(EARLY_TILES):
+            apply_gain(c, hidden[(c, 1)], hidden[(c, 1)])
+        for c in range(GROUP_TILES):
             scatter_half(c, 1)
             store_page(c)
             for k in range(CHUNKS):
                 turn(c, k)
-            if c < 3:
-                first_stage(c + 4, 0)
-                first_stage(c + 4, 1)
-                apply_gain(c + 4, c + 4)
-        first_stage(7, 0)
-        first_stage(7, 1)
+            ahead = c + GROUP_TILES
+            first_stage(ahead, 0)
+            first_stage(ahead, 1)
+            if ahead < LAST_TILE:
+                apply_gain(ahead, hidden[ahead], hidden[ahead])
         for k in range(CHUNKS):
             quantise_page(0, k)
-        apply_gain_late(7)
-        for c in range(4, 7):
-            scatter_whole(c)
+        last_values = keep.tile([P, S], F32, tag=f"turned{CHUNKS - 1}", align_bytes=ALIGN)
+        apply_gain(LAST_TILE, last_values[:], hidden[LAST_TILE])
+        for c in range(GROUP_TILES, LAST_TILE):
+            scatter_whole(c, hidden[c])
             store_page(c)
             for k in range(CHUNKS):
                 turn(c, k)
         store_codes(0, slice(0, T2))
         store_scales(0)
-        scatter_whole(7)
-        store_page(7)
-        turn(7, 0)
+        scatter_whole(LAST_TILE, last_values[:])
+        store_page(LAST_TILE)
+        turn(LAST_TILE, 0)
         for k in range(CHUNKS):
             if k + 1 < CHUNKS:
-                turn(7, k + 1)
+                turn(LAST_TILE, k + 1)
             quantise_page(1, k)
             store_codes(1, slice(k * BANK, (k + 1) * BANK))
         store_scales(1)

@@ -36,9 +36,9 @@ def tile_list_narrator_prefix_cache_kernel(
     with ExitStack() as ctx:
         lists = ctx.enter_context(tc.tile_pool(name="lists", bufs=1))
         keep = ctx.enter_context(tc.tile_pool(name="keep", bufs=1))
-        mx_banks = ctx.enter_context(tc.psum_pool(name="mx_banks", bufs=4))
-        turn_banks = ctx.enter_context(tc.psum_pool(name="turn_banks", bufs=2))
-        back_banks = ctx.enter_context(tc.psum_pool(name="back_banks", bufs=2))
+        psum = ctx.enter_context(tc.psum_pool(name="psum", bufs=1))
+        banks = [psum.tile([P, BANK], F32, name=f"bank{b}") for b in range(8)]
+        product_banks, turn_banks, back_banks = banks[0:4], banks[4:6], banks[6:8]
 
         halves = [slice(0, BANK), slice(BANK, S)]
         list_halves = [slice(0, BANK // LIST_ROWS), slice(BANK // LIST_ROWS, S // LIST_ROWS)]
@@ -71,11 +71,15 @@ def tile_list_narrator_prefix_cache_kernel(
         slots = lists.tile([P, S // LIST_ROWS], U16)
         scene_rows = scene.rearrange("(p j) s -> p j s", j=PACK)
         wc_rows = wc.rearrange("(p j) c -> p j c", j=PACK)
+        wc_pieces = [slice(0, 2 * P), slice(2 * P, 4 * P), slice(4 * P, H)]
+        w4_pieces = [slice(0, 2 * P), slice(2 * P, H)]
         scene_raw = [keep.tile([P, PACK, BANK], F32, name=f"scene_raw{i}", tag=f"scene_raw{i}", align_bytes=ALIGN)
                      for i in range(2)]
-        wc_raw = [keep.tile([P, PACK, BANK], F32, name=f"wc_raw{g}", tag=f"wc_raw{g}", align_bytes=ALIGN) for g in range(2)]
+        wc_raw = [keep.tile([P, PACK, cols.stop - cols.start], F32, name=f"wc_raw{i}", tag=f"wc_raw{i}", align_bytes=ALIGN)
+                  for i, cols in enumerate(wc_pieces)]
         tab = [keep.tile([P, T], I32, name=f"tab{a}", tag=f"table_then_result{a}") for a in range(2)]
-        w4 = [keep.tile([P, 2, 2 * BANK], U8, name=f"w4_{g}", align_bytes=ALIGN) for g in range(2)]
+        w4 = [keep.tile([P, 2, 2 * (cols.stop - cols.start)], U8, name=f"w4_{i}", align_bytes=ALIGN)
+              for i, cols in enumerate(w4_pieces)]
         wgs_sb = keep.tile([P, S], F32)
         page = [keep.tile([P, T2], F32, name=f"page{c}") for c in range(PAGE_TILES)]
         w8 = keep.tile([P, 2, N], I32, align_bytes=ALIGN)
@@ -86,8 +90,8 @@ def tile_list_narrator_prefix_cache_kernel(
         def load_table(a, cols):
             nc.sync.dma_start(out=tab[a][:, cols], in_=tab_words[a].rearrange("p t i -> p (t i)").bitcast(I32)[:, cols])
 
-        def load_wc(g):
-            nc.sync.dma_start(out=wc_raw[g][:], in_=wc_rows[:, :, halves[g]])
+        def load_wc(i):
+            nc.sync.dma_start(out=wc_raw[i][:], in_=wc_rows[:, :, wc_pieces[i]])
 
         def load_scene(i):
             nc.sync.dma_start(out=scene_raw[i][:], in_=scene_rows[:, :, halves[i]])
@@ -95,58 +99,45 @@ def tile_list_narrator_prefix_cache_kernel(
         def load_wgs(i):
             nc.sync.dma_start(out=wgs_sb[:, halves[i]], in_=wgs[:, halves[i]])
 
-        def load_w4(g):
-            columns = w4_words.rearrange("a p c -> p a c")[:, :, 2 * g * BANK : 2 * (g + 1) * BANK]
-            nc.sync.dma_start(out=w4[g][:].bitcast(I32), in_=columns.bitcast(I32))
+        def load_w4(i):
+            cols = w4_pieces[i]
+            columns = w4_words.rearrange("a p c -> p a c")[:, :, 2 * cols.start : 2 * cols.stop]
+            nc.sync.dma_start(out=w4[i][:].bitcast(I32), in_=columns.bitcast(I32))
 
         nc.sync.dma_start(picks[:], offs)
-        nc.sync.dma_start(slots[:], offs2)
         load_table(0, slice(0, T // 4))
         nc.sync.dma_start(out=tab_scale_rows[0:P:8, :, :].bitcast(I32), in_=tab_scales.rearrange("a q t -> q a t").bitcast(I32))
         load_table(0, slice(T // 4, T))
+        load_table(1, slice(0, T))
         load_wc(0)
         load_scene(0)
+        load_scene(1)
         load_w4(0)
-        load_table(1, slice(0, T))
+        nc.sync.dma_start(slots[:], offs2)
         load_wgs(0)
         load_page(0)
-        load_page(1)
-        load_scene(1)
-        load_page(2)
-        load_page(3)
         load_wgs(1)
         load_wc(1)
+        load_wc(2)
+        load_page(1)
         load_w4(1)
-        for c in range(GROUP_TILES, PAGE_TILES):
+        for c in range(2, PAGE_TILES):
             load_page(c)
         nc.sync.dma_start(out=w8[:], in_=w8_words.rearrange("a p c i -> p a (c i)").bitcast(I32))
-        load_scale_planes(w8_scale, w8_scales)
 
-        gain_bank = turn_banks.tile([P, 4, P], F32, name="turn_bank", tag="turn_bank")
-        nc.tensor.transpose(gain_bank[:, 0, :], gain_rows[:], ident[:])
         gain_cols = keep.tile([P, PAGE_TILES], F32)
-        nc.scalar.copy(gain_cols[:], gain_bank[:, 0, 0:PAGE_TILES])
-
-        def quantise_operand(raw, name, tag):
-            woven = keep.tile([P, BANK, PACK], BF16, name=name + "_woven", tag=tag, align_bytes=ALIGN)
-            codes = keep.tile([P, BANK], U32, name=name + "_codes", align_bytes=ALIGN)
-            scale = keep.tile([P, BANK], U8, name=name + "_scale", align_bytes=ALIGN)
-            nc.scalar.copy(woven[:].rearrange("p (c i) j -> p c j i", i=4), raw[:].rearrange("p j (c i) -> p c j i", i=4))
-            nc.vector.quantize_mx(out=codes[:].bitcast(FP8X4), scales=scale[:], in_=woven[:].rearrange("p c j -> p (c j)"))
-            return codes, scale
+        nc.tensor.transpose(turn_banks[1][:, 0:P], gain_rows[:], ident[:])
+        nc.scalar.copy(gain_cols[:], turn_banks[1][:, 0:PAGE_TILES])
 
         picked_rows = keep.tile([P, 2, S], U8, align_bytes=ALIGN)
         for a in range(2):
             nc.vector.tensor_copy(picked_rows[:, a, :], tab_scale_rows[:, a, :].indirect(picks[:]))
         for q in range(QUADRANTS):
             nc.gpsimd.dma_start(out=plane_rows(picked_scale, q), in_=picked_rows[32 * q : 32 * q + 32 : 8, :, :].bitcast(I32))
+        load_scale_planes(w8_scale, w8_scales)
         picked = keep.tile([P, 2, S], U32, tag="picking", align_bytes=ALIGN)
         for a in range(2):
-            for i in range(2):
-                nc.vector.tensor_copy(picked[:, a, halves[i]], tab[a][:].bitcast(U32).indirect(picks[:, list_halves[i]]))
-
-        wc_q = [quantise_operand(wc_raw[0], "wc0", "woven1")]
-        scene_q = [quantise_operand(scene_raw[0], "scene0", "woven0")]
+            nc.vector.tensor_copy(picked[:, a, :], tab[a][:].bitcast(U32).indirect(picks[:]))
 
         result = [keep.tile([P, 2, T2], F32, name=f"result{a}", tag=f"table_then_result{a}") for a in range(2)]
         bias_rows = bias.rearrange("(n p) t -> p n t", p=P)
@@ -154,40 +145,53 @@ def tile_list_narrator_prefix_cache_kernel(
         for a in range(2):
             nc.sync.dma_start(out=result[a][:], in_=bias_rows[:, 2 * a : 2 * a + 2, :])
 
-        half_tags = {(0, 0): "half0", (1, 0): "turned0", (2, 0): "half1", (3, 0): "scene_raw1",
-                     (0, 1): "half0", (1, 1): "half1", (2, 1): "wc_raw1", (3, 1): "scene_raw0"}
-        hidden = {}
+        def weave_operand(raw, name, tag, copy):
+            width = raw.shape[2]
+            woven = keep.tile([P, width, PACK], BF16, name=name + "_woven", tag=tag, align_bytes=ALIGN)
+            copy(woven[:].rearrange("p (c i) j -> p c j i", i=4), raw[:].rearrange("p j (c i) -> p c j i", i=4))
+            return woven
+
+        def quantise_operand(woven, name):
+            width = woven.shape[1]
+            codes = keep.tile([P, width], U32, name=name + "_codes", align_bytes=ALIGN)
+            scale = keep.tile([P, width], U8, name=name + "_scale", align_bytes=ALIGN)
+            nc.vector.quantize_mx(out=codes[:].bitcast(FP8X4), scales=scale[:], in_=woven[:].rearrange("p c j -> p (c j)"))
+            return codes, scale
+
+        wc_q = [quantise_operand(weave_operand(wc_raw[0], "wc0", "woven2", nc.scalar.copy), "wc0")]
+        scene_q = [quantise_operand(weave_operand(scene_raw[i], f"scene{i}", f"woven{i}", nc.vector.tensor_copy), f"scene{i}")
+                   for i in range(2)]
+
+        def piece_of(pieces, c):
+            i = max(j for j, cols in enumerate(pieces) if cols.start <= c * P)
+            return i, c * P - pieces[i].start
+
+        pair_tags = ["hidden01", "wc_raw2", "scene_raw0", "scene_raw1"]
+        pairs_of_h = []
+
+        def hidden(c):
+            return pairs_of_h[c // 2][:, c % 2, :]
 
         def first_stage(c, i):
-            g, place = divmod(c, GROUP_TILES)
-            if g == 0:
-                half = keep.tile([P, BANK], F32, name=f"hidden{c}{i}", tag=half_tags[(c, i)], align_bytes=ALIGN)
-                hidden.update({(c, i): half[:]})
-            elif i == 0:
-                whole = keep.tile([P, S], F32, name=f"hidden{c}", align_bytes=ALIGN)
-                hidden.update({c: whole[:], (c, 0): whole[:, halves[0]], (c, 1): whole[:, halves[1]]})
-            wc_codes, wc_scale = wc_q[g]
-            scene_codes, scene_scale = scene_q[i]
-            rows = slice(place * P, (place + 1) * P)
-            bank = mx_banks.tile([P, BANK], F32, name="mx_bank", tag="mx_bank")
-            nc.tensor.matmul_mx(out=bank[:], lhsT=wc_codes[:, rows].bitcast(FP8X4), lhsT_scale=wc_scale[:, rows],
-                                rhs=scene_codes[:].bitcast(FP8X4), rhs_scale=scene_scale[:], start=True, stop=False)
+            bank = banks[(2 * c + i + 6) % 8]
+            piece, at = piece_of(w4_pieces, c)
             for a in range(2):
-                nc.tensor.matmul_mx(out=bank[:], lhsT=w4[g][:, a, 2 * place * P : 2 * (place + 1) * P].bitcast(FP4X4),
+                nc.tensor.matmul_mx(out=bank[:], lhsT=w4[piece][:, a, 2 * at : 2 * (at + P)].bitcast(FP4X4),
                                     lhsT_scale=w4_scale[:, a, c * P : (c + 1) * P],
                                     rhs=picked[:, a, halves[i]].bitcast(FP8X4), rhs_scale=picked_scale[:, a, halves[i]],
-                                    start=False, stop=(a == 1))
-            nc.scalar.activation(hidden[(c, i)], bank[:], ACT.Gelu_apprx_tanh)
+                                    start=(a == 0), stop=False)
+            piece, at = piece_of(wc_pieces, c)
+            wc_codes, wc_scale = wc_q[piece]
+            scene_codes, scene_scale = scene_q[i]
+            nc.tensor.matmul_mx(out=bank[:], lhsT=wc_codes[:, at : at + P].bitcast(FP8X4), lhsT_scale=wc_scale[:, at : at + P],
+                                rhs=scene_codes[:].bitcast(FP8X4), rhs_scale=scene_scale[:], start=False, stop=True)
+            nc.scalar.activation(hidden(c)[:, halves[i]], bank[:], ACT.Gelu_apprx_tanh)
 
         def apply_gain(c, out, in_):
             nc.scalar.activation(out, in_, ACT.Copy, scale=gain_cols[:, c : c + 1])
 
-        def scatter_half(c, i):
-            nc.vector.tensor_tensor(page[c][:].indirect(slots[:, list_halves[i]]), hidden[(c, i)], wgs_sb[:, halves[i]],
-                                    ALU.mult)
-
-        def scatter_whole(c, values):
-            nc.vector.tensor_tensor(page[c][:].indirect(slots[:]), values, wgs_sb[:], ALU.mult)
+        def scatter(c, values, offsets, weights):
+            nc.vector.tensor_tensor(page[c][:].indirect(offsets), values, weights, ALU.mult)
 
         def store_page(c):
             nc.sync.dma_start(out=out_1[c * P : (c + 1) * P, :], in_=page[c][:])
@@ -197,14 +201,14 @@ def tile_list_narrator_prefix_cache_kernel(
         def turn(c, k):
             g, place = divmod(c, GROUP_TILES)
             if place == 0:
-                tag = "wc_raw0" if (g, k) == (1, CHUNKS - 1) else f"turned{k}"
+                tag = "wc_raw1" if (g, k) == (1, CHUNKS - 1) else f"turned{k}"
                 turned.update({(g, k): keep.tile([P, 4, 2, 2 * P], BF16, name=f"turned{g}{k}", tag=tag, align_bytes=ALIGN)})
-            bank = turn_banks.tile([P, 4, P], F32, name="turn_bank", tag="turn_bank")
+            bank = turn_banks[k % 2]
             for b in range(4):
-                nc.tensor.transpose(bank[:, b, :], page[c][:, k * BANK + b * P : k * BANK + (b + 1) * P], ident[:])
+                nc.tensor.transpose(bank[:, b * P : (b + 1) * P], page[c][:, k * BANK + b * P : k * BANK + (b + 1) * P], ident[:])
             nc.scalar.copy(
                 turned[(g, k)][:, :, :, 64 * place : 64 * (place + 1)].rearrange("s b u (p e) -> s b u p e", e=2),
-                bank[:].rearrange("s b (p u e) -> s b u p e", u=2, e=2))
+                bank[:].rearrange("s (b p u e) -> s b u p e", b=4, u=2, e=2))
 
         page_codes = [keep.tile([P, T2], I32, name=f"page_codes{g}", align_bytes=ALIGN) for g in range(2)]
         page_scale = [keep.tile([P, T2], U8, name=f"page_scale{g}", align_bytes=ALIGN) for g in range(2)]
@@ -215,14 +219,13 @@ def tile_list_narrator_prefix_cache_kernel(
             woven_flat = woven[:].rearrange("p s j -> p (s j)")
             woven_pairs = woven_flat.bitcast(F32)
             for two_blocks in range(2):
-                bank = back_banks.tile([P, 2, 2, P], F32, name="back_bank", tag="back_bank")
-                for b in range(2):
-                    for u in range(2):
-                        at = ((2 * two_blocks + b) * 2 + u) * P
-                        nc.tensor.transpose(bank[:, b, u, :], pairs[:, at : at + P], ident[:])
+                bank = back_banks[two_blocks]
+                for bu in range(4):
+                    at = (4 * two_blocks + bu) * P
+                    nc.tensor.transpose(bank[:, bu * P : (bu + 1) * P], pairs[:, at : at + P], ident[:])
                 nc.scalar.copy(
                     woven_pairs[:, two_blocks * BANK : (two_blocks + 1) * BANK].rearrange("p (b s u) -> p b s u", b=2, u=2),
-                    bank[:].rearrange("p b u s -> p b s u"))
+                    bank[:].rearrange("p (b u s) -> p b s u", b=2, u=2))
             cols = slice(k * BANK, (k + 1) * BANK)
             nc.vector.quantize_mx(out=page_codes[g][:, cols].bitcast(FP8X4), scales=page_scale[g][:, cols], in_=woven_flat)
 
@@ -236,7 +239,7 @@ def tile_list_narrator_prefix_cache_kernel(
         def second_stage(k):
             cols = slice(k * BANK, (k + 1) * BANK)
             for n in range(N // P):
-                bank = mx_banks.tile([P, BANK], F32, name="mx_bank", tag="mx_bank")
+                bank = product_banks[n]
                 for g in range(2):
                     nc.tensor.matmul_mx(out=bank[:], lhsT=w8[:, g, n * P : (n + 1) * P].bitcast(FP8X4),
                                         lhsT_scale=w8_scale[:, g, n * P : (n + 1) * P],
@@ -249,39 +252,36 @@ def tile_list_narrator_prefix_cache_kernel(
                 elif n % 2 == 1:
                     nc.sync.dma_start(out=out_rows[:, n - 1 : n + 1, cols], in_=result[n // 2][:, :, cols])
 
-        for c in range(GROUP_TILES):
-            if half_tags[(c, 0)] == "scene_raw1":
-                scene_q.append(quantise_operand(scene_raw[1], "scene1", "woven3"))
-            first_stage(c, 0)
-            apply_gain(c, hidden[(c, 0)], hidden[(c, 0)])
-            scatter_half(c, 0)
-        for c in range(GROUP_TILES):
-            if half_tags[(c, 1)] == "wc_raw1":
-                wc_q.append(quantise_operand(wc_raw[1], "wc1", "woven2"))
-            first_stage(c, 1)
-            apply_gain(c, hidden[(c, 1)], hidden[(c, 1)])
-        for c in range(GROUP_TILES):
-            scatter_half(c, 1)
+        for c in range(PAGE_TILES):
+            if c == 2:
+                later = [weave_operand(wc_raw[i], f"wc{i}", f"woven{(i + 2) % 4}", nc.scalar.copy) for i in (1, 2)]
+                wc_q.extend(quantise_operand(later[i - 1], f"wc{i}") for i in (1, 2))
+            if c % 2 == 0:
+                pairs_of_h.append(keep.tile([P, 2, S], F32, name=f"hidden{c}", tag=pair_tags[c // 2], align_bytes=ALIGN))
+            for i in range(2):
+                first_stage(c, i)
+                if c == 0:
+                    apply_gain(c, hidden(c)[:, halves[i]], hidden(c)[:, halves[i]])
+                    scatter(c, hidden(c)[:, halves[i]], slots[:, list_halves[i]], wgs_sb[:, halves[i]])
+            if 0 < c < LAST_TILE:
+                apply_gain(c, hidden(c), hidden(c))
+        for c in range(LAST_TILE):
+            if c > 0:
+                scatter(c, hidden(c), slots[:], wgs_sb[:])
             store_page(c)
+        for c in range(GROUP_TILES):
             for k in range(CHUNKS):
                 turn(c, k)
-            ahead = c + GROUP_TILES
-            first_stage(ahead, 0)
-            first_stage(ahead, 1)
-            if ahead < LAST_TILE:
-                apply_gain(ahead, hidden[ahead], hidden[ahead])
         for k in range(CHUNKS):
             quantise_page(0, k)
         last_values = keep.tile([P, S], F32, tag=f"turned{CHUNKS - 1}", align_bytes=ALIGN)
-        apply_gain(LAST_TILE, last_values[:], hidden[LAST_TILE])
+        apply_gain(LAST_TILE, last_values[:], hidden(LAST_TILE))
         for c in range(GROUP_TILES, LAST_TILE):
-            scatter_whole(c, hidden[c])
-            store_page(c)
             for k in range(CHUNKS):
                 turn(c, k)
         store_codes(0, slice(0, T2))
         store_scales(0)
-        scatter_whole(LAST_TILE, last_values[:])
+        scatter(LAST_TILE, last_values[:], slots[:], wgs_sb[:])
         store_page(LAST_TILE)
         turn(LAST_TILE, 0)
         for k in range(CHUNKS):

@@ -38,7 +38,12 @@ def tile_list_narrator_prefix_cache_kernel(
         keep = ctx.enter_context(tc.tile_pool(name="keep", bufs=1))
         psum = ctx.enter_context(tc.psum_pool(name="psum", bufs=1))
         banks = [psum.tile([P, BANK], F32, name=f"bank{b}") for b in range(8)]
-        product_banks, turn_banks, back_banks = banks[0:4], banks[4:6], banks[6:8]
+        product_banks = banks[0:4]
+        fills = []
+
+        def next_bank(ring):
+            fills.append(len(fills))
+            return ring[fills[-1] % len(ring)]
 
         halves = [slice(0, BANK), slice(BANK, S)]
         list_halves = [slice(0, BANK // LIST_ROWS), slice(BANK // LIST_ROWS, S // LIST_ROWS)]
@@ -71,7 +76,7 @@ def tile_list_narrator_prefix_cache_kernel(
         slots = lists.tile([P, S // LIST_ROWS], U16)
         scene_rows = scene.rearrange("(p j) s -> p j s", j=PACK)
         wc_rows = wc.rearrange("(p j) c -> p j c", j=PACK)
-        wc_pieces = [slice(0, 2 * P), slice(2 * P, 4 * P), slice(4 * P, H)]
+        wc_pieces = [slice(2 * P * i, 2 * P * (i + 1)) for i in range(4)]
         w4_pieces = [slice(0, 2 * P), slice(2 * P, H)]
         scene_raw = [keep.tile([P, PACK, BANK], F32, name=f"scene_raw{i}", tag=f"scene_raw{i}", align_bytes=ALIGN)
                      for i in range(2)]
@@ -119,6 +124,7 @@ def tile_list_narrator_prefix_cache_kernel(
         load_wgs(1)
         load_wc(1)
         load_wc(2)
+        load_wc(3)
         load_page(1)
         load_w4(1)
         for c in range(2, PAGE_TILES):
@@ -126,8 +132,8 @@ def tile_list_narrator_prefix_cache_kernel(
         nc.sync.dma_start(out=w8[:], in_=w8_words.rearrange("a p c i -> p a (c i)").bitcast(I32))
 
         gain_cols = keep.tile([P, PAGE_TILES], F32)
-        nc.tensor.transpose(turn_banks[1][:, 0:P], gain_rows[:], ident[:])
-        nc.scalar.copy(gain_cols[:], turn_banks[1][:, 0:PAGE_TILES])
+        nc.tensor.transpose(banks[7][:, 0:P], gain_rows[:], ident[:])
+        nc.scalar.copy(gain_cols[:], banks[7][:, 0:PAGE_TILES])
 
         picked_rows = keep.tile([P, 2, S], U8, align_bytes=ALIGN)
         for a in range(2):
@@ -166,14 +172,13 @@ def tile_list_narrator_prefix_cache_kernel(
             i = max(j for j, cols in enumerate(pieces) if cols.start <= c * P)
             return i, c * P - pieces[i].start
 
-        pair_tags = ["hidden01", "wc_raw2", "scene_raw0", "scene_raw1"]
-        pairs_of_h = []
+        tiles_of_h = []
 
         def hidden(c):
-            return pairs_of_h[c // 2][:, c % 2, :]
+            return tiles_of_h[c]
 
         def first_stage(c, i):
-            bank = banks[(2 * c + i + 6) % 8]
+            bank = banks[(2 * c + i) % 8]
             piece, at = piece_of(w4_pieces, c)
             for a in range(2):
                 nc.tensor.matmul_mx(out=bank[:], lhsT=w4[piece][:, a, 2 * at : 2 * (at + P)].bitcast(FP4X4),
@@ -198,12 +203,12 @@ def tile_list_narrator_prefix_cache_kernel(
 
         turned = {}
 
-        def turn(c, k):
+        def turn(c, k, ring):
             g, place = divmod(c, GROUP_TILES)
             if place == 0:
                 tag = "wc_raw1" if (g, k) == (1, CHUNKS - 1) else f"turned{k}"
                 turned.update({(g, k): keep.tile([P, 4, 2, 2 * P], BF16, name=f"turned{g}{k}", tag=tag, align_bytes=ALIGN)})
-            bank = turn_banks[k % 2]
+            bank = next_bank(ring)
             for b in range(4):
                 nc.tensor.transpose(bank[:, b * P : (b + 1) * P], page[c][:, k * BANK + b * P : k * BANK + (b + 1) * P], ident[:])
             nc.scalar.copy(
@@ -213,13 +218,13 @@ def tile_list_narrator_prefix_cache_kernel(
         page_codes = [keep.tile([P, T2], I32, name=f"page_codes{g}", align_bytes=ALIGN) for g in range(2)]
         page_scale = [keep.tile([P, T2], U8, name=f"page_scale{g}", align_bytes=ALIGN) for g in range(2)]
 
-        def quantise_page(g, k):
+        def quantise_page(g, k, ring):
             pairs = turned[(g, k)][:].rearrange("s b u w -> s (b u w)").bitcast(F32)
             woven = keep.tile([P, BANK, PACK], BF16, name=f"woven{g}{k}", tag=f"woven{k}", align_bytes=ALIGN)
             woven_flat = woven[:].rearrange("p s j -> p (s j)")
             woven_pairs = woven_flat.bitcast(F32)
             for two_blocks in range(2):
-                bank = back_banks[two_blocks]
+                bank = next_bank(ring)
                 for bu in range(4):
                     at = (4 * two_blocks + bu) * P
                     nc.tensor.transpose(bank[:, bu * P : (bu + 1) * P], pairs[:, at : at + P], ident[:])
@@ -254,10 +259,14 @@ def tile_list_narrator_prefix_cache_kernel(
 
         for c in range(PAGE_TILES):
             if c == 2:
-                later = [weave_operand(wc_raw[i], f"wc{i}", f"woven{(i + 2) % 4}", nc.scalar.copy) for i in (1, 2)]
-                wc_q.extend(quantise_operand(later[i - 1], f"wc{i}") for i in (1, 2))
-            if c % 2 == 0:
-                pairs_of_h.append(keep.tile([P, 2, S], F32, name=f"hidden{c}", tag=pair_tags[c // 2], align_bytes=ALIGN))
+                later = [weave_operand(wc_raw[i], f"wc{i}", f"woven{(i + 2) % 4}", nc.scalar.copy) for i in (1, 2, 3)]
+                wc_q.extend(quantise_operand(later[i - 1], f"wc{i}") for i in (1, 2, 3))
+            if c < GROUP_TILES:
+                tag = ["hidden0", "hidden1", "wc_raw3", "wc_raw2"][c]
+                tiles_of_h.append(keep.tile([P, S], F32, name=f"hidden{c}", tag=tag, align_bytes=ALIGN)[:])
+            elif c % 2 == 0:
+                pair = keep.tile([P, 2, S], F32, name=f"hidden{c}", tag=f"scene_raw{c // 2 - 2}", align_bytes=ALIGN)
+                tiles_of_h.extend([pair[:, 0, :], pair[:, 1, :]])
             for i in range(2):
                 first_stage(c, i)
                 if c == 0:
@@ -271,23 +280,23 @@ def tile_list_narrator_prefix_cache_kernel(
             store_page(c)
         for c in range(GROUP_TILES):
             for k in range(CHUNKS):
-                turn(c, k)
+                turn(c, k, banks)
         for k in range(CHUNKS):
-            quantise_page(0, k)
+            quantise_page(0, k, banks)
         last_values = keep.tile([P, S], F32, tag=f"turned{CHUNKS - 1}", align_bytes=ALIGN)
         apply_gain(LAST_TILE, last_values[:], hidden(LAST_TILE))
         for c in range(GROUP_TILES, LAST_TILE):
             for k in range(CHUNKS):
-                turn(c, k)
+                turn(c, k, banks)
         store_codes(0, slice(0, T2))
         store_scales(0)
         scatter(LAST_TILE, last_values[:], slots[:], wgs_sb[:])
         store_page(LAST_TILE)
-        turn(LAST_TILE, 0)
+        turn(LAST_TILE, 0, banks[4:])
         for k in range(CHUNKS):
             if k + 1 < CHUNKS:
-                turn(LAST_TILE, k + 1)
-            quantise_page(1, k)
+                turn(LAST_TILE, k + 1, banks[4:])
+            quantise_page(1, k, banks[4:])
             store_codes(1, slice(k * BANK, (k + 1) * BANK))
         store_scales(1)
         for k in range(CHUNKS):

@@ -38,10 +38,10 @@ def tile_list_narrator_prefix_cache_kernel(
         keep = ctx.enter_context(tc.tile_pool(name="keep", bufs=1))
         psum = ctx.enter_context(tc.psum_pool(name="psum", bufs=1))
         banks = [psum.tile([P, BANK], F32, name=f"bank{b}") for b in range(8)]
-        product_banks = banks[0:4]
+        ring = banks[0:6]
         fills = []
 
-        def next_bank(ring):
+        def next_bank():
             fills.append(len(fills))
             return ring[fills[-1] % len(ring)]
 
@@ -56,20 +56,21 @@ def tile_list_narrator_prefix_cache_kernel(
                 nc.gpsimd.dma_start(out=plane_rows(planes, q),
                                     in_=scales[:, 4 * q : 4 * q + 4, :].rearrange("a q c -> q a c").bitcast(I32))
 
-        tab_scale_rows = keep.tile([P, 2, T], U8, tag="picking", align_bytes=ALIGN)
+        tab_scale_rows = keep.tile([P, T], U8, tag="picking", align_bytes=ALIGN)
         picked_scale = keep.tile([P, 2, S], U8, align_bytes=ALIGN)
         w4_scale = keep.tile([P, 2, H], U8, align_bytes=ALIGN)
         w8_scale = keep.tile([P, 2, N], U8, align_bytes=ALIGN)
         gain_rows = keep.tile([P, P], F32)
         ident = keep.tile([P, P], F32)
-        nc.vector.memset(tab_scale_rows[:, 0, :].bitcast(I32), 0)
-        nc.gpsimd.memset(tab_scale_rows[:, 1, :].bitcast(I32), 0)
+        nc.vector.memset(tab_scale_rows[:].bitcast(I32), 0)
         nc.vector.memset(w4_scale[:].bitcast(I32), 0)
         nc.vector.memset(picked_scale[:].bitcast(I32), 0)
         nc.vector.memset(w8_scale[:].bitcast(I32), 0)
         load_scale_planes(w4_scale, w4_scales)
         nc.gpsimd.memset(gain_rows[:], 0.0)
-        nc.scalar.dma_start(out=gain_rows[0:PAGE_TILES, :], in_=gain.rearrange("(c p) -> c p", p=P))
+        nc.scalar.dma_start(out=gain_rows[0:GROUP_TILES, :], in_=gain[0 : GROUP_TILES * P].rearrange("(c p) -> c p", p=P))
+        gain_dealt = keep.tile([P, PACK], F32)
+        nc.scalar.dma_start(out=gain_dealt[:], in_=gain[GROUP_TILES * P :].rearrange("(p t) -> p t", t=PACK))
         make_identity(nc, ident[:])
 
         picks = lists.tile([P, S // LIST_ROWS], U16)
@@ -77,7 +78,7 @@ def tile_list_narrator_prefix_cache_kernel(
         scene_rows = scene.rearrange("(p j) s -> p j s", j=PACK)
         wc_rows = wc.rearrange("(p j) c -> p j c", j=PACK)
         wc_pieces = [slice(2 * P * i, 2 * P * (i + 1)) for i in range(4)]
-        w4_pieces = [slice(0, 2 * P), slice(2 * P, H)]
+        w4_pieces = [slice(0, 2 * P), slice(2 * P, 4 * P), slice(4 * P, H)]
         scene_raw = [keep.tile([P, PACK, BANK], F32, name=f"scene_raw{i}", tag=f"scene_raw{i}", align_bytes=ALIGN)
                      for i in range(2)]
         wc_raw = [keep.tile([P, PACK, cols.stop - cols.start], F32, name=f"wc_raw{i}", tag=f"wc_raw{i}", align_bytes=ALIGN)
@@ -89,8 +90,13 @@ def tile_list_narrator_prefix_cache_kernel(
         page = [keep.tile([P, T2], F32, name=f"page{c}") for c in range(PAGE_TILES)]
         w8 = keep.tile([P, 2, N], I32, align_bytes=ALIGN)
 
+        def rows_of_tile(matrix, c):
+            if c < GROUP_TILES:
+                return matrix[c * P : (c + 1) * P, :]
+            return matrix[GROUP_TILES * P :, :].rearrange("(p t) s -> t p s", t=PACK)[c - GROUP_TILES]
+
         def load_page(c):
-            nc.sync.dma_start(out=page[c][:], in_=page0[c * P : (c + 1) * P, :])
+            nc.sync.dma_start(out=page[c][:], in_=rows_of_tile(page0, c))
 
         def load_table(a, cols):
             nc.sync.dma_start(out=tab[a][:, cols], in_=tab_words[a].rearrange("p t i -> p (t i)").bitcast(I32)[:, cols])
@@ -101,9 +107,6 @@ def tile_list_narrator_prefix_cache_kernel(
         def load_scene(i):
             nc.sync.dma_start(out=scene_raw[i][:], in_=scene_rows[:, :, halves[i]])
 
-        def load_wgs(i):
-            nc.sync.dma_start(out=wgs_sb[:, halves[i]], in_=wgs[:, halves[i]])
-
         def load_w4(i):
             cols = w4_pieces[i]
             columns = w4_words.rearrange("a p c -> p a c")[:, :, 2 * cols.start : 2 * cols.stop]
@@ -111,17 +114,17 @@ def tile_list_narrator_prefix_cache_kernel(
 
         nc.sync.dma_start(picks[:], offs)
         load_table(0, slice(0, T // 4))
-        nc.sync.dma_start(out=tab_scale_rows[0:P:8, :, :].bitcast(I32), in_=tab_scales.rearrange("a q t -> q a t").bitcast(I32))
+        nc.sync.dma_start(out=tab_scale_rows[0:P:4, :].bitcast(I32), in_=tab_scales.rearrange("a q t -> (a q) t").bitcast(I32))
+        nc.sync.dma_start(out=wgs_sb[:], in_=wgs)
         load_table(0, slice(T // 4, T))
+        load_w4(2)
         load_table(1, slice(0, T))
         load_wc(0)
         load_scene(0)
         load_scene(1)
         load_w4(0)
         nc.sync.dma_start(slots[:], offs2)
-        load_wgs(0)
         load_page(0)
-        load_wgs(1)
         load_wc(1)
         load_wc(2)
         load_wc(3)
@@ -131,19 +134,36 @@ def tile_list_narrator_prefix_cache_kernel(
             load_page(c)
         nc.sync.dma_start(out=w8[:], in_=w8_words.rearrange("a p c i -> p a (c i)").bitcast(I32))
 
-        gain_cols = keep.tile([P, PAGE_TILES], F32)
-        nc.tensor.transpose(banks[7][:, 0:P], gain_rows[:], ident[:])
-        nc.scalar.copy(gain_cols[:], banks[7][:, 0:PAGE_TILES])
+        gain_cols = keep.tile([P, GROUP_TILES], F32)
+        nc.tensor.transpose(banks[5][:, 0:P], gain_rows[:], ident[:])
+        nc.scalar.copy(gain_cols[:], banks[5][:, 0:GROUP_TILES])
 
-        picked_rows = keep.tile([P, 2, S], U8, align_bytes=ALIGN)
+        factors = [keep.tile([P, S], F32, name=f"factors{t}") for t in range(PACK)]
+        wgs_turned = [keep.tile([P, 2, PACK, QUADRANTS, 32], F32, name=f"wgs_turned{k}", tag=f"turned{k}", align_bytes=ALIGN)
+                      for k in range(4)]
+        for i in range(2):
+            bank = banks[6 + i]
+            for b in range(4):
+                nc.tensor.transpose(bank[:, b * P : (b + 1) * P], wgs_sb[:, (4 * i + b) * P : (4 * i + b + 1) * P], ident[:])
+            for pair in range(2):
+                rows = bank[:, 2 * pair * P : 2 * (pair + 1) * P].rearrange("j (b q t) -> j b t q", b=2, t=PACK)
+                nc.scalar.copy(wgs_turned[2 * i + pair][:], rows.unsqueeze(3).to_broadcast([P, 2, PACK, QUADRANTS, 32]))
+
+        picked_rows = keep.tile([P, S], U8, align_bytes=ALIGN)
+        nc.vector.tensor_copy(picked_rows[:], tab_scale_rows[:].indirect(picks[:]))
         for a in range(2):
-            nc.vector.tensor_copy(picked_rows[:, a, :], tab_scale_rows[:, a, :].indirect(picks[:]))
-        for q in range(QUADRANTS):
-            nc.gpsimd.dma_start(out=plane_rows(picked_scale, q), in_=picked_rows[32 * q : 32 * q + 32 : 8, :, :].bitcast(I32))
+            for q in range(QUADRANTS):
+                first = 4 * (16 * a + 4 * q)
+                nc.gpsimd.dma_start(out=plane_rows(picked_scale[:, a, :], q), in_=picked_rows[first : first + 16 : 4, :].bitcast(I32))
         load_scale_planes(w8_scale, w8_scales)
         picked = keep.tile([P, 2, S], U32, tag="picking", align_bytes=ALIGN)
         for a in range(2):
             nc.vector.tensor_copy(picked[:, a, :], tab[a][:].bitcast(U32).indirect(picks[:]))
+
+        w4_dealt = keep.tile([P, 2, PACK, P, 2], U8, align_bytes=ALIGN)
+        w4_scale_dealt = keep.tile([P, 2, PACK, P], U8, align_bytes=ALIGN)
+        nc.vector.tensor_copy(w4_dealt[:], w4[2][:].rearrange("p a (q t e) -> p a t q e", t=PACK, e=2))
+        nc.vector.tensor_copy(w4_scale_dealt[:], w4_scale[:, :, GROUP_TILES * P :].rearrange("p a (q t) -> p a t q", t=PACK))
 
         result = [keep.tile([P, 2, T2], F32, name=f"result{a}", tag=f"table_then_result{a}") for a in range(2)]
         bias_rows = bias.rearrange("(n p) t -> p n t", p=P)
@@ -172,25 +192,29 @@ def tile_list_narrator_prefix_cache_kernel(
             i = max(j for j, cols in enumerate(pieces) if cols.start <= c * P)
             return i, c * P - pieces[i].start
 
-        tiles_of_h = []
+        hidden = {}
 
-        def hidden(c):
-            return tiles_of_h[c]
-
-        def first_stage(c, i):
-            bank = banks[(2 * c + i) % 8]
-            piece, at = piece_of(w4_pieces, c)
+        def first_sum(c, i, bank):
+            if c < GROUP_TILES:
+                piece, at = piece_of(w4_pieces, c)
+                words = [w4[piece][:, a, 2 * at : 2 * (at + P)] for a in range(2)]
+                scales = [w4_scale[:, a, c * P : (c + 1) * P] for a in range(2)]
+                piece, at = piece_of(wc_pieces, c)
+            else:
+                words = [w4_dealt[:, a, c - GROUP_TILES].rearrange("p q e -> p (q e)") for a in range(2)]
+                scales = [w4_scale_dealt[:, a, c - GROUP_TILES] for a in range(2)]
+                piece, at = 2, (c - GROUP_TILES) * P
             for a in range(2):
-                nc.tensor.matmul_mx(out=bank[:], lhsT=w4[piece][:, a, 2 * at : 2 * (at + P)].bitcast(FP4X4),
-                                    lhsT_scale=w4_scale[:, a, c * P : (c + 1) * P],
+                nc.tensor.matmul_mx(out=bank[:], lhsT=words[a].bitcast(FP4X4), lhsT_scale=scales[a],
                                     rhs=picked[:, a, halves[i]].bitcast(FP8X4), rhs_scale=picked_scale[:, a, halves[i]],
                                     start=(a == 0), stop=False)
-            piece, at = piece_of(wc_pieces, c)
             wc_codes, wc_scale = wc_q[piece]
             scene_codes, scene_scale = scene_q[i]
             nc.tensor.matmul_mx(out=bank[:], lhsT=wc_codes[:, at : at + P].bitcast(FP8X4), lhsT_scale=wc_scale[:, at : at + P],
                                 rhs=scene_codes[:].bitcast(FP8X4), rhs_scale=scene_scale[:], start=False, stop=True)
-            nc.scalar.activation(hidden(c)[:, halves[i]], bank[:], ACT.Gelu_apprx_tanh)
+
+        def gelu(c, i, bank):
+            nc.scalar.activation(hidden[c][:, halves[i]], bank[:], ACT.Gelu_apprx_tanh)
 
         def apply_gain(c, out, in_):
             nc.scalar.activation(out, in_, ACT.Copy, scale=gain_cols[:, c : c + 1])
@@ -199,40 +223,57 @@ def tile_list_narrator_prefix_cache_kernel(
             nc.vector.tensor_tensor(page[c][:].indirect(offsets), values, weights, ALU.mult)
 
         def store_page(c):
-            nc.sync.dma_start(out=out_1[c * P : (c + 1) * P, :], in_=page[c][:])
+            nc.sync.dma_start(out=rows_of_tile(out_1, c), in_=page[c][:])
 
         turned = {}
 
-        def turn(c, k, ring):
-            g, place = divmod(c, GROUP_TILES)
-            if place == 0:
-                tag = "wc_raw1" if (g, k) == (1, CHUNKS - 1) else f"turned{k}"
-                turned.update({(g, k): keep.tile([P, 4, 2, 2 * P], BF16, name=f"turned{g}{k}", tag=tag, align_bytes=ALIGN)})
-            bank = next_bank(ring)
+        def turn(c, k):
+            if c == 0:
+                turned.update({k: keep.tile([P, 4, 2, 2 * P], BF16, name=f"turned{k}", tag=f"turned{k}", align_bytes=ALIGN)})
+            bank = next_bank()
             for b in range(4):
                 nc.tensor.transpose(bank[:, b * P : (b + 1) * P], page[c][:, k * BANK + b * P : k * BANK + (b + 1) * P], ident[:])
             nc.scalar.copy(
-                turned[(g, k)][:, :, :, 64 * place : 64 * (place + 1)].rearrange("s b u (p e) -> s b u p e", e=2),
+                turned[k][:, :, :, 64 * c : 64 * (c + 1)].rearrange("s b u (p e) -> s b u p e", e=2),
                 bank[:].rearrange("s (b p u e) -> s b u p e", b=4, u=2, e=2))
 
         page_codes = [keep.tile([P, T2], I32, name=f"page_codes{g}", align_bytes=ALIGN) for g in range(2)]
         page_scale = [keep.tile([P, T2], U8, name=f"page_scale{g}", align_bytes=ALIGN) for g in range(2)]
 
-        def quantise_page(g, k, ring):
-            pairs = turned[(g, k)][:].rearrange("s b u w -> s (b u w)").bitcast(F32)
-            woven = keep.tile([P, BANK, PACK], BF16, name=f"woven{g}{k}", tag=f"woven{k}", align_bytes=ALIGN)
-            woven_flat = woven[:].rearrange("p s j -> p (s j)")
-            woven_pairs = woven_flat.bitcast(F32)
+        def woven_chunk(g, k):
+            return keep.tile([P, BANK, PACK], BF16, name=f"woven{g}{k}", tag=f"woven{k}", align_bytes=ALIGN)
+
+        def quantise_page(g, k, woven):
+            cols = slice(k * BANK, (k + 1) * BANK)
+            nc.vector.quantize_mx(out=page_codes[g][:, cols].bitcast(FP8X4), scales=page_scale[g][:, cols],
+                                  in_=woven[:].rearrange("p s j -> p (s j)"))
+
+        def turn_back(k):
+            pairs = turned[k][:].rearrange("s b u w -> s (b u w)").bitcast(F32)
+            woven = woven_chunk(0, k)
+            woven_pairs = woven[:].rearrange("p s j -> p (s j)").bitcast(F32)
             for two_blocks in range(2):
-                bank = next_bank(ring)
+                bank = next_bank()
                 for bu in range(4):
                     at = (4 * two_blocks + bu) * P
                     nc.tensor.transpose(bank[:, bu * P : (bu + 1) * P], pairs[:, at : at + P], ident[:])
                 nc.scalar.copy(
                     woven_pairs[:, two_blocks * BANK : (two_blocks + 1) * BANK].rearrange("p (b s u) -> p b s u", b=2, u=2),
                     bank[:].rearrange("p (b u s) -> p b s u", b=2, u=2))
-            cols = slice(k * BANK, (k + 1) * BANK)
-            nc.vector.quantize_mx(out=page_codes[g][:, cols].bitcast(FP8X4), scales=page_scale[g][:, cols], in_=woven_flat)
+            return woven
+
+        rounded = {}
+
+        def round_chunk(c, k):
+            if c == GROUP_TILES:
+                tag = "wc_raw1" if k == CHUNKS - 1 else f"turned{k}"
+                rounded.update({k: keep.tile([P, PACK, BANK], BF16, name=f"rounded{k}", tag=tag, align_bytes=ALIGN)})
+            nc.scalar.copy(rounded[k][:, c - GROUP_TILES, :], page[c][:, k * BANK : (k + 1) * BANK])
+
+        def weave_chunk(k, copy):
+            woven = woven_chunk(1, k)
+            copy(woven[:].rearrange("p (c i) j -> p c j i", i=4), rounded[k][:].rearrange("p j (c i) -> p c j i", i=4))
+            return woven
 
         def store_codes(g, cols):
             nc.sync.dma_start(out=out_2[g].rearrange("p m t -> p (m t)").bitcast(I32)[:, cols], in_=page_codes[g][:, cols])
@@ -244,7 +285,7 @@ def tile_list_narrator_prefix_cache_kernel(
         def second_stage(k):
             cols = slice(k * BANK, (k + 1) * BANK)
             for n in range(N // P):
-                bank = product_banks[n]
+                bank = banks[4 * (k % 2) + n]
                 for g in range(2):
                     nc.tensor.matmul_mx(out=bank[:], lhsT=w8[:, g, n * P : (n + 1) * P].bitcast(FP8X4),
                                         lhsT_scale=w8_scale[:, g, n * P : (n + 1) * P],
@@ -257,46 +298,68 @@ def tile_list_narrator_prefix_cache_kernel(
                 elif n % 2 == 1:
                     nc.sync.dma_start(out=out_rows[:, n - 1 : n + 1, cols], in_=result[n // 2][:, :, cols])
 
-        for c in range(PAGE_TILES):
+        def make_factors():
+            for t in range(PACK):
+                for i in range(2):
+                    bank = banks[6 + i]
+                    for b in range(4):
+                        block = wgs_turned[2 * i + b // 2][:, b % 2, t].rearrange("j r q -> j (r q)")
+                        nc.tensor.transpose(bank[:, b * P : (b + 1) * P], block, ident[:])
+                    nc.scalar.activation(factors[t][:, halves[i]], bank[:], ACT.Copy, scale=gain_dealt[:, t : t + 1])
+
+        def tile_of_h(name, tag, count):
+            tile = keep.tile([P, count, S], F32, name=name, tag=tag, align_bytes=ALIGN)
+            return [tile[:, i, :] for i in range(count)]
+
+        for c in range(LAST_TILE):
+            if c == 0:
+                hidden.update(zip([0], tile_of_h("hidden0", "wc_raw0", 1)))
+            if c == 1:
+                hidden.update(zip([1, 6], tile_of_h("hidden16", "scene_raw1", 2)))
             if c == 2:
-                later = [weave_operand(wc_raw[i], f"wc{i}", f"woven{(i + 2) % 4}", nc.scalar.copy) for i in (1, 2, 3)]
-                wc_q.extend(quantise_operand(later[i - 1], f"wc{i}") for i in (1, 2, 3))
-            if c < GROUP_TILES:
-                tag = ["hidden0", "hidden1", "wc_raw3", "wc_raw2"][c]
-                tiles_of_h.append(keep.tile([P, S], F32, name=f"hidden{c}", tag=tag, align_bytes=ALIGN)[:])
-            elif c % 2 == 0:
-                pair = keep.tile([P, 2, S], F32, name=f"hidden{c}", tag=f"scene_raw{c // 2 - 2}", align_bytes=ALIGN)
-                tiles_of_h.extend([pair[:, 0, :], pair[:, 1, :]])
+                make_factors()
+                second = weave_operand(wc_raw[1], "wc1", "woven3", nc.scalar.copy)
+                dealt = keep.tile([P, BANK, PACK], BF16, name="wc_dealt_woven", tag="woven0", align_bytes=ALIGN)
+                for i in range(2):
+                    nc.scalar.copy(dealt[:].rearrange("p (t q) j -> p q j t", t=PACK)[:, 64 * i : 64 * (i + 1)],
+                                   wc_raw[2 + i][:].rearrange("p j (q t) -> p q j t", t=PACK))
+                wc_q.extend([quantise_operand(second, "wc1"), quantise_operand(dealt, "wc_dealt")])
+                hidden.update(zip([2], tile_of_h("hidden2", "wc_raw3", 1)))
+                hidden.update(zip([3], tile_of_h("hidden3", "wc_raw2", 1)))
+                hidden.update(zip([4, 5], tile_of_h("hidden45", "scene_raw0", 2)))
             for i in range(2):
-                first_stage(c, i)
+                bank = next_bank()
+                first_sum(c, i, bank)
+                gelu(c, i, bank)
                 if c == 0:
-                    apply_gain(c, hidden(c)[:, halves[i]], hidden(c)[:, halves[i]])
-                    scatter(c, hidden(c)[:, halves[i]], slots[:, list_halves[i]], wgs_sb[:, halves[i]])
-            if 0 < c < LAST_TILE:
-                apply_gain(c, hidden(c), hidden(c))
+                    apply_gain(c, hidden[c][:, halves[i]], hidden[c][:, halves[i]])
+                    scatter(c, hidden[c][:, halves[i]], slots[:, list_halves[i]], wgs_sb[:, halves[i]])
+            if 0 < c < GROUP_TILES:
+                apply_gain(c, hidden[c], hidden[c])
+        for i in range(2):
+            first_sum(LAST_TILE, i, banks[6 + i])
         for c in range(LAST_TILE):
             if c > 0:
-                scatter(c, hidden(c), slots[:], wgs_sb[:])
+                scatter(c, hidden[c], slots[:], wgs_sb[:] if c < GROUP_TILES else factors[c - GROUP_TILES][:])
             store_page(c)
         for c in range(GROUP_TILES):
             for k in range(CHUNKS):
-                turn(c, k, banks)
+                turn(c, k)
         for k in range(CHUNKS):
-            quantise_page(0, k, banks)
-        last_values = keep.tile([P, S], F32, tag=f"turned{CHUNKS - 1}", align_bytes=ALIGN)
-        apply_gain(LAST_TILE, last_values[:], hidden(LAST_TILE))
+            quantise_page(0, k, turn_back(k))
+        hidden.update(zip([LAST_TILE], tile_of_h("hidden7", f"turned{CHUNKS - 1}", 1)))
+        for i in range(2):
+            gelu(LAST_TILE, i, banks[6 + i])
         for c in range(GROUP_TILES, LAST_TILE):
             for k in range(CHUNKS):
-                turn(c, k, banks)
+                round_chunk(c, k)
         store_codes(0, slice(0, T2))
         store_scales(0)
-        scatter(LAST_TILE, last_values[:], slots[:], wgs_sb[:])
+        scatter(LAST_TILE, hidden[LAST_TILE], slots[:], factors[PACK - 1][:])
         store_page(LAST_TILE)
-        turn(LAST_TILE, 0, banks[4:])
         for k in range(CHUNKS):
-            if k + 1 < CHUNKS:
-                turn(LAST_TILE, k + 1, banks[4:])
-            quantise_page(1, k, banks[4:])
+            round_chunk(LAST_TILE, k)
+            quantise_page(1, k, weave_chunk(k, nc.vector.tensor_copy if k == 0 else nc.scalar.copy))
             store_codes(1, slice(k * BANK, (k + 1) * BANK))
         store_scales(1)
         for k in range(CHUNKS):

@@ -107,6 +107,9 @@ def tile_list_narrator_prefix_cache_kernel(
         def load_scene(i):
             nc.sync.dma_start(out=scene_raw[i][:], in_=scene_rows[:, :, halves[i]])
 
+        def load_wgs(i):
+            nc.sync.dma_start(out=wgs_sb[:, halves[i]], in_=wgs[:, halves[i]])
+
         def load_w4(i):
             cols = w4_pieces[i]
             columns = w4_words.rearrange("a p c -> p a c")[:, :, 2 * cols.start : 2 * cols.stop]
@@ -115,16 +118,17 @@ def tile_list_narrator_prefix_cache_kernel(
         nc.sync.dma_start(picks[:], offs)
         load_table(0, slice(0, T // 4))
         nc.sync.dma_start(out=tab_scale_rows[0:P:4, :].bitcast(I32), in_=tab_scales.rearrange("a q t -> (a q) t").bitcast(I32))
-        nc.sync.dma_start(out=wgs_sb[:], in_=wgs)
+        load_wgs(0)
         load_table(0, slice(T // 4, T))
         load_w4(2)
         load_table(1, slice(0, T))
+        load_w4(0)
         load_wc(0)
         load_scene(0)
         load_scene(1)
-        load_w4(0)
         nc.sync.dma_start(slots[:], offs2)
         load_page(0)
+        load_wgs(1)
         load_wc(1)
         load_wc(2)
         load_wc(3)
@@ -141,13 +145,16 @@ def tile_list_narrator_prefix_cache_kernel(
         factors = [keep.tile([P, S], F32, name=f"factors{t}") for t in range(PACK)]
         wgs_turned = [keep.tile([P, 2, PACK, QUADRANTS, 32], F32, name=f"wgs_turned{k}", tag=f"turned{k}", align_bytes=ALIGN)
                       for k in range(4)]
-        for i in range(2):
+
+        def turn_wgs(i):
             bank = banks[6 + i]
             for b in range(4):
                 nc.tensor.transpose(bank[:, b * P : (b + 1) * P], wgs_sb[:, (4 * i + b) * P : (4 * i + b + 1) * P], ident[:])
             for pair in range(2):
                 rows = bank[:, 2 * pair * P : 2 * (pair + 1) * P].rearrange("j (b q t) -> j b t q", b=2, t=PACK)
                 nc.scalar.copy(wgs_turned[2 * i + pair][:], rows.unsqueeze(3).to_broadcast([P, 2, PACK, QUADRANTS, 32]))
+
+        turn_wgs(0)
 
         picked_rows = keep.tile([P, S], U8, align_bytes=ALIGN)
         nc.vector.tensor_copy(picked_rows[:], tab_scale_rows[:].indirect(picks[:]))
@@ -301,7 +308,7 @@ def tile_list_narrator_prefix_cache_kernel(
         def make_factors():
             for t in range(PACK):
                 for i in range(2):
-                    bank = banks[6 + i]
+                    bank = next_bank()
                     for b in range(4):
                         block = wgs_turned[2 * i + b // 2][:, b % 2, t].rearrange("j r q -> j (r q)")
                         nc.tensor.transpose(bank[:, b * P : (b + 1) * P], block, ident[:])
@@ -317,6 +324,7 @@ def tile_list_narrator_prefix_cache_kernel(
             if c == 1:
                 hidden.update(zip([1, 6], tile_of_h("hidden16", "scene_raw1", 2)))
             if c == 2:
+                turn_wgs(1)
                 make_factors()
                 second = weave_operand(wc_raw[1], "wc1", "woven3", nc.scalar.copy)
                 dealt = keep.tile([P, BANK, PACK], BF16, name="wc_dealt_woven", tag="woven0", align_bytes=ALIGN)
@@ -360,7 +368,7 @@ def tile_list_narrator_prefix_cache_kernel(
         for k in range(CHUNKS):
             round_chunk(LAST_TILE, k)
             quantise_page(1, k, weave_chunk(k, nc.vector.tensor_copy if k == 0 else nc.scalar.copy))
-            store_codes(1, slice(k * BANK, (k + 1) * BANK))
         store_scales(1)
         for k in range(CHUNKS):
+            store_codes(1, slice(k * BANK, (k + 1) * BANK))
             second_stage(k)

@@ -250,8 +250,7 @@ def tile_list_narrator_prefix_cache_kernel(
         def woven_chunk(g, k):
             return keep.tile([P, BANK, PACK], BF16, name=f"woven{g}{k}", tag=f"woven{k}", align_bytes=ALIGN)
 
-        def quantise_page(g, k, woven):
-            cols = slice(k * BANK, (k + 1) * BANK)
+        def quantise_page(g, cols, woven):
             nc.vector.quantize_mx(out=page_codes[g][:, cols].bitcast(FP8X4), scales=page_scale[g][:, cols],
                                   in_=woven[:].rearrange("p s j -> p (s j)"))
 
@@ -269,17 +268,23 @@ def tile_list_narrator_prefix_cache_kernel(
                     bank[:].rearrange("p (b u s) -> p b s u", b=2, u=2))
             return woven
 
-        rounded = {}
+        pieces = [slice(0, BANK // 2), slice(BANK // 2, BANK)] + [slice(k * BANK, (k + 1) * BANK) for k in range(1, CHUNKS)]
+        pairs = {}
 
-        def round_chunk(c, k):
-            if c == GROUP_TILES:
-                tag = "wc_raw1" if k == CHUNKS - 1 else f"turned{k}"
-                rounded.update({k: keep.tile([P, PACK, BANK], BF16, name=f"rounded{k}", tag=tag, align_bytes=ALIGN)})
-            nc.scalar.copy(rounded[k][:, c - GROUP_TILES, :], page[c][:, k * BANK : (k + 1) * BANK])
+        def round_piece(c, i):
+            t = c - GROUP_TILES
+            if t == 0:
+                tag = ["turned0", "wc_raw0", "turned1", "turned2", "wc_raw1"][i]
+                width = pieces[i].stop - pieces[i].start
+                pairs.update({i: keep.tile([P, 2, width, 2], BF16, name=f"pairs{i}", tag=tag, align_bytes=ALIGN)})
+            nc.scalar.copy(pairs[i][:, t // 2, :, t % 2], page[c][:, pieces[i]])
 
-        def weave_chunk(k, copy):
-            woven = woven_chunk(1, k)
-            copy(woven[:].rearrange("p (c i) j -> p c j i", i=4), rounded[k][:].rearrange("p j (c i) -> p c j i", i=4))
+        def weave_piece(i):
+            width = pieces[i].stop - pieces[i].start
+            tag = ["woven0", "wc_raw3", "woven1", "woven2", "woven3"][i]
+            woven = keep.tile([P, width, PACK], BF16, name=f"woven1{i}", tag=tag, align_bytes=ALIGN)
+            words = woven[:].rearrange("p s j -> p (s j)").bitcast(U32).rearrange("p (s u) -> p s u", u=2)
+            nc.scalar.copy(words, pairs[i][:].rearrange("p u s e -> p u (s e)").bitcast(U32).rearrange("p u s -> p s u"))
             return woven
 
         def store_codes(g, cols):
@@ -289,19 +294,29 @@ def tile_list_narrator_prefix_cache_kernel(
             for q in range(QUADRANTS):
                 nc.gpsimd.dma_start(out=out_3[g, 4 * q : 4 * q + 4, :].bitcast(I32), in_=plane_rows(page_scale[g], q))
 
-        def second_stage(k):
-            cols = slice(k * BANK, (k + 1) * BANK)
-            for n in range(N // P):
-                bank = banks[4 * (k % 2) + n]
-                for g in range(2):
-                    nc.tensor.matmul_mx(out=bank[:], lhsT=w8[:, g, n * P : (n + 1) * P].bitcast(FP8X4),
+        def banks_of_piece(i):
+            if i < 2:
+                return [(banks[2 * i + a], [2 * a, 2 * a + 1]) for a in range(2)]
+            return [(banks[4 * ((i + 1) % 2) + n], [n]) for n in range(N // P)]
+
+        def second_passes(i, g):
+            cols = pieces[i]
+            width = cols.stop - cols.start
+            for bank, blocks in banks_of_piece(i):
+                for at, n in enumerate(blocks):
+                    nc.tensor.matmul_mx(out=bank[:, at * width : (at + 1) * width], lhsT=w8[:, g, n * P : (n + 1) * P].bitcast(FP8X4),
                                         lhsT_scale=w8_scale[:, g, n * P : (n + 1) * P],
                                         rhs=page_codes[g][:, cols].bitcast(FP8X4), rhs_scale=page_scale[g][:, cols],
-                                        start=(g == 0), stop=(g == 1))
-                sums = result[n // 2][:, n % 2, cols]
-                nc.vector.tensor_tensor(sums, bank[:], sums, ALU.add)
-                if k == CHUNKS - 1:
-                    nc.sync.dma_start(out=out_rows[:, n, cols], in_=sums)
+                                        start=(g == 0 and at == 0), stop=(g == 1 and at == len(blocks) - 1))
+
+        def add_and_store(i):
+            cols = pieces[i]
+            for bank, blocks in banks_of_piece(i):
+                n = blocks[-1]
+                sums = result[n // 2][:, blocks[0] % 2 : n % 2 + 1, cols]
+                nc.vector.tensor_tensor(sums, bank[:].rearrange("p (n s) -> p n s", n=len(blocks)), sums, ALU.add)
+                if i == len(pieces) - 1:
+                    nc.sync.dma_start(out=out_rows[:, n, cols], in_=result[n // 2][:, n % 2, cols])
                 elif n % 2 == 1:
                     nc.sync.dma_start(out=out_rows[:, n - 1 : n + 1, cols], in_=result[n // 2][:, :, cols])
 
@@ -354,21 +369,26 @@ def tile_list_narrator_prefix_cache_kernel(
             for k in range(CHUNKS):
                 turn(c, k)
         for k in range(CHUNKS):
-            quantise_page(0, k, turn_back(k))
+            quantise_page(0, slice(k * BANK, (k + 1) * BANK), turn_back(k))
         hidden.update(zip([LAST_TILE], tile_of_h("hidden7", f"turned{CHUNKS - 1}", 1)))
         for i in range(2):
             gelu(LAST_TILE, i, banks[6 + i])
         for c in range(GROUP_TILES, LAST_TILE):
-            for k in range(CHUNKS):
-                round_chunk(c, k)
+            for i in range(len(pieces)):
+                round_piece(c, i)
         store_codes(0, slice(0, T2))
         store_scales(0)
+        for i in range(3):
+            second_passes(i, 0)
         scatter(LAST_TILE, hidden[LAST_TILE], slots[:], factors[PACK - 1][:])
         store_page(LAST_TILE)
-        for k in range(CHUNKS):
-            round_chunk(LAST_TILE, k)
-            quantise_page(1, k, weave_chunk(k, nc.vector.tensor_copy if k == 0 else nc.scalar.copy))
-        store_scales(1)
-        for k in range(CHUNKS):
-            store_codes(1, slice(k * BANK, (k + 1) * BANK))
-            second_stage(k)
+        for i in range(len(pieces)):
+            round_piece(LAST_TILE, i)
+            quantise_page(1, pieces[i], weave_piece(i))
+            if i == len(pieces) - 1:
+                store_scales(1)
+            store_codes(1, pieces[i])
+            if i >= 3:
+                second_passes(i, 0)
+            second_passes(i, 1)
+            add_and_store(i)

@@ -127,12 +127,12 @@ def tile_list_narrator_prefix_cache_kernel(
         load_scene(0)
         load_scene(1)
         nc.sync.dma_start(slots[:], offs2)
+        load_page(1)
         load_page(0)
         load_wgs(1)
         load_wc(1)
         load_wc(2)
         load_wc(3)
-        load_page(1)
         load_w4(1)
         for c in range(2, PAGE_TILES):
             load_page(c)

@@ -20,10 +20,12 @@ PACK = 4
 QUADRANTS = 4
 LIST_ROWS = 16
 BANK = 512
+GROUP = 512
 PAGE_TILES = H // P
-GROUP_TILES = 4
+GROUP_TILES = GROUP // P
 LAST_TILE = PAGE_TILES - 1
 CHUNKS = T2 // BANK
+EARLY_CHUNKS = 2
 ALIGN = 64
 FLOPS = 2 * (1024 + 512) * H * S + 2 * H * N * T2
 
@@ -45,8 +47,12 @@ def tile_list_narrator_prefix_cache_kernel(
             fills.append(len(fills))
             return ring[fills[-1] % len(ring)]
 
+        def sbuf(name, shape, dtype, home=None):
+            return keep.tile([P] + shape, dtype, name=name, tag=home or name, align_bytes=ALIGN)
+
         halves = [slice(0, BANK), slice(BANK, S)]
         list_halves = [slice(0, BANK // LIST_ROWS), slice(BANK // LIST_ROWS, S // LIST_ROWS)]
+        chunks = [slice(k * BANK, (k + 1) * BANK) for k in range(CHUNKS)]
 
         def plane_rows(plane, q):
             return plane[32 * q : 32 * q + 4].bitcast(I32)
@@ -56,21 +62,19 @@ def tile_list_narrator_prefix_cache_kernel(
                 nc.gpsimd.dma_start(out=plane_rows(planes, q),
                                     in_=scales[:, 4 * q : 4 * q + 4, :].rearrange("a q c -> q a c").bitcast(I32))
 
-        tab_scale_rows = keep.tile([P, T], U8, tag="picking", align_bytes=ALIGN)
-        picked_scale = keep.tile([P, 2, S], U8, align_bytes=ALIGN)
-        w4_scale = keep.tile([P, 2, H], U8, align_bytes=ALIGN)
-        w8_scale = keep.tile([P, 2, N], U8, align_bytes=ALIGN)
-        gain_rows = keep.tile([P, P], F32)
-        ident = keep.tile([P, P], F32)
-        nc.vector.memset(tab_scale_rows[:].bitcast(I32), 0)
-        nc.vector.memset(w4_scale[:].bitcast(I32), 0)
-        nc.vector.memset(picked_scale[:].bitcast(I32), 0)
-        nc.vector.memset(w8_scale[:].bitcast(I32), 0)
+        tab_scale_rows = sbuf("tab_scale_rows", [T], U8, "picking")
+        picked_scale = sbuf("picked_scale", [2, S], U8)
+        w4_scale = sbuf("w4_scale", [2, H], U8)
+        w8_scale = sbuf("w8_scale", [2, N], U8)
+        gain_rows = sbuf("gain_rows", [P], F32)
+        gain_dealt = sbuf("gain_dealt", [PACK], F32)
+        ident = sbuf("ident", [P], F32)
+        for plane in (tab_scale_rows, w4_scale, picked_scale, w8_scale):
+            nc.vector.memset(plane[:].bitcast(I32), 0)
         load_scale_planes(w4_scale, w4_scales)
         nc.gpsimd.memset(gain_rows[:], 0.0)
-        nc.scalar.dma_start(out=gain_rows[0:GROUP_TILES, :], in_=gain[0 : GROUP_TILES * P].rearrange("(c p) -> c p", p=P))
-        gain_dealt = keep.tile([P, PACK], F32)
-        nc.scalar.dma_start(out=gain_dealt[:], in_=gain[GROUP_TILES * P :].rearrange("(p t) -> p t", t=PACK))
+        nc.scalar.dma_start(out=gain_rows[0:GROUP_TILES, :], in_=gain[0:GROUP].rearrange("(c p) -> c p", p=P))
+        nc.scalar.dma_start(out=gain_dealt[:], in_=gain[GROUP:].rearrange("(p t) -> p t", t=PACK))
         make_identity(nc, ident[:])
 
         picks = lists.tile([P, S // LIST_ROWS], U16)
@@ -78,22 +82,19 @@ def tile_list_narrator_prefix_cache_kernel(
         scene_rows = scene.rearrange("(p j) s -> p j s", j=PACK)
         wc_rows = wc.rearrange("(p j) c -> p j c", j=PACK)
         wc_pieces = [slice(2 * P * i, 2 * P * (i + 1)) for i in range(4)]
-        w4_pieces = [slice(0, 2 * P), slice(2 * P, 4 * P), slice(4 * P, H)]
-        scene_raw = [keep.tile([P, PACK, BANK], F32, name=f"scene_raw{i}", tag=f"scene_raw{i}", align_bytes=ALIGN)
-                     for i in range(2)]
-        wc_raw = [keep.tile([P, PACK, cols.stop - cols.start], F32, name=f"wc_raw{i}", tag=f"wc_raw{i}", align_bytes=ALIGN)
-                  for i, cols in enumerate(wc_pieces)]
-        tab = [keep.tile([P, T], I32, name=f"tab{a}", tag=f"table_then_result{a}") for a in range(2)]
-        w4 = [keep.tile([P, 2, 2 * (cols.stop - cols.start)], U8, name=f"w4_{i}", align_bytes=ALIGN)
-              for i, cols in enumerate(w4_pieces)]
-        wgs_sb = keep.tile([P, S], F32)
-        page = [keep.tile([P, T2], F32, name=f"page{c}") for c in range(PAGE_TILES)]
-        w8 = keep.tile([P, 2, N], I32, align_bytes=ALIGN)
+        w4_pieces = [slice(0, 2 * P), slice(2 * P, GROUP), slice(GROUP, H)]
+        scene_raw = [sbuf(f"scene_raw{i}", [PACK, BANK], F32) for i in range(2)]
+        wc_raw = [sbuf(f"wc_raw{i}", [PACK, 2 * P], F32) for i in range(4)]
+        tab = [sbuf(f"tab{a}", [T], I32, f"table_then_result{a}") for a in range(2)]
+        w4 = [sbuf(f"w4_{i}", [2, 2 * (cols.stop - cols.start)], U8) for i, cols in enumerate(w4_pieces)]
+        wgs_sb = sbuf("wgs_sb", [S], F32)
+        page = [sbuf(f"page{c}", [T2], F32) for c in range(PAGE_TILES)]
+        w8 = sbuf("w8", [2, N], I32)
 
         def rows_of_tile(matrix, c):
             if c < GROUP_TILES:
                 return matrix[c * P : (c + 1) * P, :]
-            return matrix[GROUP_TILES * P :, :].rearrange("(p t) s -> t p s", t=PACK)[c - GROUP_TILES]
+            return matrix[GROUP:, :].rearrange("(p t) s -> t p s", t=PACK)[c - GROUP_TILES]
 
         def load_page(c):
             nc.sync.dma_start(out=page[c][:], in_=rows_of_tile(page0, c))
@@ -120,143 +121,192 @@ def tile_list_narrator_prefix_cache_kernel(
         nc.sync.dma_start(out=tab_scale_rows[0:P:4, :].bitcast(I32), in_=tab_scales.rearrange("a q t -> (a q) t").bitcast(I32))
         load_wgs(0)
         load_table(0, slice(T // 4, T))
-        load_w4(2)
         load_table(1, slice(0, T))
+        load_scene(0)
         load_w4(0)
         load_wc(0)
-        load_scene(0)
         load_scene(1)
         nc.sync.dma_start(slots[:], offs2)
-        load_page(1)
         load_page(0)
-        load_wgs(1)
         load_wc(1)
+        load_wgs(1)
+        load_w4(1)
+        load_page(1)
         load_wc(2)
         load_wc(3)
-        load_w4(1)
+        load_w4(2)
         for c in range(2, PAGE_TILES):
             load_page(c)
         nc.sync.dma_start(out=w8[:], in_=w8_words.rearrange("a p c i -> p a (c i)").bitcast(I32))
 
-        gain_cols = keep.tile([P, GROUP_TILES], F32)
+        gain_cols = sbuf("gain_cols", [GROUP_TILES], F32)
         nc.tensor.transpose(banks[5][:, 0:P], gain_rows[:], ident[:])
         nc.scalar.copy(gain_cols[:], banks[5][:, 0:GROUP_TILES])
 
-        factors = [keep.tile([P, S], F32, name=f"factors{t}") for t in range(PACK)]
-        wgs_turned = [keep.tile([P, 2, PACK, QUADRANTS, 32], F32, name=f"wgs_turned{k}", tag=f"turned{k}", align_bytes=ALIGN)
-                      for k in range(4)]
+        wgs_dealt = [sbuf(f"wgs_dealt{t}", [S], F32) for t in range(PACK)]
+        wgs_turned = [sbuf(f"wgs_turned{k}", [2, PACK, QUADRANTS, 32], F32, f"turned{k}") for k in range(4)]
 
-        def turn_wgs(i):
-            bank = banks[6 + i]
+        def turn_wgs(i, first_bank):
             for b in range(4):
-                nc.tensor.transpose(bank[:, b * P : (b + 1) * P], wgs_sb[:, (4 * i + b) * P : (4 * i + b + 1) * P], ident[:])
+                nc.tensor.transpose(first_bank[:, b * P : (b + 1) * P], wgs_sb[:, (4 * i + b) * P : (4 * i + b + 1) * P], ident[:])
             for pair in range(2):
-                rows = bank[:, 2 * pair * P : 2 * (pair + 1) * P].rearrange("j (b q t) -> j b t q", b=2, t=PACK)
+                rows = first_bank[:, 2 * pair * P : 2 * (pair + 1) * P].rearrange("j (b q t) -> j b t q", b=2, t=PACK)
                 nc.scalar.copy(wgs_turned[2 * i + pair][:], rows.unsqueeze(3).to_broadcast([P, 2, PACK, QUADRANTS, 32]))
 
-        turn_wgs(0)
+        def deal_wgs(i, t, bank):
+            for b in range(4):
+                block = wgs_turned[2 * i + b // 2][:, b % 2, t].rearrange("j r q -> j (r q)")
+                nc.tensor.transpose(bank[:, b * P : (b + 1) * P], block, ident[:])
+            nc.scalar.copy(wgs_dealt[t][:, halves[i]], bank[:])
 
-        picked_rows = keep.tile([P, S], U8, align_bytes=ALIGN)
+        def times_gain(out, in_, column):
+            nc.scalar.activation(out, in_, ACT.Copy, scale=column)
+
+        first_factors = sbuf("first_factors", [BANK], F32)
+        times_gain(first_factors[:], wgs_sb[:, halves[0]], gain_cols[:, 0:1])
+        turn_wgs(0, banks[7])
+        for t in range(PACK):
+            deal_wgs(0, t, banks[6 + t % 2])
+
+        picked_rows = sbuf("picked_rows", [S], U8)
         nc.vector.tensor_copy(picked_rows[:], tab_scale_rows[:].indirect(picks[:]))
         for a in range(2):
             for q in range(QUADRANTS):
                 first = 4 * (16 * a + 4 * q)
                 nc.gpsimd.dma_start(out=plane_rows(picked_scale[:, a, :], q), in_=picked_rows[first : first + 16 : 4, :].bitcast(I32))
         load_scale_planes(w8_scale, w8_scales)
-        picked = keep.tile([P, 2, S], U32, tag="picking", align_bytes=ALIGN)
+        picked = sbuf("picked", [2, S], U32, "picking")
         for a in range(2):
             nc.vector.tensor_copy(picked[:, a, :], tab[a][:].bitcast(U32).indirect(picks[:]))
 
-        w4_dealt = keep.tile([P, 2, PACK, P, 2], U8, align_bytes=ALIGN)
-        w4_scale_dealt = keep.tile([P, 2, PACK, P], U8, align_bytes=ALIGN)
-        nc.vector.tensor_copy(w4_dealt[:], w4[2][:].rearrange("p a (q t e) -> p a t q e", t=PACK, e=2))
-        nc.vector.tensor_copy(w4_scale_dealt[:], w4_scale[:, :, GROUP_TILES * P :].rearrange("p a (q t) -> p a t q", t=PACK))
-
-        result = [keep.tile([P, 2, T2], F32, name=f"result{a}", tag=f"table_then_result{a}") for a in range(2)]
+        result = [sbuf(f"result{a}", [2, T2], F32, f"table_then_result{a}") for a in range(2)]
         bias_rows = bias.rearrange("(n p) t -> p n t", p=P)
         out_rows = out_0.rearrange("(n p) t -> p n t", p=P)
         for a in range(2):
             nc.sync.dma_start(out=result[a][:], in_=bias_rows[:, 2 * a : 2 * a + 2, :])
 
-        def weave_operand(raw, name, tag, copy):
-            width = raw.shape[2]
-            woven = keep.tile([P, width, PACK], BF16, name=name + "_woven", tag=tag, align_bytes=ALIGN)
-            copy(woven[:].rearrange("p (c i) j -> p c j i", i=4), raw[:].rearrange("p j (c i) -> p c j i", i=4))
-            return woven
+        def weave(woven, raw, copy):
+            copy(woven.rearrange("p (c i) j -> p c j i", i=4), raw[:].rearrange("p j (c i) -> p c j i", i=4))
 
-        def quantise_operand(woven, name):
-            width = woven.shape[1]
-            codes = keep.tile([P, width], U32, name=name + "_codes", align_bytes=ALIGN)
-            scale = keep.tile([P, width], U8, name=name + "_scale", align_bytes=ALIGN)
-            nc.vector.quantize_mx(out=codes[:].bitcast(FP8X4), scales=scale[:], in_=woven[:].rearrange("p c j -> p (c j)"))
+        def quantise(codes, scale, woven):
+            nc.vector.quantize_mx(out=codes.bitcast(FP8X4), scales=scale, in_=woven[:].rearrange("p c j -> p (c j)"))
+
+        def quantised_operand(name, raws, copy, woven_home, codes_home=None):
+            width = sum(raw.shape[2] for raw in raws)
+            woven = sbuf(name + "_woven", [width, PACK], BF16, woven_home)
+            for i, raw in enumerate(raws):
+                weave(woven[:, i * raw.shape[2] : (i + 1) * raw.shape[2]], raw, copy)
+            codes = sbuf(name + "_codes", [width], U32, codes_home)
+            scale = sbuf(name + "_scale", [width], U8)
+            quantise(codes[:], scale[:], woven)
             return codes, scale
 
-        wc_q = [quantise_operand(weave_operand(wc_raw[0], "wc0", "woven2", nc.scalar.copy), "wc0")]
-        scene_q = [quantise_operand(weave_operand(scene_raw[i], f"scene{i}", f"woven{i}", nc.vector.tensor_copy), f"scene{i}")
-                   for i in range(2)]
+        wc_q = [quantised_operand("wc0", wc_raw[0:1], nc.scalar.copy, "woven2")]
+        scene_q = [quantised_operand(f"scene{i}", scene_raw[i : i + 1], nc.vector.tensor_copy, f"woven{i}") for i in range(2)]
 
-        def piece_of(pieces, c):
-            i = max(j for j, cols in enumerate(pieces) if cols.start <= c * P)
-            return i, c * P - pieces[i].start
+        def mx_pass(out, stationary, moving, start, stop):
+            nc.tensor.matmul_mx(out=out, lhsT=stationary[0], lhsT_scale=stationary[1], rhs=moving[0], rhs_scale=moving[1],
+                                start=start, stop=stop)
 
-        hidden = {}
+        def w4_operand(a, piece, cols):
+            at = w4_pieces[piece].start
+            return w4[piece][:, a, 2 * (cols.start - at) : 2 * (cols.stop - at)].bitcast(FP4X4), w4_scale[:, a, cols]
 
-        def first_sum(c, i, bank):
-            if c < GROUP_TILES:
-                piece, at = piece_of(w4_pieces, c)
-                words = [w4[piece][:, a, 2 * at : 2 * (at + P)] for a in range(2)]
-                scales = [w4_scale[:, a, c * P : (c + 1) * P] for a in range(2)]
-                piece, at = piece_of(wc_pieces, c)
-            else:
-                words = [w4_dealt[:, a, c - GROUP_TILES].rearrange("p q e -> p (q e)") for a in range(2)]
-                scales = [w4_scale_dealt[:, a, c - GROUP_TILES] for a in range(2)]
-                piece, at = 2, (c - GROUP_TILES) * P
+        def picked_operand(a, entries):
+            return picked[:, a, entries].bitcast(FP8X4), picked_scale[:, a, entries]
+
+        def columns_of(operand, cols):
+            return operand[0][:, cols].bitcast(FP8X4), operand[1][:, cols]
+
+        def table_passes(c, i, bank):
             for a in range(2):
-                nc.tensor.matmul_mx(out=bank[:], lhsT=words[a].bitcast(FP4X4), lhsT_scale=scales[a],
-                                    rhs=picked[:, a, halves[i]].bitcast(FP8X4), rhs_scale=picked_scale[:, a, halves[i]],
-                                    start=(a == 0), stop=False)
-            wc_codes, wc_scale = wc_q[piece]
-            scene_codes, scene_scale = scene_q[i]
-            nc.tensor.matmul_mx(out=bank[:], lhsT=wc_codes[:, at : at + P].bitcast(FP8X4), lhsT_scale=wc_scale[:, at : at + P],
-                                rhs=scene_codes[:].bitcast(FP8X4), rhs_scale=scene_scale[:], start=False, stop=True)
+                mx_pass(bank[:], w4_operand(a, c // 2, slice(c * P, (c + 1) * P)), picked_operand(a, halves[i]), a == 0, False)
 
-        def gelu(c, i, bank):
-            nc.scalar.activation(hidden[c][:, halves[i]], bank[:], ACT.Gelu_apprx_tanh)
+        def scene_pass_and_gelu(c, i, bank, out):
+            mx_pass(bank[:], columns_of(wc_q[c // 2], slice(c % 2 * P, (c % 2 + 1) * P)), columns_of(scene_q[i], slice(0, BANK)),
+                    False, True)
+            nc.scalar.activation(out, bank[:], ACT.Gelu_apprx_tanh)
 
-        def apply_gain(c, out, in_):
-            nc.scalar.activation(out, in_, ACT.Copy, scale=gain_cols[:, c : c + 1])
+        def natural_tile(c, out):
+            used = [next_bank() for i in range(2)]
+            for i in range(2):
+                table_passes(c, i, used[i])
+                scene_pass_and_gelu(c, i, used[i], out[:, halves[i]])
+            return used
 
         def scatter(c, values, offsets, weights):
             nc.vector.tensor_tensor(page[c][:].indirect(offsets), values, weights, ALU.mult)
 
+        hidden = {0: sbuf("hidden0", [S], F32, "wc_raw0")}
+        first_banks = [next_bank() for i in range(2)]
+        for i in range(2):
+            table_passes(0, i, first_banks[i])
+        scene_pass_and_gelu(0, 0, first_banks[0], hidden[0][:, halves[0]])
+        scatter(0, hidden[0][:, halves[0]], slots[:, list_halves[0]], first_factors[:])
+        scene_pass_and_gelu(0, 1, first_banks[1], hidden[0][:, halves[1]])
+        times_gain(hidden[0][:, halves[1]], hidden[0][:, halves[1]], gain_cols[:, 0:1])
+        wc_q.append(quantised_operand("wc1", wc_raw[1:2], nc.scalar.copy, "woven3", "first_factors"))
+        scatter(0, hidden[0][:, halves[1]], slots[:, list_halves[1]], wgs_sb[:, halves[1]])
+
+        before_gain = sbuf("hidden1_before_gain", [S], F32, "scene_raw1")
+        natural_tile(1, before_gain)
+        hidden.update({1: sbuf("hidden1", [S], F32, "spare")})
+        times_gain(hidden[1][:], before_gain[:], gain_cols[:, 1:2])
+        scatter(1, hidden[1][:], slots[:], wgs_sb[:])
+
+        hidden.update({2: sbuf("hidden2", [S], F32, "wc_raw1")})
+        used = natural_tile(2, hidden[2])
+        times_gain(hidden[2][:], hidden[2][:], gain_cols[:, 2:3])
+        wc_q.append(quantised_operand("wc2", wc_raw[2:4], nc.scalar.copy, "scene_raw1", "spare"))
+        hidden.update({3: sbuf("hidden3", [S], F32, "wc_raw3")})
+        natural_tile(3, hidden[3])
+        times_gain(hidden[3][:], hidden[3][:], gain_cols[:, 3:4])
+        turn_wgs(1, used[1])
+
+        two_tiles = sbuf("hidden45", [2, S], F32, "scene_raw0")
+        hidden.update({4: two_tiles[:, 0], 5: two_tiles[:, 1], 6: sbuf("hidden6", [S], F32, "scene_raw1")[:]})
+        last_before_gain = sbuf("hidden7_before_gain", [S], F32, "wc_raw2")
+        by_entry = [sbuf(f"by_entry{pair}", [2, PACK, P], F32, f"woven{pair}") for pair in range(4)]
+        for b in range(S // P):
+            bank = next_bank()
+            entries = slice(b * P, (b + 1) * P)
+            for a in range(2):
+                mx_pass(bank[:], picked_operand(a, entries), w4_operand(a, 2, slice(GROUP, H)), a == 0, False)
+            mx_pass(bank[:], columns_of(scene_q[b // 4], slice(b % 4 * P, (b % 4 + 1) * P)), columns_of(wc_q[2], slice(0, GROUP)),
+                    False, True)
+            nc.scalar.activation(by_entry[b // 2][:, b % 2], bank[:].rearrange("j (q t) -> j t q", t=PACK), ACT.Gelu_apprx_tanh)
+        for t in range(PACK):
+            deal_wgs(1, t, next_bank())
+            for i in range(2):
+                bank = next_bank()
+                for b in range(4):
+                    nc.tensor.transpose(bank[:, b * P : (b + 1) * P], by_entry[2 * i + b // 2][:, b % 2, t], ident[:])
+                if t < PACK - 1:
+                    times_gain(hidden[GROUP_TILES + t][:, halves[i]], bank[:], gain_dealt[:, t : t + 1])
+                else:
+                    nc.scalar.copy(last_before_gain[:, halves[i]], bank[:])
+
         def store_page(c):
             nc.sync.dma_start(out=rows_of_tile(out_1, c), in_=page[c][:])
 
-        turned = {}
+        for c in range(LAST_TILE):
+            if c > 1:
+                scatter(c, hidden[c][:], slots[:], wgs_sb[:] if c < GROUP_TILES else wgs_dealt[c - GROUP_TILES][:])
+            store_page(c)
 
-        def turn(c, k):
-            if c == 0:
-                turned.update({k: keep.tile([P, 4, 2, 2 * P], BF16, name=f"turned{k}", tag=f"turned{k}", align_bytes=ALIGN)})
-            bank = next_bank()
-            for b in range(4):
-                nc.tensor.transpose(bank[:, b * P : (b + 1) * P], page[c][:, k * BANK + b * P : k * BANK + (b + 1) * P], ident[:])
-            nc.scalar.copy(
-                turned[k][:, :, :, 64 * c : 64 * (c + 1)].rearrange("s b u (p e) -> s b u p e", e=2),
-                bank[:].rearrange("s (b p u e) -> s b u p e", b=4, u=2, e=2))
-
-        page_codes = [keep.tile([P, T2], I32, name=f"page_codes{g}", align_bytes=ALIGN) for g in range(2)]
-        page_scale = [keep.tile([P, T2], U8, name=f"page_scale{g}", align_bytes=ALIGN) for g in range(2)]
-
-        def woven_chunk(g, k):
-            return keep.tile([P, BANK, PACK], BF16, name=f"woven{g}{k}", tag=f"woven{k}", align_bytes=ALIGN)
-
-        def quantise_page(g, cols, woven):
-            nc.vector.quantize_mx(out=page_codes[g][:, cols].bitcast(FP8X4), scales=page_scale[g][:, cols],
-                                  in_=woven[:].rearrange("p s j -> p (s j)"))
+        turned = [sbuf(f"turned{k}", [4, 2, 2 * P], BF16) for k in range(CHUNKS)]
+        for c in range(GROUP_TILES):
+            for k in range(CHUNKS):
+                bank = next_bank()
+                for b in range(4):
+                    nc.tensor.transpose(bank[:, b * P : (b + 1) * P], page[c][:, k * BANK + b * P : k * BANK + (b + 1) * P], ident[:])
+                nc.scalar.copy(
+                    turned[k][:, :, :, 64 * c : 64 * (c + 1)].rearrange("s b u (p e) -> s b u p e", e=2),
+                    bank[:].rearrange("s (b p u e) -> s b u p e", b=4, u=2, e=2))
 
         def turn_back(k):
             pairs = turned[k][:].rearrange("s b u w -> s (b u w)").bitcast(F32)
-            woven = woven_chunk(0, k)
+            woven = sbuf(f"woven_page0{k}", [BANK, PACK], BF16, f"woven{k}")
             woven_pairs = woven[:].rearrange("p s j -> p (s j)").bitcast(F32)
             for two_blocks in range(2):
                 bank = next_bank()
@@ -268,31 +318,42 @@ def tile_list_narrator_prefix_cache_kernel(
                     bank[:].rearrange("p (b u s) -> p b s u", b=2, u=2))
             return woven
 
-        pieces = [slice(0, BANK // 2), slice(BANK // 2, BANK)] + [slice(k * BANK, (k + 1) * BANK) for k in range(1, CHUNKS)]
-        pairs = {}
+        code_tiles = {(0, 0): sbuf("early_codes", [EARLY_CHUNKS * BANK], I32)}
+        page_scale = [sbuf(f"page_scale{g}", [T2], U8) for g in range(2)]
 
-        def round_piece(c, i):
-            t = c - GROUP_TILES
-            if t == 0:
-                tag = ["turned0", "wc_raw0", "turned1", "turned2", "wc_raw1"][i]
-                width = pieces[i].stop - pieces[i].start
-                pairs.update({i: keep.tile([P, 2, width, 2], BF16, name=f"pairs{i}", tag=tag, align_bytes=ALIGN)})
-            nc.scalar.copy(pairs[i][:, t // 2, :, t % 2], page[c][:, pieces[i]])
-
-        def weave_piece(i):
-            width = pieces[i].stop - pieces[i].start
-            tag = ["woven0", "wc_raw3", "woven1", "woven2", "woven3"][i]
-            woven = keep.tile([P, width, PACK], BF16, name=f"woven1{i}", tag=tag, align_bytes=ALIGN)
-            words = woven[:].rearrange("p s j -> p (s j)").bitcast(U32).rearrange("p (s u) -> p s u", u=2)
-            nc.scalar.copy(words, pairs[i][:].rearrange("p u s e -> p u (s e)").bitcast(U32).rearrange("p u s -> p s u"))
-            return woven
+        def page_codes(g, cols):
+            first = max(first for group, first in code_tiles if group == g and first <= cols.start)
+            return code_tiles[(g, first)][:, cols.start - first : cols.stop - first]
 
         def store_codes(g, cols):
-            nc.sync.dma_start(out=out_2[g].rearrange("p m t -> p (m t)").bitcast(I32)[:, cols], in_=page_codes[g][:, cols])
+            nc.sync.dma_start(out=out_2[g].rearrange("p m t -> p (m t)").bitcast(I32)[:, cols], in_=page_codes(g, cols))
 
         def store_scales(g):
             for q in range(QUADRANTS):
                 nc.gpsimd.dma_start(out=out_3[g, 4 * q : 4 * q + 4, :].bitcast(I32), in_=plane_rows(page_scale[g], q))
+
+        woven_group0 = []
+        for k in range(CHUNKS):
+            woven_group0.append(turn_back(k))
+            if k < EARLY_CHUNKS:
+                quantise(page_codes(0, chunks[k]), page_scale[0][:, chunks[k]], woven_group0[k])
+        hidden.update({LAST_TILE: sbuf("hidden7", [S], F32, f"turned{EARLY_CHUNKS - 1}")})
+        times_gain(hidden[LAST_TILE][:], last_before_gain[:], gain_dealt[:, PACK - 1 : PACK])
+
+        pieces = [slice(0, BANK // 2), slice(BANK // 2, BANK)] + chunks[1:]
+        pairs = [sbuf(f"pairs{i}", [2, cols.stop - cols.start, 2], BF16, home)
+                 for i, (cols, home) in enumerate(zip(pieces, ["turned0", "wc_raw0", "turned3", "turned2", "wc_raw1"]))]
+
+        def round_piece(c, i):
+            t = c - GROUP_TILES
+            nc.scalar.copy(pairs[i][:, t // 2, :, t % 2], page[c][:, pieces[i]])
+
+        def weave_piece(i):
+            home = ["woven0", "wc_raw3", "woven1", "woven2", "woven3"][i]
+            woven = sbuf(f"woven_page1{i}", [pieces[i].stop - pieces[i].start, PACK], BF16, home)
+            words = woven[:].rearrange("p s j -> p (s j)").bitcast(U32).rearrange("p (s u) -> p s u", u=2)
+            nc.scalar.copy(words, pairs[i][:].rearrange("p u s e -> p u (s e)").bitcast(U32).rearrange("p u s -> p s u"))
+            return woven
 
         def banks_of_piece(i):
             if i < 2:
@@ -304,10 +365,10 @@ def tile_list_narrator_prefix_cache_kernel(
             width = cols.stop - cols.start
             for bank, blocks in banks_of_piece(i):
                 for at, n in enumerate(blocks):
-                    nc.tensor.matmul_mx(out=bank[:, at * width : (at + 1) * width], lhsT=w8[:, g, n * P : (n + 1) * P].bitcast(FP8X4),
-                                        lhsT_scale=w8_scale[:, g, n * P : (n + 1) * P],
-                                        rhs=page_codes[g][:, cols].bitcast(FP8X4), rhs_scale=page_scale[g][:, cols],
-                                        start=(g == 0 and at == 0), stop=(g == 1 and at == len(blocks) - 1))
+                    mx_pass(bank[:, at * width : (at + 1) * width],
+                            (w8[:, g, n * P : (n + 1) * P].bitcast(FP8X4), w8_scale[:, g, n * P : (n + 1) * P]),
+                            (page_codes(g, cols).bitcast(FP8X4), page_scale[g][:, cols]),
+                            g == 0 and at == 0, g == 1 and at == len(blocks) - 1)
 
         def add_and_store(i):
             cols = pieces[i]
@@ -320,71 +381,23 @@ def tile_list_narrator_prefix_cache_kernel(
                 elif n % 2 == 1:
                     nc.sync.dma_start(out=out_rows[:, n - 1 : n + 1, cols], in_=result[n // 2][:, :, cols])
 
-        def make_factors():
-            for t in range(PACK):
-                for i in range(2):
-                    bank = next_bank()
-                    for b in range(4):
-                        block = wgs_turned[2 * i + b // 2][:, b % 2, t].rearrange("j r q -> j (r q)")
-                        nc.tensor.transpose(bank[:, b * P : (b + 1) * P], block, ident[:])
-                    nc.scalar.activation(factors[t][:, halves[i]], bank[:], ACT.Copy, scale=gain_dealt[:, t : t + 1])
-
-        def tile_of_h(name, tag, count):
-            tile = keep.tile([P, count, S], F32, name=name, tag=tag, align_bytes=ALIGN)
-            return [tile[:, i, :] for i in range(count)]
-
-        for c in range(LAST_TILE):
-            if c == 0:
-                hidden.update(zip([0], tile_of_h("hidden0", "wc_raw0", 1)))
-            if c == 1:
-                hidden.update(zip([1, 6], tile_of_h("hidden16", "scene_raw1", 2)))
-            if c == 2:
-                turn_wgs(1)
-                make_factors()
-                second = weave_operand(wc_raw[1], "wc1", "woven3", nc.scalar.copy)
-                dealt = keep.tile([P, BANK, PACK], BF16, name="wc_dealt_woven", tag="woven0", align_bytes=ALIGN)
-                for i in range(2):
-                    nc.scalar.copy(dealt[:].rearrange("p (t q) j -> p q j t", t=PACK)[:, 64 * i : 64 * (i + 1)],
-                                   wc_raw[2 + i][:].rearrange("p j (q t) -> p q j t", t=PACK))
-                wc_q.extend([quantise_operand(second, "wc1"), quantise_operand(dealt, "wc_dealt")])
-                hidden.update(zip([2], tile_of_h("hidden2", "wc_raw3", 1)))
-                hidden.update(zip([3], tile_of_h("hidden3", "wc_raw2", 1)))
-                hidden.update(zip([4, 5], tile_of_h("hidden45", "scene_raw0", 2)))
-            for i in range(2):
-                bank = next_bank()
-                first_sum(c, i, bank)
-                gelu(c, i, bank)
-                if c == 0:
-                    apply_gain(c, hidden[c][:, halves[i]], hidden[c][:, halves[i]])
-                    scatter(c, hidden[c][:, halves[i]], slots[:, list_halves[i]], wgs_sb[:, halves[i]])
-            if 0 < c < GROUP_TILES:
-                apply_gain(c, hidden[c], hidden[c])
-        for i in range(2):
-            first_sum(LAST_TILE, i, banks[6 + i])
-        for c in range(LAST_TILE):
-            if c > 0:
-                scatter(c, hidden[c], slots[:], wgs_sb[:] if c < GROUP_TILES else factors[c - GROUP_TILES][:])
-            store_page(c)
-        for c in range(GROUP_TILES):
-            for k in range(CHUNKS):
-                turn(c, k)
-        for k in range(CHUNKS):
-            quantise_page(0, slice(k * BANK, (k + 1) * BANK), turn_back(k))
-        hidden.update(zip([LAST_TILE], tile_of_h("hidden7", f"turned{CHUNKS - 1}", 1)))
-        for i in range(2):
-            gelu(LAST_TILE, i, banks[6 + i])
         for c in range(GROUP_TILES, LAST_TILE):
             for i in range(len(pieces)):
                 round_piece(c, i)
-        store_codes(0, slice(0, T2))
-        store_scales(0)
+        store_codes(0, slice(0, EARLY_CHUNKS * BANK))
         for i in range(3):
             second_passes(i, 0)
-        scatter(LAST_TILE, hidden[LAST_TILE], slots[:], factors[PACK - 1][:])
+        scatter(LAST_TILE, hidden[LAST_TILE][:], slots[:], wgs_dealt[PACK - 1][:])
         store_page(LAST_TILE)
+        code_tiles.update({(0, EARLY_CHUNKS * BANK): sbuf("late_codes", [T2 - EARLY_CHUNKS * BANK], I32, f"wgs_dealt{PACK - 1}")})
+        code_tiles.update({(1, 0): sbuf("codes_of_group1", [T2], I32, "picking")})
+        for k in range(EARLY_CHUNKS, CHUNKS):
+            quantise(page_codes(0, chunks[k]), page_scale[0][:, chunks[k]], woven_group0[k])
+        store_codes(0, slice(EARLY_CHUNKS * BANK, T2))
+        store_scales(0)
         for i in range(len(pieces)):
             round_piece(LAST_TILE, i)
-            quantise_page(1, pieces[i], weave_piece(i))
+            quantise(page_codes(1, pieces[i]), page_scale[1][:, pieces[i]], weave_piece(i))
             if i == len(pieces) - 1:
                 store_scales(1)
             store_codes(1, pieces[i])

@@ -65,11 +65,10 @@ def tile_list_narrator_prefix_cache_kernel(
         tab_scale_rows = sbuf("tab_scale_rows", [T], U8, "picking")
         picked_scale = sbuf("picked_scale", [2, S], U8)
         w4_scale = sbuf("w4_scale", [2, H], U8)
-        w8_scale = sbuf("w8_scale", [2, N], U8)
         gain_rows = sbuf("gain_rows", [P], F32)
         gain_dealt = sbuf("gain_dealt", [PACK], F32)
         ident = sbuf("ident", [P], F32)
-        for plane in (tab_scale_rows, w4_scale, picked_scale, w8_scale):
+        for plane in (tab_scale_rows, w4_scale, picked_scale):
             nc.vector.memset(plane[:].bitcast(I32), 0)
         load_scale_planes(w4_scale, w4_scales)
         nc.gpsimd.memset(gain_rows[:], 0.0)
@@ -174,6 +173,8 @@ def tile_list_narrator_prefix_cache_kernel(
             for q in range(QUADRANTS):
                 first = 4 * (16 * a + 4 * q)
                 nc.gpsimd.dma_start(out=plane_rows(picked_scale[:, a, :], q), in_=picked_rows[first : first + 16 : 4, :].bitcast(I32))
+        w8_scale = sbuf("w8_scale", [2, N], U8, "picked_rows")
+        nc.gpsimd.memset(w8_scale[:].bitcast(I32), 0)
         load_scale_planes(w8_scale, w8_scales)
         picked = sbuf("picked", [2, S], U32, "picking")
         for a in range(2):
@@ -355,31 +356,30 @@ def tile_list_narrator_prefix_cache_kernel(
             nc.scalar.copy(words, pairs[i][:].rearrange("p u s e -> p u (s e)").bitcast(U32).rearrange("p u s -> p s u"))
             return woven
 
+        def second_pass(out, n, g, cols, start, stop):
+            mx_pass(out, (w8[:, g, n * P : (n + 1) * P].bitcast(FP8X4), w8_scale[:, g, n * P : (n + 1) * P]),
+                    (page_codes(g, cols).bitcast(FP8X4), page_scale[g][:, cols]), start, stop)
+
         def banks_of_piece(i):
             if i < 2:
                 return [(banks[2 * i + a], [2 * a, 2 * a + 1]) for a in range(2)]
-            return [(banks[4 * ((i + 1) % 2) + n], [n]) for n in range(N // P)]
+            return [(banks[4 + n], [n]) for n in range(N // P)]
 
         def second_passes(i, g):
             cols = pieces[i]
             width = cols.stop - cols.start
             for bank, blocks in banks_of_piece(i):
                 for at, n in enumerate(blocks):
-                    mx_pass(bank[:, at * width : (at + 1) * width],
-                            (w8[:, g, n * P : (n + 1) * P].bitcast(FP8X4), w8_scale[:, g, n * P : (n + 1) * P]),
-                            (page_codes(g, cols).bitcast(FP8X4), page_scale[g][:, cols]),
-                            g == 0 and at == 0, g == 1 and at == len(blocks) - 1)
+                    second_pass(bank[:, at * width : (at + 1) * width], n, g, cols,
+                                g == 0 and at == 0, g == 1 and at == len(blocks) - 1)
 
-        def add_and_store(i):
-            cols = pieces[i]
-            for bank, blocks in banks_of_piece(i):
-                n = blocks[-1]
-                sums = result[n // 2][:, blocks[0] % 2 : n % 2 + 1, cols]
-                nc.vector.tensor_tensor(sums, bank[:].rearrange("p (n s) -> p n s", n=len(blocks)), sums, ALU.add)
-                if i == len(pieces) - 1:
-                    nc.sync.dma_start(out=out_rows[:, n, cols], in_=result[n // 2][:, n % 2, cols])
-                elif n % 2 == 1:
-                    nc.sync.dma_start(out=out_rows[:, n - 1 : n + 1, cols], in_=result[n // 2][:, :, cols])
+        def add_bias(bank, blocks, cols):
+            sums = result[blocks[0] // 2][:, blocks[0] % 2 : blocks[-1] % 2 + 1, cols]
+            nc.vector.tensor_tensor(sums, bank[:].rearrange("p (n s) -> p n s", n=len(blocks)), sums, ALU.add)
+
+        def store_result(blocks, cols):
+            nc.sync.dma_start(out=out_rows[:, blocks[0] : blocks[-1] + 1, cols],
+                              in_=result[blocks[0] // 2][:, blocks[0] % 2 : blocks[-1] % 2 + 1, cols])
 
         for c in range(GROUP_TILES, LAST_TILE):
             for i in range(len(pieces)):
@@ -395,13 +395,28 @@ def tile_list_narrator_prefix_cache_kernel(
             quantise(page_codes(0, chunks[k]), page_scale[0][:, chunks[k]], woven_group0[k])
         store_codes(0, slice(EARLY_CHUNKS * BANK, T2))
         store_scales(0)
-        for i in range(len(pieces)):
+        for i in range(3):
             round_piece(LAST_TILE, i)
             quantise(page_codes(1, pieces[i]), page_scale[1][:, pieces[i]], weave_piece(i))
-            if i == len(pieces) - 1:
-                store_scales(1)
             store_codes(1, pieces[i])
-            if i >= 3:
-                second_passes(i, 0)
             second_passes(i, 1)
-            add_and_store(i)
+            for bank, blocks in banks_of_piece(i):
+                add_bias(bank, blocks, pieces[i])
+                if blocks[-1] % 2 == 1:
+                    store_result([blocks[-1] - 1, blocks[-1]], pieces[i])
+        for i in (3, 4):
+            round_piece(LAST_TILE, i)
+            quantise(page_codes(1, pieces[i]), page_scale[1][:, pieces[i]], weave_piece(i))
+        store_scales(1)
+        second_half = slice(pieces[3].start, T2)
+        store_codes(1, second_half)
+        for n in range(N // P):
+            for i in (3, 4):
+                bank = banks[2 * n + i - 3]
+                for g in range(2):
+                    second_pass(bank[:], n, g, pieces[i], g == 0, g == 1)
+                add_bias(bank, [n], pieces[i])
+                if n == N // P - 1:
+                    store_result([n], pieces[i])
+            if n < N // P - 1:
+                store_result([n], second_half)

@@ -25,9 +25,15 @@ PAGE_TILES = H // P
 GROUP_TILES = GROUP // P
 LAST_TILE = PAGE_TILES - 1
 CHUNKS = T2 // BANK
-EARLY_CHUNKS = 2
 ALIGN = 64
+KIB = 1024
 FLOPS = 2 * (1024 + 512) * H * S + 2 * H * N * T2
+
+AT_PAGE, AT_TABLE, AT_SCENE, AT_TURNED, AT_WOVEN, AT_FACTORS, AT_DEALT = 0, 64, 96, 112, 128, 144, 160
+AT_PICKED, AT_SCALE_ROWS, AT_DEALT_SCALE, AT_WC, AT_W4, AT_WGS = 176, 181, 184, 185, 201, 207
+AT_W4_DEALT = AT_W4 + 3
+AT_PICKED_SCALE, AT_PICKED_ROWS, AT_W4_SCALE, AT_CODES, AT_SCALES, AT_FIRST, AT_PAGE_SCALE, AT_SMALL = (
+    211, 213, 214, 216, 224, 226, 230, 234)
 
 
 def tile_list_narrator_prefix_cache_kernel(
@@ -40,37 +46,34 @@ def tile_list_narrator_prefix_cache_kernel(
         keep = ctx.enter_context(tc.tile_pool(name="keep", bufs=1))
         psum = ctx.enter_context(tc.psum_pool(name="psum", bufs=1))
         banks = [psum.tile([P, BANK], F32, name=f"bank{b}") for b in range(8)]
-        ring = banks[0:6]
         fills = []
 
         def next_bank():
             fills.append(len(fills))
-            return ring[fills[-1] % len(ring)]
+            return banks[fills[-1] % len(banks)]
 
-        def sbuf(name, shape, dtype, home=None):
-            return keep.tile([P] + shape, dtype, name=name, tag=home or name, align_bytes=ALIGN)
+        def sbuf(name, shape, dtype, at):
+            return keep.tile([P] + shape, dtype, name=name, align_bytes=ALIGN, offset=int(at * KIB))
 
         halves = [slice(0, BANK), slice(BANK, S)]
         list_halves = [slice(0, BANK // LIST_ROWS), slice(BANK // LIST_ROWS, S // LIST_ROWS)]
         chunks = [slice(k * BANK, (k + 1) * BANK) for k in range(CHUNKS)]
 
-        def plane_rows(plane, q):
-            return plane[32 * q : 32 * q + 4].bitcast(I32)
+        def plane_rows(plane, q, first=0):
+            return plane[32 * q + first : 32 * q + first + 4].bitcast(I32)
 
-        def load_scale_planes(planes, scales):
-            for q in range(QUADRANTS):
-                nc.gpsimd.dma_start(out=plane_rows(planes, q),
-                                    in_=scales[:, 4 * q : 4 * q + 4, :].rearrange("a q c -> q a c").bitcast(I32))
-
-        tab_scale_rows = sbuf("tab_scale_rows", [T], U8, "picking")
-        picked_scale = sbuf("picked_scale", [2, S], U8)
-        w4_scale = sbuf("w4_scale", [2, H], U8)
-        gain_rows = sbuf("gain_rows", [P], F32)
-        gain_dealt = sbuf("gain_dealt", [PACK], F32)
-        ident = sbuf("ident", [P], F32)
-        for plane in (tab_scale_rows, w4_scale, picked_scale):
+        tab_scale_rows = sbuf("tab_scale_rows", [T], U8, AT_SCALE_ROWS)
+        picked_scale = sbuf("picked_scale", [2, S], U8, AT_PICKED_SCALE)
+        weight_scale = sbuf("weight_scale", [2, H], U8, AT_W4_SCALE)
+        ident = sbuf("ident", [P], F32, AT_SMALL)
+        gain_rows = sbuf("gain_rows", [P], F32, AT_SMALL + 0.5)
+        gain_cols = sbuf("gain_cols", [GROUP_TILES], F32, AT_SMALL + 1)
+        gain_dealt = sbuf("gain_dealt", [PACK], F32, AT_SMALL + 1.0625)
+        for plane in (tab_scale_rows, weight_scale, picked_scale):
             nc.vector.memset(plane[:].bitcast(I32), 0)
-        load_scale_planes(w4_scale, w4_scales)
+        for q in range(QUADRANTS):
+            nc.gpsimd.dma_start(out=plane_rows(weight_scale, q),
+                                in_=w4_scales[:, 4 * q : 4 * q + 4, :].rearrange("a q c -> q a c").bitcast(I32))
         nc.gpsimd.memset(gain_rows[:], 0.0)
         nc.scalar.dma_start(out=gain_rows[0:GROUP_TILES, :], in_=gain[0:GROUP].rearrange("(c p) -> c p", p=P))
         nc.scalar.dma_start(out=gain_dealt[:], in_=gain[GROUP:].rearrange("(p t) -> p t", t=PACK))
@@ -78,17 +81,17 @@ def tile_list_narrator_prefix_cache_kernel(
 
         picks = lists.tile([P, S // LIST_ROWS], U16)
         slots = lists.tile([P, S // LIST_ROWS], U16)
-        scene_rows = scene.rearrange("(p j) s -> p j s", j=PACK)
         wc_rows = wc.rearrange("(p j) c -> p j c", j=PACK)
-        wc_pieces = [slice(2 * P * i, 2 * P * (i + 1)) for i in range(4)]
+        wc_pieces = [slice(0, P), slice(P, 2 * P), slice(2 * P, GROUP), slice(GROUP, H)]
         w4_pieces = [slice(0, 2 * P), slice(2 * P, GROUP), slice(GROUP, H)]
-        scene_raw = [sbuf(f"scene_raw{i}", [PACK, BANK], F32) for i in range(2)]
-        wc_raw = [sbuf(f"wc_raw{i}", [PACK, 2 * P], F32) for i in range(4)]
-        tab = [sbuf(f"tab{a}", [T], I32, f"table_then_result{a}") for a in range(2)]
-        w4 = [sbuf(f"w4_{i}", [2, 2 * (cols.stop - cols.start)], U8) for i, cols in enumerate(w4_pieces)]
-        wgs_sb = sbuf("wgs_sb", [S], F32)
-        page = [sbuf(f"page{c}", [T2], F32) for c in range(PAGE_TILES)]
-        w8 = sbuf("w8", [2, N], I32)
+        scene_raw = sbuf("scene_raw", [PACK, S], F32, AT_SCENE)
+        wc_raw = [sbuf(f"wc_raw{i}", [PACK, cols.stop - cols.start], F32, AT_WC + cols.start / 64)
+                  for i, cols in enumerate(wc_pieces)]
+        tab = [sbuf(f"tab{a}", [T], I32, AT_TABLE + 16 * a) for a in range(2)]
+        w4 = [sbuf(f"w4_{i}", [2, 2 * (cols.stop - cols.start)], U8, AT_W4 + (0, 3, 1)[i])
+              for i, cols in enumerate(w4_pieces)]
+        wgs_sb = [sbuf(f"wgs_sb{i}", [BANK], F32, AT_WGS + 2 * i) for i in range(2)]
+        page = [sbuf(f"page{c}", [T2], F32, AT_PAGE + 8 * c) for c in range(PAGE_TILES)]
 
         def rows_of_tile(matrix, c):
             if c < GROUP_TILES:
@@ -104,11 +107,8 @@ def tile_list_narrator_prefix_cache_kernel(
         def load_wc(i):
             nc.sync.dma_start(out=wc_raw[i][:], in_=wc_rows[:, :, wc_pieces[i]])
 
-        def load_scene(i):
-            nc.sync.dma_start(out=scene_raw[i][:], in_=scene_rows[:, :, halves[i]])
-
         def load_wgs(i):
-            nc.sync.dma_start(out=wgs_sb[:, halves[i]], in_=wgs[:, halves[i]])
+            nc.sync.dma_start(out=wgs_sb[i][:], in_=wgs[:, halves[i]])
 
         def load_w4(i):
             cols = w4_pieces[i]
@@ -121,302 +121,298 @@ def tile_list_narrator_prefix_cache_kernel(
         load_wgs(0)
         load_table(0, slice(T // 4, T))
         load_table(1, slice(0, T))
-        load_scene(0)
+        nc.sync.dma_start(out=scene_raw[:], in_=scene.rearrange("(p j) s -> p j s", j=PACK))
         load_w4(0)
         load_wc(0)
-        load_scene(1)
         nc.sync.dma_start(slots[:], offs2)
         load_page(0)
         load_wc(1)
-        load_wgs(1)
         load_w4(1)
-        load_page(1)
+        load_wgs(1)
         load_wc(2)
+        load_page(1)
         load_wc(3)
         load_w4(2)
         for c in range(2, PAGE_TILES):
             load_page(c)
-        nc.sync.dma_start(out=w8[:], in_=w8_words.rearrange("a p c i -> p a (c i)").bitcast(I32))
 
-        gain_cols = sbuf("gain_cols", [GROUP_TILES], F32)
-        nc.tensor.transpose(banks[5][:, 0:P], gain_rows[:], ident[:])
-        nc.scalar.copy(gain_cols[:], banks[5][:, 0:GROUP_TILES])
-
-        wgs_dealt = [sbuf(f"wgs_dealt{t}", [S], F32) for t in range(PACK)]
-        wgs_turned = [sbuf(f"wgs_turned{k}", [2, PACK, QUADRANTS, 32], F32, f"turned{k}") for k in range(4)]
-
-        def turn_wgs(i, first_bank):
-            for b in range(4):
-                nc.tensor.transpose(first_bank[:, b * P : (b + 1) * P], wgs_sb[:, (4 * i + b) * P : (4 * i + b + 1) * P], ident[:])
-            for pair in range(2):
-                rows = first_bank[:, 2 * pair * P : 2 * (pair + 1) * P].rearrange("j (b q t) -> j b t q", b=2, t=PACK)
-                nc.scalar.copy(wgs_turned[2 * i + pair][:], rows.unsqueeze(3).to_broadcast([P, 2, PACK, QUADRANTS, 32]))
-
-        def deal_wgs(i, t, bank):
-            for b in range(4):
-                block = wgs_turned[2 * i + b // 2][:, b % 2, t].rearrange("j r q -> j (r q)")
-                nc.tensor.transpose(bank[:, b * P : (b + 1) * P], block, ident[:])
-            nc.scalar.copy(wgs_dealt[t][:, halves[i]], bank[:])
+        bank = next_bank()
+        nc.tensor.transpose(bank[:, 0:P], gain_rows[:], ident[:])
+        nc.scalar.copy(gain_cols[:], bank[:, 0:GROUP_TILES])
 
         def times_gain(out, in_, column):
             nc.scalar.activation(out, in_, ACT.Copy, scale=column)
 
-        first_factors = sbuf("first_factors", [BANK], F32)
-        times_gain(first_factors[:], wgs_sb[:, halves[0]], gain_cols[:, 0:1])
-        turn_wgs(0, banks[7])
-        for t in range(PACK):
-            deal_wgs(0, t, banks[6 + t % 2])
+        factors = [sbuf(f"factors{c}", [S], F32, AT_FACTORS + 4 * c) for c in range(PAGE_TILES)]
 
-        picked_rows = sbuf("picked_rows", [S], U8)
+        def natural_factors(c, i, gains):
+            times_gain(factors[c][:, halves[i]], wgs_sb[i][:], gains[:, c : c + 1])
+
+        def turn_wgs(i):
+            turned_wgs = [sbuf(f"wgs_turned{i}{pair}", [2, PACK, QUADRANTS, 32], F32, AT_TURNED + 4 * (2 * i + pair)) for pair in range(2)]
+            bank = next_bank()
+            for b in range(4):
+                nc.tensor.transpose(bank[:, b * P : (b + 1) * P], wgs_sb[i][:, b * P : (b + 1) * P], ident[:])
+            for pair in range(2):
+                rows = bank[:, 2 * pair * P : 2 * (pair + 1) * P].rearrange("j (b q t) -> j b t q", b=2, t=PACK)
+                nc.scalar.copy(turned_wgs[pair][:], rows.unsqueeze(3).to_broadcast([P, 2, PACK, QUADRANTS, 32]))
+            return turned_wgs
+
+        def dealt_factors(turned_wgs, i, t):
+            bank = next_bank()
+            for b in range(4):
+                block = turned_wgs[b // 2][:, b % 2, t].rearrange("j r q -> j (r q)")
+                nc.tensor.transpose(bank[:, b * P : (b + 1) * P], block, ident[:])
+            times_gain(factors[GROUP_TILES + t][:, halves[i]], bank[:], gain_dealt[:, t : t + 1])
+
+        for c in range(GROUP_TILES):
+            natural_factors(c, 0, gain_cols)
+        turned_wgs = turn_wgs(0)
+        for t in range(PACK):
+            dealt_factors(turned_wgs, 0, t)
+
+        picked_rows = sbuf("picked_rows", [S], U8, AT_PICKED_ROWS)
         nc.vector.tensor_copy(picked_rows[:], tab_scale_rows[:].indirect(picks[:]))
         for a in range(2):
             for q in range(QUADRANTS):
                 first = 4 * (16 * a + 4 * q)
                 nc.gpsimd.dma_start(out=plane_rows(picked_scale[:, a, :], q), in_=picked_rows[first : first + 16 : 4, :].bitcast(I32))
-        w8_scale = sbuf("w8_scale", [2, N], U8, "picked_rows")
-        nc.gpsimd.memset(w8_scale[:].bitcast(I32), 0)
-        load_scale_planes(w8_scale, w8_scales)
-        picked = sbuf("picked", [2, S], U32, "picking")
+        dealt_scale = sbuf("dealt_scale", [2, GROUP], U8, AT_DEALT_SCALE)
+        nc.vector.tensor_copy(dealt_scale[:].rearrange("p a (t m) -> p a t m", t=PACK),
+                              weight_scale[:, :, GROUP:].rearrange("p a (m t) -> p a t m", t=PACK))
+        picked = sbuf("picked", [2, S], U32, AT_PICKED)
         for a in range(2):
             nc.vector.tensor_copy(picked[:, a, :], tab[a][:].bitcast(U32).indirect(picks[:]))
 
-        result = [sbuf(f"result{a}", [2, T2], F32, f"table_then_result{a}") for a in range(2)]
+        result = [sbuf(f"result{a}", [2, T2], F32, AT_TABLE + 16 * a) for a in range(2)]
         bias_rows = bias.rearrange("(n p) t -> p n t", p=P)
         out_rows = out_0.rearrange("(n p) t -> p n t", p=P)
         for a in range(2):
             nc.sync.dma_start(out=result[a][:], in_=bias_rows[:, 2 * a : 2 * a + 2, :])
 
         def weave(woven, raw, copy):
-            copy(woven.rearrange("p (c i) j -> p c j i", i=4), raw[:].rearrange("p j (c i) -> p c j i", i=4))
+            copy(woven.rearrange("p (c i) j -> p c j i", i=4), raw.rearrange("p j (c i) -> p c j i", i=4))
 
         def quantise(codes, scale, woven):
             nc.vector.quantize_mx(out=codes.bitcast(FP8X4), scales=scale, in_=woven[:].rearrange("p c j -> p (c j)"))
 
-        def quantised_operand(name, raws, copy, woven_home, codes_home=None):
-            width = sum(raw.shape[2] for raw in raws)
-            woven = sbuf(name + "_woven", [width, PACK], BF16, woven_home)
-            for i, raw in enumerate(raws):
-                weave(woven[:, i * raw.shape[2] : (i + 1) * raw.shape[2]], raw, copy)
-            codes = sbuf(name + "_codes", [width], U32, codes_home)
-            scale = sbuf(name + "_scale", [width], U8)
+        def quantised(name, woven, first, codes_at=None):
+            width = woven.shape[1]
+            codes = sbuf(name + "_codes", [width], U32, codes_at or AT_CODES + first / 256)
+            scale = sbuf(name + "_scale", [width], U8, AT_SCALES + first / 1024)
             quantise(codes[:], scale[:], woven)
             return codes, scale
 
-        wc_q = [quantised_operand("wc0", wc_raw[0:1], nc.scalar.copy, "woven2")]
-        scene_q = [quantised_operand(f"scene{i}", scene_raw[i : i + 1], nc.vector.tensor_copy, f"woven{i}") for i in range(2)]
+        scene_woven = [sbuf(f"scene_woven{i}", [BANK, PACK], BF16, AT_WOVEN + 4 * i) for i in range(2)]
+
+        def woven_wc(i, at):
+            return sbuf(f"wc_woven{i}", [wc_pieces[i].stop - wc_pieces[i].start, PACK], BF16, at)
+
+        shared = BANK // 2
+        weave(scene_woven[1][:, 0:shared], scene_raw[:, :, BANK : BANK + shared], nc.scalar.copy)
+        weave(scene_woven[0][:], scene_raw[:, :, halves[0]], nc.vector.tensor_copy)
+        scene_q = [quantised("scene0", scene_woven[0], 0)]
+        woven = woven_wc(0, AT_WOVEN + 8)
+        weave(woven[:], wc_raw[0][:], nc.scalar.copy)
+        wc_q = [quantised("wc0", woven, S, AT_WOVEN + 9)]
+        weave(scene_woven[1][:, shared:], scene_raw[:, :, BANK + shared :], nc.vector.tensor_copy)
+        scene_q.append(quantised("scene1", scene_woven[1], BANK))
 
         def mx_pass(out, stationary, moving, start, stop):
             nc.tensor.matmul_mx(out=out, lhsT=stationary[0], lhsT_scale=stationary[1], rhs=moving[0], rhs_scale=moving[1],
                                 start=start, stop=stop)
 
-        def w4_operand(a, piece, cols):
-            at = w4_pieces[piece].start
-            return w4[piece][:, a, 2 * (cols.start - at) : 2 * (cols.stop - at)].bitcast(FP4X4), w4_scale[:, a, cols]
-
-        def picked_operand(a, entries):
-            return picked[:, a, entries].bitcast(FP8X4), picked_scale[:, a, entries]
-
         def columns_of(operand, cols):
             return operand[0][:, cols].bitcast(FP8X4), operand[1][:, cols]
 
-        def table_passes(c, i, bank):
+        w4_dealt = []
+
+        def w4_operand(a, c):
+            if c >= GROUP_TILES:
+                at = (c - GROUP_TILES) * P
+                return w4_dealt[0][:, a, 2 * at : 2 * (at + P)].bitcast(FP4X4), dealt_scale[:, a, at : at + P]
+            piece = c // 2
+            at = c * P - w4_pieces[piece].start
+            return w4[piece][:, a, 2 * at : 2 * (at + P)].bitcast(FP4X4), weight_scale[:, a, c * P : (c + 1) * P]
+
+        def wc_operand(c):
+            piece = max(i for i, cols in enumerate(wc_pieces) if cols.start <= c * P)
+            at = c * P - wc_pieces[piece].start
+            return columns_of(wc_q[piece], slice(at, at + P))
+
+        def table_passes(c, i, bank, opening):
             for a in range(2):
-                mx_pass(bank[:], w4_operand(a, c // 2, slice(c * P, (c + 1) * P)), picked_operand(a, halves[i]), a == 0, False)
+                mx_pass(bank[:], w4_operand(a, c), (picked[:, a, halves[i]].bitcast(FP8X4), picked_scale[:, a, halves[i]]),
+                        opening and a == 0, not opening and a == 1)
 
-        def scene_pass_and_gelu(c, i, bank, out):
-            mx_pass(bank[:], columns_of(wc_q[c // 2], slice(c % 2 * P, (c % 2 + 1) * P)), columns_of(scene_q[i], slice(0, BANK)),
-                    False, True)
-            nc.scalar.activation(out, bank[:], ACT.Gelu_apprx_tanh)
+        def scene_pass(c, i, bank, opening):
+            mx_pass(bank[:], wc_operand(c), columns_of(scene_q[i], slice(0, BANK)), opening, not opening)
 
-        def natural_tile(c, out):
-            used = [next_bank() for i in range(2)]
-            for i in range(2):
-                table_passes(c, i, used[i])
-                scene_pass_and_gelu(c, i, used[i], out[:, halves[i]])
-            return used
+        def gelu(i, bank, out):
+            nc.scalar.activation(out[:, halves[i]], bank[:], ACT.Gelu_apprx_tanh)
 
-        def scatter(c, values, offsets, weights):
-            nc.vector.tensor_tensor(page[c][:].indirect(offsets), values, weights, ALU.mult)
+        hidden_at = [AT_FIRST, AT_SCENE, AT_SCENE + 4, AT_SCENE + 8, AT_SCENE + 12, AT_WC + 4, AT_WC + 8, AT_WC + 12]
+        hidden = {}
 
-        hidden = {0: sbuf("hidden0", [S], F32, "wc_raw0")}
-        first_banks = [next_bank() for i in range(2)]
-        for i in range(2):
-            table_passes(0, i, first_banks[i])
-        scene_pass_and_gelu(0, 0, first_banks[0], hidden[0][:, halves[0]])
-        scatter(0, hidden[0][:, halves[0]], slots[:, list_halves[0]], first_factors[:])
-        scene_pass_and_gelu(0, 1, first_banks[1], hidden[0][:, halves[1]])
-        times_gain(hidden[0][:, halves[1]], hidden[0][:, halves[1]], gain_cols[:, 0:1])
-        wc_q.append(quantised_operand("wc1", wc_raw[1:2], nc.scalar.copy, "woven3", "first_factors"))
-        scatter(0, hidden[0][:, halves[1]], slots[:, list_halves[1]], wgs_sb[:, halves[1]])
-
-        before_gain = sbuf("hidden1_before_gain", [S], F32, "scene_raw1")
-        natural_tile(1, before_gain)
-        hidden.update({1: sbuf("hidden1", [S], F32, "spare")})
-        times_gain(hidden[1][:], before_gain[:], gain_cols[:, 1:2])
-        scatter(1, hidden[1][:], slots[:], wgs_sb[:])
-
-        hidden.update({2: sbuf("hidden2", [S], F32, "wc_raw1")})
-        used = natural_tile(2, hidden[2])
-        times_gain(hidden[2][:], hidden[2][:], gain_cols[:, 2:3])
-        wc_q.append(quantised_operand("wc2", wc_raw[2:4], nc.scalar.copy, "scene_raw1", "spare"))
-        hidden.update({3: sbuf("hidden3", [S], F32, "wc_raw3")})
-        natural_tile(3, hidden[3])
-        times_gain(hidden[3][:], hidden[3][:], gain_cols[:, 3:4])
-        turn_wgs(1, used[1])
-
-        two_tiles = sbuf("hidden45", [2, S], F32, "scene_raw0")
-        hidden.update({4: two_tiles[:, 0], 5: two_tiles[:, 1], 6: sbuf("hidden6", [S], F32, "scene_raw1")[:]})
-        last_before_gain = sbuf("hidden7_before_gain", [S], F32, "wc_raw2")
-        by_entry = [sbuf(f"by_entry{pair}", [2, PACK, P], F32, f"woven{pair}") for pair in range(4)]
-        for b in range(S // P):
-            bank = next_bank()
-            entries = slice(b * P, (b + 1) * P)
-            for a in range(2):
-                mx_pass(bank[:], picked_operand(a, entries), w4_operand(a, 2, slice(GROUP, H)), a == 0, False)
-            mx_pass(bank[:], columns_of(scene_q[b // 4], slice(b % 4 * P, (b % 4 + 1) * P)), columns_of(wc_q[2], slice(0, GROUP)),
-                    False, True)
-            nc.scalar.activation(by_entry[b // 2][:, b % 2], bank[:].rearrange("j (q t) -> j t q", t=PACK), ACT.Gelu_apprx_tanh)
-        for t in range(PACK):
-            deal_wgs(1, t, next_bank())
+        def make_hidden(c):
+            hidden.update({c: sbuf(f"hidden{c}", [S], F32, hidden_at[c])})
             for i in range(2):
                 bank = next_bank()
-                for b in range(4):
-                    nc.tensor.transpose(bank[:, b * P : (b + 1) * P], by_entry[2 * i + b // 2][:, b % 2, t], ident[:])
-                if t < PACK - 1:
-                    times_gain(hidden[GROUP_TILES + t][:, halves[i]], bank[:], gain_dealt[:, t : t + 1])
-                else:
-                    nc.scalar.copy(last_before_gain[:, halves[i]], bank[:])
+                if c < 2:
+                    table_passes(c, i, bank, True)
+                scene_pass(c, i, bank, c >= 2)
+                if c >= 2:
+                    table_passes(c, i, bank, False)
+                gelu(i, bank, hidden[c])
 
         def store_page(c):
             nc.sync.dma_start(out=rows_of_tile(out_1, c), in_=page[c][:])
 
+        def scatter(c):
+            nc.vector.tensor_tensor(page[c][:].indirect(slots[:]), hidden[c][:], factors[c][:], ALU.mult)
+
+        def scatter_half(c, i, weights):
+            nc.vector.tensor_tensor(page[c][:].indirect(slots[:, list_halves[i]]), hidden[c][:, halves[i]], weights, ALU.mult)
+
+        hidden.update({0: sbuf("hidden0", [S], F32, hidden_at[0])})
+        first_banks = [next_bank() for i in range(2)]
+        for i in range(2):
+            table_passes(0, i, first_banks[i], True)
+        for i in range(2):
+            scene_pass(0, i, first_banks[i], False)
+            gelu(i, first_banks[i], hidden[0])
+        scatter_half(0, 0, factors[0][:, halves[0]])
+        woven = woven_wc(1, AT_WOVEN + 9)
+        weave(woven[:], wc_raw[1][:], nc.scalar.copy)
+        wc_q.append(quantised("wc1", woven, S + wc_pieces[1].start))
+        late_factors = sbuf("late_factors", [BANK], F32, AT_WC + 2)
+        times_gain(late_factors[:], wgs_sb[1][:], gain_cols[:, 0:1])
+        scatter_half(0, 1, late_factors[:])
+        late_gain = sbuf("late_gain", [GROUP_TILES], F32, AT_SCALES + 1)
+        nc.scalar.copy(late_gain[:], gain_cols[:])
+        natural_factors(1, 1, late_gain)
+        woven = woven_wc(2, AT_WOVEN + 9)
+        weave(woven[:], wc_raw[2][:], nc.scalar.copy)
+        wc_q.append(quantised("wc2", woven, S + wc_pieces[2].start))
+        make_hidden(1)
+        scatter(1)
+        woven = woven_wc(3, AT_WOVEN + 10)
+        nc.scalar.copy(woven[:].rearrange("p (t m) j -> p m j t", t=PACK), wc_raw[3][:].rearrange("p j (m t) -> p m j t", t=PACK))
+        wc_q.append(quantised("wc3", woven, S + wc_pieces[3].start))
+        for c in (2, 3):
+            natural_factors(c, 1, late_gain)
+            make_hidden(c)
+        w4_dealt.append(sbuf("w4_dealt", [2, 2 * GROUP], U8, AT_W4_DEALT))
+        nc.scalar.copy(w4_dealt[0][:].bitcast(U16).rearrange("p a (t m) -> p a t m", t=PACK),
+                       w4[2][:].bitcast(U16).rearrange("p a (m t) -> p a t m", t=PACK))
+        turned_wgs = turn_wgs(1)
+        for t in range(PACK):
+            dealt_factors(turned_wgs, 1, t)
+            make_hidden(GROUP_TILES + t)
+
+        w8 = sbuf("w8", [2, N], I32, AT_FIRST)
+        nc.sync.dma_start(out=w8[:], in_=w8_words.rearrange("a p c i -> p a (c i)").bitcast(I32))
+        for q in range(QUADRANTS):
+            nc.sync.dma_start(out=plane_rows(weight_scale[:, :, 0:N], q, 4),
+                              in_=w8_scales[:, 4 * q : 4 * q + 4, :].rearrange("a q c -> q a c").bitcast(I32))
+
         for c in range(LAST_TILE):
             if c > 1:
-                scatter(c, hidden[c][:], slots[:], wgs_sb[:] if c < GROUP_TILES else wgs_dealt[c - GROUP_TILES][:])
+                scatter(c)
             store_page(c)
 
-        turned = [sbuf(f"turned{k}", [4, 2, 2 * P], BF16) for k in range(CHUNKS)]
+        turned = sbuf("turned", [CHUNKS, 4, 2, 2 * P], BF16, AT_TURNED)
         for c in range(GROUP_TILES):
             for k in range(CHUNKS):
                 bank = next_bank()
                 for b in range(4):
                     nc.tensor.transpose(bank[:, b * P : (b + 1) * P], page[c][:, k * BANK + b * P : k * BANK + (b + 1) * P], ident[:])
                 nc.scalar.copy(
-                    turned[k][:, :, :, 64 * c : 64 * (c + 1)].rearrange("s b u (p e) -> s b u p e", e=2),
+                    turned[:, k, :, :, 64 * c : 64 * (c + 1)].rearrange("s b u (p e) -> s b u p e", e=2),
                     bank[:].rearrange("s (b p u e) -> s b u p e", b=4, u=2, e=2))
 
         def turn_back(k):
-            pairs = turned[k][:].rearrange("s b u w -> s (b u w)").bitcast(F32)
-            woven = sbuf(f"woven_page0{k}", [BANK, PACK], BF16, f"woven{k}")
+            words = turned[:, k].rearrange("s b u w -> s (b u w)").bitcast(F32)
+            woven = sbuf(f"woven_page0{k}", [BANK, PACK], BF16, AT_WOVEN + 4 * k)
             woven_pairs = woven[:].rearrange("p s j -> p (s j)").bitcast(F32)
             for two_blocks in range(2):
                 bank = next_bank()
                 for bu in range(4):
                     at = (4 * two_blocks + bu) * P
-                    nc.tensor.transpose(bank[:, bu * P : (bu + 1) * P], pairs[:, at : at + P], ident[:])
+                    nc.tensor.transpose(bank[:, bu * P : (bu + 1) * P], words[:, at : at + P], ident[:])
                 nc.scalar.copy(
                     woven_pairs[:, two_blocks * BANK : (two_blocks + 1) * BANK].rearrange("p (b s u) -> p b s u", b=2, u=2),
                     bank[:].rearrange("p (b u s) -> p b s u", b=2, u=2))
             return woven
 
-        code_tiles = {(0, 0): sbuf("early_codes", [EARLY_CHUNKS * BANK], I32)}
-        page_scale = [sbuf(f"page_scale{g}", [T2], U8) for g in range(2)]
+        woven_group0 = [turn_back(k) for k in range(CHUNKS)]
+        pairs = [sbuf(f"pairs{k}", [2, BANK, 2], BF16, AT_TURNED + 4 * k) for k in range(CHUNKS)]
 
-        def page_codes(g, cols):
-            first = max(first for group, first in code_tiles if group == g and first <= cols.start)
-            return code_tiles[(g, first)][:, cols.start - first : cols.stop - first]
+        def round_chunk(c, k):
+            t = c - GROUP_TILES
+            nc.scalar.copy(pairs[k][:, t // 2, :, t % 2], page[c][:, chunks[k]])
+
+        for c in range(GROUP_TILES, LAST_TILE):
+            for k in range(CHUNKS):
+                round_chunk(c, k)
+        scatter(LAST_TILE)
+        store_page(LAST_TILE)
+
+        page_codes = [sbuf(f"page_codes{g}", [T2], I32, at) for g, at in enumerate((AT_FACTORS, AT_PICKED))]
+        page_scale = [sbuf(f"page_scale{g}", [T2], U8, AT_PAGE_SCALE + 2 * g) for g in range(2)]
 
         def store_codes(g, cols):
-            nc.sync.dma_start(out=out_2[g].rearrange("p m t -> p (m t)").bitcast(I32)[:, cols], in_=page_codes(g, cols))
+            nc.sync.dma_start(out=out_2[g].rearrange("p m t -> p (m t)").bitcast(I32)[:, cols], in_=page_codes[g][:, cols])
 
         def store_scales(g):
             for q in range(QUADRANTS):
-                nc.gpsimd.dma_start(out=out_3[g, 4 * q : 4 * q + 4, :].bitcast(I32), in_=plane_rows(page_scale[g], q))
+                nc.sync.dma_start(out=out_3[g, 4 * q : 4 * q + 4, :].bitcast(I32), in_=plane_rows(page_scale[g], q))
 
-        woven_group0 = []
-        for k in range(CHUNKS):
-            woven_group0.append(turn_back(k))
-            if k < EARLY_CHUNKS:
-                quantise(page_codes(0, chunks[k]), page_scale[0][:, chunks[k]], woven_group0[k])
-        hidden.update({LAST_TILE: sbuf("hidden7", [S], F32, f"turned{EARLY_CHUNKS - 1}")})
-        times_gain(hidden[LAST_TILE][:], last_before_gain[:], gain_dealt[:, PACK - 1 : PACK])
-
-        pieces = [slice(0, BANK // 2), slice(BANK // 2, BANK)] + chunks[1:]
-        pairs = [sbuf(f"pairs{i}", [2, cols.stop - cols.start, 2], BF16, home)
-                 for i, (cols, home) in enumerate(zip(pieces, ["turned0", "wc_raw0", "turned3", "turned2", "wc_raw1"]))]
-
-        def round_piece(c, i):
-            t = c - GROUP_TILES
-            nc.scalar.copy(pairs[i][:, t // 2, :, t % 2], page[c][:, pieces[i]])
-
-        def weave_piece(i):
-            home = ["woven0", "wc_raw3", "woven1", "woven2", "woven3"][i]
-            woven = sbuf(f"woven_page1{i}", [pieces[i].stop - pieces[i].start, PACK], BF16, home)
+        def quantise_last(k):
+            round_chunk(LAST_TILE, k)
+            woven = sbuf(f"woven_page1{k}", [BANK, PACK], BF16, AT_WOVEN + 4 * k)
             words = woven[:].rearrange("p s j -> p (s j)").bitcast(U32).rearrange("p (s u) -> p s u", u=2)
-            nc.scalar.copy(words, pairs[i][:].rearrange("p u s e -> p u (s e)").bitcast(U32).rearrange("p u s -> p s u"))
-            return woven
+            nc.scalar.copy(words, pairs[k][:].rearrange("p u s e -> p u (s e)").bitcast(U32).rearrange("p u s -> p s u"))
+            quantise(page_codes[1][:, chunks[k]], page_scale[1][:, chunks[k]], woven)
 
-        def second_pass(out, n, g, cols, start, stop):
-            mx_pass(out, (w8[:, g, n * P : (n + 1) * P].bitcast(FP8X4), w8_scale[:, g, n * P : (n + 1) * P]),
-                    (page_codes(g, cols).bitcast(FP8X4), page_scale[g][:, cols]), start, stop)
+        def second_pass(n, k, g):
+            mx_pass(banks[2 * n + k % 2][:],
+                    (w8[:, g, n * P : (n + 1) * P].bitcast(FP8X4), weight_scale[4:P, g, n * P : (n + 1) * P]),
+                    (page_codes[g][:, chunks[k]].bitcast(FP8X4), page_scale[g][:, chunks[k]]), g == 0, g == 1)
 
-        def banks_of_piece(i):
-            if i < 2:
-                return [(banks[2 * i + a], [2 * a, 2 * a + 1]) for a in range(2)]
-            return [(banks[4 + n], [n]) for n in range(N // P)]
+        def add_bias(n, k):
+            sums = result[n // 2][:, n % 2, chunks[k]]
+            nc.vector.tensor_tensor(sums, banks[2 * n + k % 2][:], sums, ALU.add)
 
-        def second_passes(i, g):
-            cols = pieces[i]
-            width = cols.stop - cols.start
-            for bank, blocks in banks_of_piece(i):
-                for at, n in enumerate(blocks):
-                    second_pass(bank[:, at * width : (at + 1) * width], n, g, cols,
-                                g == 0 and at == 0, g == 1 and at == len(blocks) - 1)
+        def store_result(n, cols):
+            nc.sync.dma_start(out=out_rows[:, n, cols], in_=result[n // 2][:, n % 2, cols])
 
-        def add_bias(bank, blocks, cols):
-            sums = result[blocks[0] // 2][:, blocks[0] % 2 : blocks[-1] % 2 + 1, cols]
-            nc.vector.tensor_tensor(sums, bank[:].rearrange("p (n s) -> p n s", n=len(blocks)), sums, ALU.add)
-
-        def store_result(blocks, cols):
-            nc.sync.dma_start(out=out_rows[:, blocks[0] : blocks[-1] + 1, cols],
-                              in_=result[blocks[0] // 2][:, blocks[0] % 2 : blocks[-1] % 2 + 1, cols])
-
-        for c in range(GROUP_TILES, LAST_TILE):
-            for i in range(len(pieces)):
-                round_piece(c, i)
-        store_codes(0, slice(0, EARLY_CHUNKS * BANK))
-        for i in range(3):
-            second_passes(i, 0)
-        scatter(LAST_TILE, hidden[LAST_TILE][:], slots[:], wgs_dealt[PACK - 1][:])
-        store_page(LAST_TILE)
-        code_tiles.update({(0, EARLY_CHUNKS * BANK): sbuf("late_codes", [T2 - EARLY_CHUNKS * BANK], I32, f"wgs_dealt{PACK - 1}")})
-        code_tiles.update({(1, 0): sbuf("codes_of_group1", [T2], I32, "picking")})
-        for k in range(EARLY_CHUNKS, CHUNKS):
-            quantise(page_codes(0, chunks[k]), page_scale[0][:, chunks[k]], woven_group0[k])
-        store_codes(0, slice(EARLY_CHUNKS * BANK, T2))
+        for k in range(CHUNKS):
+            quantise(page_codes[0][:, chunks[k]], page_scale[0][:, chunks[k]], woven_group0[k])
+        store_codes(0, slice(0, T2))
         store_scales(0)
-        for i in range(3):
-            round_piece(LAST_TILE, i)
-            quantise(page_codes(1, pieces[i]), page_scale[1][:, pieces[i]], weave_piece(i))
-            store_codes(1, pieces[i])
-            second_passes(i, 1)
-            for bank, blocks in banks_of_piece(i):
-                add_bias(bank, blocks, pieces[i])
-                if blocks[-1] % 2 == 1:
-                    store_result([blocks[-1] - 1, blocks[-1]], pieces[i])
-        for i in (3, 4):
-            round_piece(LAST_TILE, i)
-            quantise(page_codes(1, pieces[i]), page_scale[1][:, pieces[i]], weave_piece(i))
-        store_scales(1)
-        second_half = slice(pieces[3].start, T2)
-        store_codes(1, second_half)
+        for k in (0, 1):
+            quantise_last(k)
+        first_half, second_half = slice(0, T2 // 2), slice(T2 // 2, T2)
+        store_codes(1, first_half)
+        for k in (0, 1):
+            for g in range(2):
+                for n in range(N // P):
+                    second_pass(n, k, g)
         for n in range(N // P):
-            for i in (3, 4):
-                bank = banks[2 * n + i - 3]
+            for k in (0, 1):
+                add_bias(n, k)
+            store_result(n, first_half)
+        for k in (2, 3):
+            quantise_last(k)
+        store_codes(1, second_half)
+        store_scales(1)
+        for n in range(N // P):
+            for k in (2, 3):
                 for g in range(2):
-                    second_pass(bank[:], n, g, pieces[i], g == 0, g == 1)
-                add_bias(bank, [n], pieces[i])
+                    second_pass(n, k, g)
+                add_bias(n, k)
                 if n == N // P - 1:
-                    store_result([n], pieces[i])
+                    store_result(n, chunks[k])
             if n < N // P - 1:
-                store_result([n], second_half)
+                store_result(n, second_half)

@@ -30,10 +30,10 @@ KIB = 1024
 FLOPS = 2 * (1024 + 512) * H * S + 2 * H * N * T2
 
 AT_PAGE, AT_TABLE, AT_SCENE, AT_TURNED, AT_WOVEN, AT_FACTORS, AT_DEALT = 0, 64, 96, 112, 128, 144, 160
-AT_PICKED, AT_SCALE_ROWS, AT_DEALT_SCALE, AT_WC, AT_W4, AT_WGS = 176, 181, 184, 185, 201, 207
+AT_PICKED, AT_SCALE_ROWS, AT_WC, AT_W4, AT_WGS = 176, 176, 185, 201, 207
 AT_W4_DEALT = AT_W4 + 3
 AT_PICKED_SCALE, AT_PICKED_ROWS, AT_W4_SCALE, AT_CODES, AT_SCALES, AT_FIRST, AT_PAGE_SCALE, AT_SMALL = (
-    211, 213, 214, 216, 224, 226, 230, 234)
+    211, 236, 214, 216, 224, 226, 230, 234)
 
 
 def tile_list_narrator_prefix_cache_kernel(
@@ -62,7 +62,7 @@ def tile_list_narrator_prefix_cache_kernel(
         def plane_rows(plane, q, first=0):
             return plane[32 * q + first : 32 * q + first + 4].bitcast(I32)
 
-        tab_scale_rows = sbuf("tab_scale_rows", [T], U8, AT_SCALE_ROWS)
+        tab_scale_rows = sbuf("tab_scale_rows", [2, T], U8, AT_SCALE_ROWS)
         picked_scale = sbuf("picked_scale", [2, S], U8, AT_PICKED_SCALE)
         weight_scale = sbuf("weight_scale", [2, H], U8, AT_W4_SCALE)
         ident = sbuf("ident", [P], F32, AT_SMALL)
@@ -117,7 +117,7 @@ def tile_list_narrator_prefix_cache_kernel(
 
         nc.sync.dma_start(picks[:], offs)
         load_table(0, slice(0, T // 4))
-        nc.sync.dma_start(out=tab_scale_rows[0:P:4, :].bitcast(I32), in_=tab_scales.rearrange("a q t -> (a q) t").bitcast(I32))
+        nc.sync.dma_start(out=tab_scale_rows[4:P:8].bitcast(I32), in_=tab_scales.rearrange("a q t -> q a t").bitcast(I32))
         load_wgs(0)
         load_table(0, slice(T // 4, T))
         load_table(1, slice(0, T))
@@ -148,9 +148,8 @@ def tile_list_narrator_prefix_cache_kernel(
         def natural_factors(c, i, gains):
             times_gain(factors[c][:, halves[i]], wgs_sb[i][:], gains[:, c : c + 1])
 
-        def turn_wgs(i):
+        def turn_wgs(i, bank):
             turned_wgs = [sbuf(f"wgs_turned{i}{pair}", [2, PACK, QUADRANTS, 32], F32, AT_TURNED + 4 * (2 * i + pair)) for pair in range(2)]
-            bank = next_bank()
             for b in range(4):
                 nc.tensor.transpose(bank[:, b * P : (b + 1) * P], wgs_sb[i][:, b * P : (b + 1) * P], ident[:])
             for pair in range(2):
@@ -167,28 +166,22 @@ def tile_list_narrator_prefix_cache_kernel(
 
         for c in range(GROUP_TILES):
             natural_factors(c, 0, gain_cols)
-        turned_wgs = turn_wgs(0)
+        turned_wgs = turn_wgs(0, next_bank())
         for t in range(PACK):
             dealt_factors(turned_wgs, 0, t)
 
-        picked_rows = sbuf("picked_rows", [S], U8, AT_PICKED_ROWS)
-        nc.vector.tensor_copy(picked_rows[:], tab_scale_rows[:].indirect(picks[:]))
+        picked_rows = sbuf("picked_rows", [2, S], U8, AT_PICKED_ROWS)
         for a in range(2):
-            for q in range(QUADRANTS):
-                first = 4 * (16 * a + 4 * q)
-                nc.gpsimd.dma_start(out=plane_rows(picked_scale[:, a, :], q), in_=picked_rows[first : first + 16 : 4, :].bitcast(I32))
-        dealt_scale = sbuf("dealt_scale", [2, GROUP], U8, AT_DEALT_SCALE)
-        nc.vector.tensor_copy(dealt_scale[:].rearrange("p a (t m) -> p a t m", t=PACK),
-                              weight_scale[:, :, GROUP:].rearrange("p a (m t) -> p a t m", t=PACK))
+            nc.vector.tensor_copy(picked_rows[:, a, :], tab_scale_rows[:, a, :].indirect(picks[:]))
+        for q in range(QUADRANTS):
+            nc.gpsimd.dma_start(out=plane_rows(picked_scale, q), in_=picked_rows[32 * q + 4 : 32 * (q + 1) : 8].bitcast(I32))
         picked = sbuf("picked", [2, S], U32, AT_PICKED)
         for a in range(2):
             nc.vector.tensor_copy(picked[:, a, :], tab[a][:].bitcast(U32).indirect(picks[:]))
+        dealt_scale = sbuf("dealt_scale", [2, GROUP], U8, AT_TABLE + 16)
+        nc.vector.tensor_copy(dealt_scale[:].rearrange("p a (t m) -> p a t m", t=PACK),
+                              weight_scale[:, :, GROUP:].rearrange("p a (m t) -> p a t m", t=PACK))
 
-        result = [sbuf(f"result{a}", [2, T2], F32, AT_TABLE + 16 * a) for a in range(2)]
-        bias_rows = bias.rearrange("(n p) t -> p n t", p=P)
-        out_rows = out_0.rearrange("(n p) t -> p n t", p=P)
-        for a in range(2):
-            nc.sync.dma_start(out=result[a][:], in_=bias_rows[:, 2 * a : 2 * a + 2, :])
 
         def weave(woven, raw, copy):
             copy(woven.rearrange("p (c i) j -> p c j i", i=4), raw.rearrange("p j (c i) -> p c j i", i=4))
@@ -257,7 +250,7 @@ def tile_list_narrator_prefix_cache_kernel(
         def make_hidden(c):
             hidden.update({c: sbuf(f"hidden{c}", [S], F32, hidden_at[c])})
             for i in range(2):
-                bank = next_bank()
+                bank = first_banks[i] if c == 1 else next_bank()
                 if c < 2:
                     table_passes(c, i, bank, True)
                 scene_pass(c, i, bank, c >= 2)
@@ -278,7 +271,6 @@ def tile_list_narrator_prefix_cache_kernel(
         first_banks = [next_bank() for i in range(2)]
         for i in range(2):
             table_passes(0, i, first_banks[i], True)
-        for i in range(2):
             scene_pass(0, i, first_banks[i], False)
             gelu(i, first_banks[i], hidden[0])
         scatter_half(0, 0, factors[0][:, halves[0]])
@@ -305,11 +297,16 @@ def tile_list_narrator_prefix_cache_kernel(
         w4_dealt.append(sbuf("w4_dealt", [2, 2 * GROUP], U8, AT_W4_DEALT))
         nc.scalar.copy(w4_dealt[0][:].bitcast(U16).rearrange("p a (t m) -> p a t m", t=PACK),
                        w4[2][:].bitcast(U16).rearrange("p a (m t) -> p a t m", t=PACK))
-        turned_wgs = turn_wgs(1)
+        turned_wgs = turn_wgs(1, banks[0])
         for t in range(PACK):
             dealt_factors(turned_wgs, 1, t)
             make_hidden(GROUP_TILES + t)
 
+        result = [sbuf(f"result{a}", [2, T2], F32, AT_TABLE + 16 * a) for a in range(2)]
+        bias_rows = bias.rearrange("(n p) t -> p n t", p=P)
+        out_rows = out_0.rearrange("(n p) t -> p n t", p=P)
+        for a in range(2):
+            nc.sync.dma_start(out=result[a][:], in_=bias_rows[:, 2 * a : 2 * a + 2, :])
         w8 = sbuf("w8", [2, N], I32, AT_FIRST)
         nc.sync.dma_start(out=w8[:], in_=w8_words.rearrange("a p c i -> p a (c i)").bitcast(I32))
         for q in range(QUADRANTS):

@@ -25,15 +25,14 @@ PAGE_TILES = H // P
 GROUP_TILES = GROUP // P
 LAST_TILE = PAGE_TILES - 1
 CHUNKS = T2 // BANK
+BLOCKS = N // P
 ALIGN = 64
 KIB = 1024
 FLOPS = 2 * (1024 + 512) * H * S + 2 * H * N * T2
 
-AT_PAGE, AT_TABLE, AT_SCENE, AT_TURNED, AT_WOVEN, AT_FACTORS, AT_DEALT = 0, 64, 96, 112, 128, 144, 160
-AT_PICKED, AT_SCALE_ROWS, AT_WC, AT_W4, AT_WGS = 176, 176, 185, 201, 207
-AT_W4_DEALT = AT_W4 + 3
-AT_PICKED_SCALE, AT_PICKED_ROWS, AT_W4_SCALE, AT_CODES, AT_SCALES, AT_FIRST, AT_PAGE_SCALE, AT_SMALL = (
-    211, 236, 214, 216, 224, 226, 230, 234)
+AT_PAGE, AT_TABLE, AT_SCENE, AT_TURNED, AT_WOVEN, AT_FACTORS, AT_PICKED = 0, 64, 97, 113, 129, 145, 177
+AT_WC, AT_W4, AT_WGS, AT_PICKED_SCALE, AT_WEIGHT_SCALE, AT_CODES, AT_SCALES = 185, 201, 206, 210, 212, 214, 222
+AT_FIRST, AT_PAGE_SCALE, AT_SMALL, AT_PICKED_ROWS = 224, 228, 232, 234
 
 
 def tile_list_narrator_prefix_cache_kernel(
@@ -62,9 +61,9 @@ def tile_list_narrator_prefix_cache_kernel(
         def plane_rows(plane, q, first=0):
             return plane[32 * q + first : 32 * q + first + 4].bitcast(I32)
 
-        tab_scale_rows = sbuf("tab_scale_rows", [2, T], U8, AT_SCALE_ROWS)
+        tab_scale_rows = sbuf("tab_scale_rows", [T], U8, AT_PICKED)
         picked_scale = sbuf("picked_scale", [2, S], U8, AT_PICKED_SCALE)
-        weight_scale = sbuf("weight_scale", [2, H], U8, AT_W4_SCALE)
+        weight_scale = sbuf("weight_scale", [2, H], U8, AT_WEIGHT_SCALE)
         ident = sbuf("ident", [P], F32, AT_SMALL)
         gain_rows = sbuf("gain_rows", [P], F32, AT_SMALL + 0.5)
         gain_cols = sbuf("gain_cols", [GROUP_TILES], F32, AT_SMALL + 1)
@@ -101,8 +100,8 @@ def tile_list_narrator_prefix_cache_kernel(
         def load_page(c):
             nc.sync.dma_start(out=page[c][:], in_=rows_of_tile(page0, c))
 
-        def load_table(a, cols):
-            nc.sync.dma_start(out=tab[a][:, cols], in_=tab_words[a].rearrange("p t i -> p (t i)").bitcast(I32)[:, cols])
+        def load_table(a):
+            nc.sync.dma_start(out=tab[a][:], in_=tab_words[a].rearrange("p t i -> p (t i)").bitcast(I32))
 
         def load_wc(i):
             nc.sync.dma_start(out=wc_raw[i][:], in_=wc_rows[:, :, wc_pieces[i]])
@@ -115,12 +114,11 @@ def tile_list_narrator_prefix_cache_kernel(
             columns = w4_words.rearrange("a p c -> p a c")[:, :, 2 * cols.start : 2 * cols.stop]
             nc.sync.dma_start(out=w4[i][:].bitcast(I32), in_=columns.bitcast(I32))
 
+        load_table(0)
         nc.sync.dma_start(picks[:], offs)
-        load_table(0, slice(0, T // 4))
-        nc.sync.dma_start(out=tab_scale_rows[4:P:8].bitcast(I32), in_=tab_scales.rearrange("a q t -> q a t").bitcast(I32))
+        nc.sync.dma_start(out=tab_scale_rows[0:P:4].bitcast(I32), in_=tab_scales.rearrange("a b t -> b a t").bitcast(I32))
         load_wgs(0)
-        load_table(0, slice(T // 4, T))
-        load_table(1, slice(0, T))
+        load_table(1)
         nc.sync.dma_start(out=scene_raw[:], in_=scene.rearrange("(p j) s -> p j s", j=PACK))
         load_w4(0)
         load_wc(0)
@@ -170,18 +168,16 @@ def tile_list_narrator_prefix_cache_kernel(
         for t in range(PACK):
             dealt_factors(turned_wgs, 0, t)
 
-        picked_rows = sbuf("picked_rows", [2, S], U8, AT_PICKED_ROWS)
-        for a in range(2):
-            nc.vector.tensor_copy(picked_rows[:, a, :], tab_scale_rows[:, a, :].indirect(picks[:]))
+        picked_rows = sbuf("picked_rows", [S], U8, AT_PICKED_ROWS)
+        nc.vector.tensor_copy(picked_rows[:], tab_scale_rows[:].indirect(picks[:]))
         for q in range(QUADRANTS):
-            nc.gpsimd.dma_start(out=plane_rows(picked_scale, q), in_=picked_rows[32 * q + 4 : 32 * (q + 1) : 8].bitcast(I32))
+            nc.gpsimd.dma_start(out=plane_rows(picked_scale, q), in_=picked_rows[32 * q : 32 * (q + 1) : 4].bitcast(I32))
         picked = sbuf("picked", [2, S], U32, AT_PICKED)
         for a in range(2):
             nc.vector.tensor_copy(picked[:, a, :], tab[a][:].bitcast(U32).indirect(picks[:]))
         dealt_scale = sbuf("dealt_scale", [2, GROUP], U8, AT_TABLE + 16)
         nc.vector.tensor_copy(dealt_scale[:].rearrange("p a (t m) -> p a t m", t=PACK),
                               weight_scale[:, :, GROUP:].rearrange("p a (m t) -> p a t m", t=PACK))
-
 
         def weave(woven, raw, copy):
             copy(woven.rearrange("p (c i) j -> p c j i", i=4), raw.rearrange("p j (c i) -> p c j i", i=4))
@@ -294,7 +290,7 @@ def tile_list_narrator_prefix_cache_kernel(
         for c in (2, 3):
             natural_factors(c, 1, late_gain)
             make_hidden(c)
-        w4_dealt.append(sbuf("w4_dealt", [2, 2 * GROUP], U8, AT_W4_DEALT))
+        w4_dealt.append(sbuf("w4_dealt", [2, 2 * GROUP], U8, AT_W4 + 3))
         nc.scalar.copy(w4_dealt[0][:].bitcast(U16).rearrange("p a (t m) -> p a t m", t=PACK),
                        w4[2][:].bitcast(U16).rearrange("p a (m t) -> p a t m", t=PACK))
         turned_wgs = turn_wgs(1, banks[0])
@@ -302,7 +298,7 @@ def tile_list_narrator_prefix_cache_kernel(
             dealt_factors(turned_wgs, 1, t)
             make_hidden(GROUP_TILES + t)
 
-        result = [sbuf(f"result{a}", [2, T2], F32, AT_TABLE + 16 * a) for a in range(2)]
+        result = [sbuf(f"result{a}", [2, T2], F32, AT_TABLE + 17 * a) for a in range(2)]
         bias_rows = bias.rearrange("(n p) t -> p n t", p=P)
         out_rows = out_0.rearrange("(n p) t -> p n t", p=P)
         for a in range(2):
@@ -357,15 +353,19 @@ def tile_list_narrator_prefix_cache_kernel(
 
         page_codes = [sbuf(f"page_codes{g}", [T2], I32, at) for g, at in enumerate((AT_FACTORS, AT_PICKED))]
         page_scale = [sbuf(f"page_scale{g}", [T2], U8, AT_PAGE_SCALE + 2 * g) for g in range(2)]
+        page_halves = [slice(0, T2 // 2), slice(T2 // 2, T2)]
 
         def store_codes(g, cols):
             nc.sync.dma_start(out=out_2[g].rearrange("p m t -> p (m t)").bitcast(I32)[:, cols], in_=page_codes[g][:, cols])
 
         def store_scales(g):
-            for q in range(QUADRANTS):
-                nc.sync.dma_start(out=out_3[g, 4 * q : 4 * q + 4, :].bitcast(I32), in_=plane_rows(page_scale[g], q))
+            for r in range(4):
+                nc.sync.dma_start(out=out_3[g, r : 16 : 4, :].bitcast(I32), in_=page_scale[g][r : P : 32].bitcast(I32))
 
-        def quantise_last(k):
+        def quantise_early(k):
+            quantise(page_codes[0][:, chunks[k]], page_scale[0][:, chunks[k]], woven_group0[k])
+
+        def quantise_late(k):
             round_chunk(LAST_TILE, k)
             woven = sbuf(f"woven_page1{k}", [BANK, PACK], BF16, AT_WOVEN + 4 * k)
             words = woven[:].rearrange("p s j -> p (s j)").bitcast(U32).rearrange("p (s u) -> p s u", u=2)
@@ -377,6 +377,10 @@ def tile_list_narrator_prefix_cache_kernel(
                     (w8[:, g, n * P : (n + 1) * P].bitcast(FP8X4), weight_scale[4:P, g, n * P : (n + 1) * P]),
                     (page_codes[g][:, chunks[k]].bitcast(FP8X4), page_scale[g][:, chunks[k]]), g == 0, g == 1)
 
+        def passes(k, g):
+            for n in range(BLOCKS):
+                second_pass(n, k, g)
+
         def add_bias(n, k):
             sums = result[n // 2][:, n % 2, chunks[k]]
             nc.vector.tensor_tensor(sums, banks[2 * n + k % 2][:], sums, ALU.add)
@@ -384,32 +388,38 @@ def tile_list_narrator_prefix_cache_kernel(
         def store_result(n, cols):
             nc.sync.dma_start(out=out_rows[:, n, cols], in_=result[n // 2][:, n % 2, cols])
 
-        for k in range(CHUNKS):
-            quantise(page_codes[0][:, chunks[k]], page_scale[0][:, chunks[k]], woven_group0[k])
-        store_codes(0, slice(0, T2))
+        for k in (0, 1):
+            quantise_early(k)
+        store_codes(0, page_halves[0])
+        passes(0, 0)
+        quantise_early(2)
+        quantise_late(0)
+        passes(0, 1)
+        passes(1, 0)
+        quantise_early(3)
+        store_codes(0, page_halves[1])
+        add_bias(0, 0)
+        quantise_late(1)
+        store_codes(1, page_halves[0])
+        passes(1, 1)
+        add_bias(1, 0)
+        for n in (0, 1):
+            add_bias(n, 1)
+            store_result(n, page_halves[0])
         store_scales(0)
-        for k in (0, 1):
-            quantise_last(k)
-        first_half, second_half = slice(0, T2 // 2), slice(T2 // 2, T2)
-        store_codes(1, first_half)
-        for k in (0, 1):
-            for g in range(2):
-                for n in range(N // P):
-                    second_pass(n, k, g)
-        for n in range(N // P):
+        for n in (2, 3):
+            quantise_late(n)
             for k in (0, 1):
                 add_bias(n, k)
-            store_result(n, first_half)
-        for k in (2, 3):
-            quantise_last(k)
-        store_codes(1, second_half)
+            store_result(n, page_halves[0])
+        store_codes(1, page_halves[1])
         store_scales(1)
-        for n in range(N // P):
+        for n in range(BLOCKS):
             for k in (2, 3):
                 for g in range(2):
                     second_pass(n, k, g)
                 add_bias(n, k)
-                if n == N // P - 1:
+                if n == BLOCKS - 1:
                     store_result(n, chunks[k])
-            if n < N // P - 1:
-                store_result(n, second_half)
+            if n < BLOCKS - 1:
+                store_result(n, page_halves[1])

@@ -372,54 +372,62 @@ def tile_list_narrator_prefix_cache_kernel(
             nc.scalar.copy(words, pairs[k][:].rearrange("p u s e -> p u (s e)").bitcast(U32).rearrange("p u s -> p s u"))
             quantise(page_codes[1][:, chunks[k]], page_scale[1][:, chunks[k]], woven)
 
+        sums = [(n, k) for k in (0, 1) for n in range(BLOCKS)] + [(n, k) for n in range(BLOCKS) for k in (2, 3)]
+
+        def bank_of(n, k):
+            return banks[sums.index((n, k)) % len(banks)]
+
         def second_pass(n, k, g):
-            mx_pass(banks[2 * n + k % 2][:],
+            mx_pass(bank_of(n, k)[:],
                     (w8[:, g, n * P : (n + 1) * P].bitcast(FP8X4), weight_scale[4:P, g, n * P : (n + 1) * P]),
                     (page_codes[g][:, chunks[k]].bitcast(FP8X4), page_scale[g][:, chunks[k]]), g == 0, g == 1)
 
-        def passes(k, g):
-            for n in range(BLOCKS):
-                second_pass(n, k, g)
-
         def add_bias(n, k):
-            sums = result[n // 2][:, n % 2, chunks[k]]
-            nc.vector.tensor_tensor(sums, banks[2 * n + k % 2][:], sums, ALU.add)
+            values = result[n // 2][:, n % 2, chunks[k]]
+            nc.vector.tensor_tensor(values, bank_of(n, k)[:], values, ALU.add)
+
+        def finish(n, k):
+            for g in range(2):
+                second_pass(n, k, g)
+            add_bias(n, k)
 
         def store_result(n, cols):
             nc.sync.dma_start(out=out_rows[:, n, cols], in_=result[n // 2][:, n % 2, cols])
 
-        for k in (0, 1):
+        later_chunks = slice(BANK, T2)
+        for k in range(CHUNKS):
             quantise_early(k)
-        store_codes(0, page_halves[0])
-        passes(0, 0)
-        quantise_early(2)
-        quantise_late(0)
-        passes(0, 1)
-        passes(1, 0)
-        quantise_early(3)
-        store_codes(0, page_halves[1])
-        add_bias(0, 0)
-        quantise_late(1)
-        store_codes(1, page_halves[0])
-        passes(1, 1)
-        add_bias(1, 0)
-        for n in (0, 1):
-            add_bias(n, 1)
-            store_result(n, page_halves[0])
+        store_codes(0, slice(0, T2))
         store_scales(0)
-        for n in (2, 3):
-            quantise_late(n)
-            for k in (0, 1):
-                add_bias(n, k)
-            store_result(n, page_halves[0])
-        store_codes(1, page_halves[1])
-        store_scales(1)
         for n in range(BLOCKS):
-            for k in (2, 3):
-                for g in range(2):
-                    second_pass(n, k, g)
-                add_bias(n, k)
-                if n == BLOCKS - 1:
-                    store_result(n, chunks[k])
-            if n < BLOCKS - 1:
-                store_result(n, page_halves[1])
+            second_pass(n, 0, 0)
+        quantise_late(0)
+        store_codes(1, chunks[0])
+        for n in range(BLOCKS):
+            second_pass(n, 0, 1)
+        for n in range(BLOCKS):
+            add_bias(n, 0)
+            store_result(n, chunks[0])
+            if n == 0:
+                quantise_late(1)
+        for n in range(BLOCKS):
+            for g in range(2):
+                second_pass(n, 1, g)
+        quantise_late(2)
+        add_bias(0, 1)
+        quantise_late(3)
+        store_codes(1, later_chunks)
+        store_scales(1)
+        for n in range(1, BLOCKS):
+            staged = sbuf(f"staged{n}", [BANK], F32, AT_TURNED + 16 - 2 * n)
+            nc.scalar.copy(staged[:], bank_of(n, 1)[:])
+            values = result[n // 2][:, n % 2, chunks[1]]
+            nc.gpsimd.tensor_tensor(values, staged[:], values, ALU.add)
+        for n, k in sums[2 * BLOCKS :]:
+            finish(n, k)
+            if (n, k) == sums[-2]:
+                store_result(n, slice(BANK, T2 - BANK))
+            elif (n, k) == sums[-1]:
+                store_result(n, chunks[k])
+            elif k == CHUNKS - 1:
+                store_result(n, later_chunks)

@@ -82,12 +82,12 @@ def tile_list_narrator_prefix_cache_kernel(
         slots = lists.tile([P, S // LIST_ROWS], U16)
         wc_rows = wc.rearrange("(p j) c -> p j c", j=PACK)
         wc_pieces = [slice(0, P), slice(P, 2 * P), slice(2 * P, GROUP), slice(GROUP, H)]
-        w4_pieces = [slice(0, 2 * P), slice(2 * P, GROUP), slice(GROUP, H)]
+        w4_pieces = [slice(0, P), slice(P, GROUP), slice(GROUP, H)]
         scene_raw = sbuf("scene_raw", [PACK, S], F32, AT_SCENE)
         wc_raw = [sbuf(f"wc_raw{i}", [PACK, cols.stop - cols.start], F32, AT_WC + cols.start / 64)
                   for i, cols in enumerate(wc_pieces)]
         tab = [sbuf(f"tab{a}", [T], I32, AT_TABLE + 16 * a) for a in range(2)]
-        w4 = [sbuf(f"w4_{i}", [2, 2 * (cols.stop - cols.start)], U8, AT_W4 + (0, 3, 1)[i])
+        w4 = [sbuf(f"w4_{i}", [2, 2 * (cols.stop - cols.start)], U8, (AT_WOVEN + 8.75, AT_W4 + 3, AT_W4 + 1)[i])
               for i, cols in enumerate(w4_pieces)]
         wgs_sb = [sbuf(f"wgs_sb{i}", [BANK], F32, AT_WGS + 2 * i) for i in range(2)]
         page = [sbuf(f"page{c}", [T2], F32, AT_PAGE + 8 * c) for c in range(PAGE_TILES)]
@@ -118,10 +118,10 @@ def tile_list_narrator_prefix_cache_kernel(
         nc.sync.dma_start(picks[:], offs)
         nc.sync.dma_start(out=tab_scale_rows[0:P:4].bitcast(I32), in_=tab_scales.rearrange("a b t -> b a t").bitcast(I32))
         load_wgs(0)
-        load_table(1)
         nc.sync.dma_start(out=scene_raw[:], in_=scene.rearrange("(p j) s -> p j s", j=PACK))
-        load_w4(0)
         load_wc(0)
+        load_table(1)
+        load_w4(0)
         nc.sync.dma_start(slots[:], offs2)
         load_page(0)
         load_wc(1)
@@ -173,11 +173,7 @@ def tile_list_narrator_prefix_cache_kernel(
         for q in range(QUADRANTS):
             nc.gpsimd.dma_start(out=plane_rows(picked_scale, q), in_=picked_rows[32 * q : 32 * (q + 1) : 4].bitcast(I32))
         picked = sbuf("picked", [2, S], U32, AT_PICKED)
-        for a in range(2):
-            nc.vector.tensor_copy(picked[:, a, :], tab[a][:].bitcast(U32).indirect(picks[:]))
-        dealt_scale = sbuf("dealt_scale", [2, GROUP], U8, AT_TABLE + 16)
-        nc.vector.tensor_copy(dealt_scale[:].rearrange("p a (t m) -> p a t m", t=PACK),
-                              weight_scale[:, :, GROUP:].rearrange("p a (m t) -> p a t m", t=PACK))
+        nc.vector.tensor_copy(picked[:, 0, :], tab[0][:].bitcast(U32).indirect(picks[:]))
 
         def weave(woven, raw, copy):
             copy(woven.rearrange("p (c i) j -> p c j i", i=4), raw.rearrange("p j (c i) -> p c j i", i=4))
@@ -185,9 +181,9 @@ def tile_list_narrator_prefix_cache_kernel(
         def quantise(codes, scale, woven):
             nc.vector.quantize_mx(out=codes.bitcast(FP8X4), scales=scale, in_=woven[:].rearrange("p c j -> p (c j)"))
 
-        def quantised(name, woven, first, codes_at=None):
+        def quantised(name, woven, first):
             width = woven.shape[1]
-            codes = sbuf(name + "_codes", [width], U32, codes_at or AT_CODES + first / 256)
+            codes = sbuf(name + "_codes", [width], U32, AT_CODES + first / 256)
             scale = sbuf(name + "_scale", [width], U8, AT_SCALES + first / 1024)
             quantise(codes[:], scale[:], woven)
             return codes, scale
@@ -201,11 +197,16 @@ def tile_list_narrator_prefix_cache_kernel(
         weave(scene_woven[1][:, 0:shared], scene_raw[:, :, BANK : BANK + shared], nc.scalar.copy)
         weave(scene_woven[0][:], scene_raw[:, :, halves[0]], nc.vector.tensor_copy)
         scene_q = [quantised("scene0", scene_woven[0], 0)]
-        woven = woven_wc(0, AT_WOVEN + 8)
+        woven = woven_wc(0, AT_WOVEN + 14)
         weave(woven[:], wc_raw[0][:], nc.scalar.copy)
-        wc_q = [quantised("wc0", woven, S, AT_WOVEN + 9)]
+        wc_q = [quantised("wc0", woven, S)]
         weave(scene_woven[1][:, shared:], scene_raw[:, :, BANK + shared :], nc.vector.tensor_copy)
         scene_q.append(quantised("scene1", scene_woven[1], BANK))
+        dealt_scale = sbuf("dealt_scale", [2, GROUP], U8, AT_WOVEN + 4)
+        nc.vector.tensor_copy(dealt_scale[:].rearrange("p a (t m) -> p a t m", t=PACK),
+                              weight_scale[:, :, GROUP:].rearrange("p a (m t) -> p a t m", t=PACK))
+        for i in range(2):
+            nc.vector.tensor_copy(picked[:, 1, halves[i]], tab[1][:].bitcast(U32).indirect(picks[:, list_halves[i]]))
 
         def mx_pass(out, stationary, moving, start, stop):
             nc.tensor.matmul_mx(out=out, lhsT=stationary[0], lhsT_scale=stationary[1], rhs=moving[0], rhs_scale=moving[1],
@@ -220,7 +221,7 @@ def tile_list_narrator_prefix_cache_kernel(
             if c >= GROUP_TILES:
                 at = (c - GROUP_TILES) * P
                 return w4_dealt[0][:, a, 2 * at : 2 * (at + P)].bitcast(FP4X4), dealt_scale[:, a, at : at + P]
-            piece = c // 2
+            piece = min(c, 1)
             at = c * P - w4_pieces[piece].start
             return w4[piece][:, a, 2 * at : 2 * (at + P)].bitcast(FP4X4), weight_scale[:, a, c * P : (c + 1) * P]
 
@@ -266,8 +267,8 @@ def tile_list_narrator_prefix_cache_kernel(
         hidden.update({0: sbuf("hidden0", [S], F32, hidden_at[0])})
         first_banks = [next_bank() for i in range(2)]
         for i in range(2):
-            table_passes(0, i, first_banks[i], True)
-            scene_pass(0, i, first_banks[i], False)
+            scene_pass(0, i, first_banks[i], True)
+            table_passes(0, i, first_banks[i], False)
             gelu(i, first_banks[i], hidden[0])
         scatter_half(0, 0, factors[0][:, halves[0]])
         woven = woven_wc(1, AT_WOVEN + 9)
@@ -276,7 +277,7 @@ def tile_list_narrator_prefix_cache_kernel(
         late_factors = sbuf("late_factors", [BANK], F32, AT_WC + 2)
         times_gain(late_factors[:], wgs_sb[1][:], gain_cols[:, 0:1])
         scatter_half(0, 1, late_factors[:])
-        late_gain = sbuf("late_gain", [GROUP_TILES], F32, AT_SCALES + 1)
+        late_gain = sbuf("late_gain", [GROUP_TILES], F32, AT_WOVEN + 8.75)
         nc.scalar.copy(late_gain[:], gain_cols[:])
         natural_factors(1, 1, late_gain)
         woven = woven_wc(2, AT_WOVEN + 9)
@@ -298,7 +299,7 @@ def tile_list_narrator_prefix_cache_kernel(
             dealt_factors(turned_wgs, 1, t)
             make_hidden(GROUP_TILES + t)
 
-        result = [sbuf(f"result{a}", [2, T2], F32, AT_TABLE + 17 * a) for a in range(2)]
+        result = [sbuf(f"result{a}", [2, T2], F32, AT_TABLE + 1 + 16 * a) for a in range(2)]
         bias_rows = bias.rearrange("(n p) t -> p n t", p=P)
         out_rows = out_0.rearrange("(n p) t -> p n t", p=P)
         for a in range(2):

@@ -68,8 +68,8 @@ def tile_list_narrator_prefix_cache_kernel(
         gain_rows = sbuf("gain_rows", [P], F32, AT_SMALL + 0.5)
         gain_cols = sbuf("gain_cols", [GROUP_TILES], F32, AT_SMALL + 1)
         gain_dealt = sbuf("gain_dealt", [PACK], F32, AT_SMALL + 1.0625)
-        for plane in (tab_scale_rows, weight_scale, picked_scale):
-            nc.vector.memset(plane[:].bitcast(I32), 0)
+        for plane in (weight_scale[:], tab_scale_rows[32:64], tab_scale_rows[64:P], picked_scale[:]):
+            nc.vector.memset(plane.bitcast(I32), 0)
         for q in range(QUADRANTS):
             nc.gpsimd.dma_start(out=plane_rows(weight_scale, q),
                                 in_=w4_scales[:, 4 * q : 4 * q + 4, :].rearrange("a q c -> q a c").bitcast(I32))
@@ -114,9 +114,9 @@ def tile_list_narrator_prefix_cache_kernel(
             columns = w4_words.rearrange("a p c -> p a c")[:, :, 2 * cols.start : 2 * cols.stop]
             nc.sync.dma_start(out=w4[i][:].bitcast(I32), in_=columns.bitcast(I32))
 
-        load_table(0)
         nc.sync.dma_start(picks[:], offs)
-        nc.sync.dma_start(out=tab_scale_rows[0:P:4].bitcast(I32), in_=tab_scales.rearrange("a b t -> b a t").bitcast(I32))
+        nc.sync.dma_start(out=tab_scale_rows[0:32].bitcast(I32), in_=tab_scales.rearrange("a b t -> b a t").bitcast(I32))
+        load_table(0)
         load_wgs(0)
         nc.sync.dma_start(out=scene_raw[:], in_=scene.rearrange("(p j) s -> p j s", j=PACK))
         load_wc(0)
@@ -171,7 +171,7 @@ def tile_list_narrator_prefix_cache_kernel(
         picked_rows = sbuf("picked_rows", [S], U8, AT_PICKED_ROWS)
         nc.vector.tensor_copy(picked_rows[:], tab_scale_rows[:].indirect(picks[:]))
         for q in range(QUADRANTS):
-            nc.gpsimd.dma_start(out=plane_rows(picked_scale, q), in_=picked_rows[32 * q : 32 * (q + 1) : 4].bitcast(I32))
+            nc.gpsimd.dma_start(out=plane_rows(picked_scale, q), in_=picked_rows[8 * q : 8 * (q + 1)].bitcast(I32))
         picked = sbuf("picked", [2, S], U32, AT_PICKED)
         nc.vector.tensor_copy(picked[:, 0, :], tab[0][:].bitcast(U32).indirect(picks[:]))
 

@@ -20,6 +20,7 @@ PACK = 4
 QUADRANTS = 4
 LIST_ROWS = 16
 BANK = 512
+QUARTER = S // 4
 GROUP = 512
 PAGE_TILES = H // P
 GROUP_TILES = GROUP // P
@@ -32,7 +33,7 @@ FLOPS = 2 * (1024 + 512) * H * S + 2 * H * N * T2
 
 AT_PAGE, AT_TABLE, AT_SCENE, AT_TURNED, AT_WOVEN, AT_FACTORS, AT_PICKED = 0, 64, 97, 113, 129, 145, 177
 AT_WC, AT_W4, AT_WGS, AT_PICKED_SCALE, AT_WEIGHT_SCALE, AT_CODES, AT_SCALES = 185, 201, 206, 210, 212, 214, 222
-AT_FIRST, AT_PAGE_SCALE, AT_SMALL, AT_PICKED_ROWS = 224, 228, 232, 234
+AT_FIRST, AT_PAGE_SCALE, AT_SMALL, AT_PICKED_ROWS, AT_W4_ROWS = 224, 228, 232, 234, 235
 
 
 def tile_list_narrator_prefix_cache_kernel(
@@ -55,24 +56,29 @@ def tile_list_narrator_prefix_cache_kernel(
             return keep.tile([P] + shape, dtype, name=name, align_bytes=ALIGN, offset=int(at * KIB))
 
         halves = [slice(0, BANK), slice(BANK, S)]
-        list_halves = [slice(0, BANK // LIST_ROWS), slice(BANK // LIST_ROWS, S // LIST_ROWS)]
+        quarters = [slice(q * QUARTER, (q + 1) * QUARTER) for q in range(4)]
         chunks = [slice(k * BANK, (k + 1) * BANK) for k in range(CHUNKS)]
+
+        def entries(offsets, cols):
+            return offsets[:, cols.start // LIST_ROWS : cols.stop // LIST_ROWS]
 
         def plane_rows(plane, q, first=0):
             return plane[32 * q + first : 32 * q + first + 4].bitcast(I32)
 
         tab_scale_rows = sbuf("tab_scale_rows", [T], U8, AT_PICKED)
-        picked_scale = sbuf("picked_scale", [2, S], U8, AT_PICKED_SCALE)
+        picked_scale = [sbuf(f"picked_scale{i}", [2, BANK], U8, AT_PICKED_SCALE + i) for i in range(2)]
         weight_scale = sbuf("weight_scale", [2, H], U8, AT_WEIGHT_SCALE)
         ident = sbuf("ident", [P], F32, AT_SMALL)
         gain_rows = sbuf("gain_rows", [P], F32, AT_SMALL + 0.5)
         gain_cols = sbuf("gain_cols", [GROUP_TILES], F32, AT_SMALL + 1)
         gain_dealt = sbuf("gain_dealt", [PACK], F32, AT_SMALL + 1.0625)
-        for plane in (weight_scale[:], tab_scale_rows[32:64], tab_scale_rows[64:P], picked_scale[:]):
-            nc.vector.memset(plane.bitcast(I32), 0)
+        w4_scale_rows = sbuf("w4_scale_rows", [GROUP], U8, AT_W4_ROWS)
+        w4_scale_dealt = sbuf("w4_scale_dealt", [GROUP], U8, AT_W4_ROWS + 0.5)
+        for plane in (tab_scale_rows, weight_scale, picked_scale[0], picked_scale[1], w4_scale_rows):
+            nc.vector.memset(plane[:].bitcast(I32), 0)
         for q in range(QUADRANTS):
-            nc.gpsimd.dma_start(out=plane_rows(weight_scale, q),
-                                in_=w4_scales[:, 4 * q : 4 * q + 4, :].rearrange("a q c -> q a c").bitcast(I32))
+            nc.gpsimd.dma_start(out=plane_rows(weight_scale[:, :, 0:GROUP], q),
+                                in_=w4_scales[:, 4 * q : 4 * q + 4, 0:GROUP].rearrange("a q c -> q a c").bitcast(I32))
         nc.gpsimd.memset(gain_rows[:], 0.0)
         nc.scalar.dma_start(out=gain_rows[0:GROUP_TILES, :], in_=gain[0:GROUP].rearrange("(c p) -> c p", p=P))
         nc.scalar.dma_start(out=gain_dealt[:], in_=gain[GROUP:].rearrange("(p t) -> p t", t=PACK))
@@ -81,14 +87,16 @@ def tile_list_narrator_prefix_cache_kernel(
         picks = lists.tile([P, S // LIST_ROWS], U16)
         slots = lists.tile([P, S // LIST_ROWS], U16)
         wc_rows = wc.rearrange("(p j) c -> p j c", j=PACK)
-        wc_pieces = [slice(0, P), slice(P, 2 * P), slice(2 * P, GROUP), slice(GROUP, H)]
-        w4_pieces = [slice(0, P), slice(P, GROUP), slice(GROUP, H)]
-        scene_raw = sbuf("scene_raw", [PACK, S], F32, AT_SCENE)
+        weight_pieces = [slice(0, 2 * P), slice(2 * P, GROUP), slice(GROUP, H)]
+        scene_rows = scene.rearrange("(p j) s -> p j s", j=PACK)
+        scene_pieces = [halves[0]] + quarters[2:]
+        scene_raw = [sbuf(f"scene_raw{i}", [PACK, cols.stop - cols.start], F32, AT_SCENE + cols.start / 64)
+                     for i, cols in enumerate(scene_pieces)]
         wc_raw = [sbuf(f"wc_raw{i}", [PACK, cols.stop - cols.start], F32, AT_WC + cols.start / 64)
-                  for i, cols in enumerate(wc_pieces)]
+                  for i, cols in enumerate(weight_pieces)]
         tab = [sbuf(f"tab{a}", [T], I32, AT_TABLE + 16 * a) for a in range(2)]
-        w4 = [sbuf(f"w4_{i}", [2, 2 * (cols.stop - cols.start)], U8, (AT_WOVEN + 8.75, AT_W4 + 3, AT_W4 + 1)[i])
-              for i, cols in enumerate(w4_pieces)]
+        w4 = [sbuf(f"w4_{i}", [2, 2 * (cols.stop - cols.start)], U8, AT_W4 + (0, 3, 1)[i])
+              for i, cols in enumerate(weight_pieces)]
         wgs_sb = [sbuf(f"wgs_sb{i}", [BANK], F32, AT_WGS + 2 * i) for i in range(2)]
         page = [sbuf(f"page{c}", [T2], F32, AT_PAGE + 8 * c) for c in range(PAGE_TILES)]
 
@@ -100,38 +108,59 @@ def tile_list_narrator_prefix_cache_kernel(
         def load_page(c):
             nc.sync.dma_start(out=page[c][:], in_=rows_of_tile(page0, c))
 
-        def load_table(a):
-            nc.sync.dma_start(out=tab[a][:], in_=tab_words[a].rearrange("p t i -> p (t i)").bitcast(I32))
+        def load_table(a, cols):
+            nc.sync.dma_start(out=tab[a][:, cols], in_=tab_words[a].rearrange("p t i -> p (t i)").bitcast(I32)[:, cols])
 
         def load_wc(i):
-            nc.sync.dma_start(out=wc_raw[i][:], in_=wc_rows[:, :, wc_pieces[i]])
+            nc.sync.dma_start(out=wc_raw[i][:], in_=wc_rows[:, :, weight_pieces[i]])
+
+        def load_scene(i):
+            nc.sync.dma_start(out=scene_raw[i][:], in_=scene_rows[:, :, scene_pieces[i]])
 
         def load_wgs(i):
             nc.sync.dma_start(out=wgs_sb[i][:], in_=wgs[:, halves[i]])
 
         def load_w4(i):
-            cols = w4_pieces[i]
+            cols = weight_pieces[i]
             columns = w4_words.rearrange("a p c -> p a c")[:, :, 2 * cols.start : 2 * cols.stop]
             nc.sync.dma_start(out=w4[i][:].bitcast(I32), in_=columns.bitcast(I32))
 
+        picked_rows = sbuf("picked_rows", [S], U8, AT_PICKED_ROWS)
+
+        def move_scales(planes, rows):
+            for q in (0, 2, 1, 3):
+                nc.sync.dma_start(out=plane_rows(planes, q), in_=rows[32 * q : 32 * (q + 1) : 4].bitcast(I32))
+
         nc.sync.dma_start(picks[:], offs)
-        nc.sync.dma_start(out=tab_scale_rows[0:32].bitcast(I32), in_=tab_scales.rearrange("a b t -> b a t").bitcast(I32))
-        load_table(0)
         load_wgs(0)
-        nc.sync.dma_start(out=scene_raw[:], in_=scene.rearrange("(p j) s -> p j s", j=PACK))
+        load_table(0, slice(0, T // 4))
+        nc.sync.dma_start(out=tab_scale_rows[0:P:4].bitcast(I32), in_=tab_scales.rearrange("a b t -> b a t").bitcast(I32))
+        load_table(0, slice(T // 4, T))
+        for i in range(2):
+            nc.vector.tensor_copy(picked_rows[:, halves[i]], tab_scale_rows[:].indirect(entries(picks, halves[i])))
+        load_scene(0)
+        move_scales(picked_scale[0], picked_rows[:, halves[0]])
         load_wc(0)
-        load_table(1)
+        nc.sync.dma_start(out=w4_scale_rows[0:P:4].bitcast(I32), in_=w4_scales[:, :, GROUP:].rearrange("a b c -> b a c").bitcast(I32))
+        nc.vector.tensor_copy(w4_scale_dealt[:].rearrange("p (t m) -> p t m", t=PACK),
+                              w4_scale_rows[:].rearrange("p (m t) -> p t m", t=PACK))
+        load_table(1, slice(0, T))
         load_w4(0)
         nc.sync.dma_start(slots[:], offs2)
         load_page(0)
+        load_page(1)
+        load_scene(1)
+        load_scene(2)
+        move_scales(picked_scale[1], picked_rows[:, halves[1]])
+        load_wgs(1)
         load_wc(1)
         load_w4(1)
-        load_wgs(1)
+        load_page(2)
         load_wc(2)
-        load_page(1)
-        load_wc(3)
         load_w4(2)
-        for c in range(2, PAGE_TILES):
+        load_page(3)
+        move_scales(weight_scale[:, :, GROUP:], w4_scale_dealt)
+        for c in range(GROUP_TILES, PAGE_TILES):
             load_page(c)
 
         bank = next_bank()
@@ -143,8 +172,9 @@ def tile_list_narrator_prefix_cache_kernel(
 
         factors = [sbuf(f"factors{c}", [S], F32, AT_FACTORS + 4 * c) for c in range(PAGE_TILES)]
 
-        def natural_factors(c, i, gains):
-            times_gain(factors[c][:, halves[i]], wgs_sb[i][:], gains[:, c : c + 1])
+        def natural_factors(c, cols):
+            i = cols.start // BANK
+            times_gain(factors[c][:, cols], wgs_sb[i][:, cols.start - i * BANK : cols.stop - i * BANK], gain_cols[:, c : c + 1])
 
         def turn_wgs(i, bank):
             turned_wgs = [sbuf(f"wgs_turned{i}{pair}", [2, PACK, QUADRANTS, 32], F32, AT_TURNED + 4 * (2 * i + pair)) for pair in range(2)]
@@ -162,16 +192,6 @@ def tile_list_narrator_prefix_cache_kernel(
                 nc.tensor.transpose(bank[:, b * P : (b + 1) * P], block, ident[:])
             times_gain(factors[GROUP_TILES + t][:, halves[i]], bank[:], gain_dealt[:, t : t + 1])
 
-        for c in range(GROUP_TILES):
-            natural_factors(c, 0, gain_cols)
-        turned_wgs = turn_wgs(0, next_bank())
-        for t in range(PACK):
-            dealt_factors(turned_wgs, 0, t)
-
-        picked_rows = sbuf("picked_rows", [S], U8, AT_PICKED_ROWS)
-        nc.vector.tensor_copy(picked_rows[:], tab_scale_rows[:].indirect(picks[:]))
-        for q in range(QUADRANTS):
-            nc.gpsimd.dma_start(out=plane_rows(picked_scale, q), in_=picked_rows[8 * q : 8 * (q + 1)].bitcast(I32))
         picked = sbuf("picked", [2, S], U32, AT_PICKED)
         nc.vector.tensor_copy(picked[:, 0, :], tab[0][:].bitcast(U32).indirect(picks[:]))
 
@@ -188,25 +208,32 @@ def tile_list_narrator_prefix_cache_kernel(
             quantise(codes[:], scale[:], woven)
             return codes, scale
 
-        scene_woven = [sbuf(f"scene_woven{i}", [BANK, PACK], BF16, AT_WOVEN + 4 * i) for i in range(2)]
+        scene_q = sbuf("scene_codes", [S], U32, AT_CODES), sbuf("scene_scale", [S], U8, AT_SCALES)
 
-        def woven_wc(i, at):
-            return sbuf(f"wc_woven{i}", [wc_pieces[i].stop - wc_pieces[i].start, PACK], BF16, at)
+        def quantise_scene(i, copy):
+            cols = scene_pieces[i]
+            woven = sbuf(f"scene_woven{i}", [cols.stop - cols.start, PACK], BF16, AT_WOVEN + 4 * min(i, 1))
+            weave(woven[:], scene_raw[i][:], copy)
+            quantise(scene_q[0][:, cols], scene_q[1][:, cols], woven)
 
-        shared = BANK // 2
-        weave(scene_woven[1][:, 0:shared], scene_raw[:, :, BANK : BANK + shared], nc.scalar.copy)
-        weave(scene_woven[0][:], scene_raw[:, :, halves[0]], nc.vector.tensor_copy)
-        scene_q = [quantised("scene0", scene_woven[0], 0)]
-        woven = woven_wc(0, AT_WOVEN + 14)
-        weave(woven[:], wc_raw[0][:], nc.scalar.copy)
-        wc_q = [quantised("wc0", woven, S)]
-        weave(scene_woven[1][:, shared:], scene_raw[:, :, BANK + shared :], nc.vector.tensor_copy)
-        scene_q.append(quantised("scene1", scene_woven[1], BANK))
-        dealt_scale = sbuf("dealt_scale", [2, GROUP], U8, AT_WOVEN + 4)
-        nc.vector.tensor_copy(dealt_scale[:].rearrange("p a (t m) -> p a t m", t=PACK),
-                              weight_scale[:, :, GROUP:].rearrange("p a (m t) -> p a t m", t=PACK))
-        for i in range(2):
-            nc.vector.tensor_copy(picked[:, 1, halves[i]], tab[1][:].bitcast(U32).indirect(picks[:, list_halves[i]]))
+        def woven_wc(i):
+            cols = weight_pieces[i]
+            return sbuf(f"wc_woven{i}", [cols.stop - cols.start, PACK], BF16, AT_WOVEN + 8 + cols.start / 128)
+
+        def quantised_wc(i):
+            woven = woven_wc(i)
+            weave(woven[:], wc_raw[i][:], nc.scalar.copy)
+            return quantised(f"wc{i}", woven, S + weight_pieces[i].start)
+
+        quantise_scene(0, nc.vector.tensor_copy)
+        wc_q = [quantised_wc(0)]
+        for c in range(GROUP_TILES):
+            natural_factors(c, halves[0])
+        turned_wgs = turn_wgs(0, next_bank())
+        for t in range(PACK):
+            dealt_factors(turned_wgs, 0, t)
+        for cols in quarters[:2] + halves[1:]:
+            nc.vector.tensor_copy(picked[:, 1, cols], tab[1][:].bitcast(U32).indirect(entries(picks, cols)))
 
         def mx_pass(out, stationary, moving, start, stop):
             nc.tensor.matmul_mx(out=out, lhsT=stationary[0], lhsT_scale=stationary[1], rhs=moving[0], rhs_scale=moving[1],
@@ -218,42 +245,40 @@ def tile_list_narrator_prefix_cache_kernel(
         w4_dealt = []
 
         def w4_operand(a, c):
-            if c >= GROUP_TILES:
-                at = (c - GROUP_TILES) * P
-                return w4_dealt[0][:, a, 2 * at : 2 * (at + P)].bitcast(FP4X4), dealt_scale[:, a, at : at + P]
-            piece = min(c, 1)
-            at = c * P - w4_pieces[piece].start
-            return w4[piece][:, a, 2 * at : 2 * (at + P)].bitcast(FP4X4), weight_scale[:, a, c * P : (c + 1) * P]
+            words, at = (w4_dealt[0], c * P - GROUP) if c >= GROUP_TILES else (w4[c // 2], c % 2 * P)
+            return words[:, a, 2 * at : 2 * (at + P)].bitcast(FP4X4), weight_scale[:, a, c * P : (c + 1) * P]
 
         def wc_operand(c):
-            piece = max(i for i, cols in enumerate(wc_pieces) if cols.start <= c * P)
-            at = c * P - wc_pieces[piece].start
+            piece = min(c // 2, 2)
+            at = c * P - weight_pieces[piece].start
             return columns_of(wc_q[piece], slice(at, at + P))
 
-        def table_passes(c, i, bank, opening):
+        def table_passes(c, cols, sums, opening):
+            i = cols.start // BANK
+            within = slice(cols.start - i * BANK, cols.stop - i * BANK)
             for a in range(2):
-                mx_pass(bank[:], w4_operand(a, c), (picked[:, a, halves[i]].bitcast(FP8X4), picked_scale[:, a, halves[i]]),
+                mx_pass(sums, w4_operand(a, c), (picked[:, a, cols].bitcast(FP8X4), picked_scale[i][:, a, within]),
                         opening and a == 0, not opening and a == 1)
 
-        def scene_pass(c, i, bank, opening):
-            mx_pass(bank[:], wc_operand(c), columns_of(scene_q[i], slice(0, BANK)), opening, not opening)
+        def scene_pass(c, cols, sums, opening):
+            mx_pass(sums, wc_operand(c), columns_of(scene_q, cols), opening, not opening)
 
-        def gelu(i, bank, out):
-            nc.scalar.activation(out[:, halves[i]], bank[:], ACT.Gelu_apprx_tanh)
+        def gelu_of_sums(c, cols, out, scene_first):
+            sums = next_bank()[:, 0 : cols.stop - cols.start]
+            if scene_first:
+                scene_pass(c, cols, sums, True)
+            table_passes(c, cols, sums, not scene_first)
+            if not scene_first:
+                scene_pass(c, cols, sums, False)
+            nc.scalar.activation(out, sums, ACT.Gelu_apprx_tanh)
 
-        hidden_at = [AT_FIRST, AT_SCENE, AT_SCENE + 4, AT_SCENE + 8, AT_SCENE + 12, AT_WC + 4, AT_WC + 8, AT_WC + 12]
+        hidden_at = {2: AT_SCENE, 3: AT_WC + 8, 4: AT_SCENE + 4, 5: AT_SCENE + 8, 6: AT_SCENE + 12, 7: AT_WC + 12}
         hidden = {}
 
         def make_hidden(c):
             hidden.update({c: sbuf(f"hidden{c}", [S], F32, hidden_at[c])})
-            for i in range(2):
-                bank = first_banks[i] if c == 1 else next_bank()
-                if c < 2:
-                    table_passes(c, i, bank, True)
-                scene_pass(c, i, bank, c >= 2)
-                if c >= 2:
-                    table_passes(c, i, bank, False)
-                gelu(i, bank, hidden[c])
+            for cols in halves:
+                gelu_of_sums(c, cols, hidden[c][:, cols], c > 2)
 
         def store_page(c):
             nc.sync.dma_start(out=rows_of_tile(out_1, c), in_=page[c][:])
@@ -261,40 +286,42 @@ def tile_list_narrator_prefix_cache_kernel(
         def scatter(c):
             nc.vector.tensor_tensor(page[c][:].indirect(slots[:]), hidden[c][:], factors[c][:], ALU.mult)
 
-        def scatter_half(c, i, weights):
-            nc.vector.tensor_tensor(page[c][:].indirect(slots[:, list_halves[i]]), hidden[c][:, halves[i]], weights, ALU.mult)
+        def scatter_piece(c, cols, values):
+            nc.vector.tensor_tensor(page[c][:].indirect(entries(slots, cols)), values, factors[c][:, cols], ALU.mult)
 
-        hidden.update({0: sbuf("hidden0", [S], F32, hidden_at[0])})
-        first_banks = [next_bank() for i in range(2)]
-        for i in range(2):
-            scene_pass(0, i, first_banks[i], True)
-            table_passes(0, i, first_banks[i], False)
-            gelu(i, first_banks[i], hidden[0])
-        scatter_half(0, 0, factors[0][:, halves[0]])
-        woven = woven_wc(1, AT_WOVEN + 9)
-        weave(woven[:], wc_raw[1][:], nc.scalar.copy)
-        wc_q.append(quantised("wc1", woven, S + wc_pieces[1].start))
-        late_factors = sbuf("late_factors", [BANK], F32, AT_WC + 2)
-        times_gain(late_factors[:], wgs_sb[1][:], gain_cols[:, 0:1])
-        scatter_half(0, 1, late_factors[:])
-        late_gain = sbuf("late_gain", [GROUP_TILES], F32, AT_WOVEN + 8.75)
-        nc.scalar.copy(late_gain[:], gain_cols[:])
-        natural_factors(1, 1, late_gain)
-        woven = woven_wc(2, AT_WOVEN + 9)
-        weave(woven[:], wc_raw[2][:], nc.scalar.copy)
-        wc_q.append(quantised("wc2", woven, S + wc_pieces[2].start))
-        make_hidden(1)
-        scatter(1)
-        woven = woven_wc(3, AT_WOVEN + 10)
-        nc.scalar.copy(woven[:].rearrange("p (t m) j -> p m j t", t=PACK), wc_raw[3][:].rearrange("p j (m t) -> p m j t", t=PACK))
-        wc_q.append(quantised("wc3", woven, S + wc_pieces[3].start))
-        for c in (2, 3):
-            natural_factors(c, 1, late_gain)
-            make_hidden(c)
+        def quarter_piece(c, q, at):
+            values = sbuf(f"hidden{c}_{q}", [QUARTER], F32, at)
+            gelu_of_sums(c, quarters[q], values[:], q < 2)
+            scatter_piece(c, quarters[q], values[:])
+
+        first = sbuf("hidden0_first", [BANK], F32, AT_FIRST)
+        for cols in quarters[:2]:
+            gelu_of_sums(0, cols, first[:, cols], True)
+        scatter_piece(0, halves[0], first[:])
+        quarter_piece(1, 0, AT_FIRST + 2)
+        quantise_scene(1, nc.scalar.copy)
+        quarter_piece(1, 1, AT_SCENE + 8)
+        quantise_scene(2, nc.scalar.copy)
+        natural_factors(0, quarters[2])
+        quarter_piece(0, 2, AT_FIRST + 3)
+        natural_factors(1, halves[1])
+        quarter_piece(1, 2, AT_WOVEN + 6)
+        wc_q.append(quantised_wc(1))
+        natural_factors(0, quarters[3])
+        for c in range(2):
+            quarter_piece(c, 3, AT_WC + 4 + c)
+        natural_factors(2, halves[1])
+        make_hidden(2)
+        natural_factors(3, halves[1])
+        woven = woven_wc(2)
+        nc.scalar.copy(woven[:].rearrange("p (t m) j -> p m j t", t=PACK), wc_raw[2][:].rearrange("p j (m t) -> p m j t", t=PACK))
+        scatter(2)
+        wc_q.append(quantised("wc2", woven, S + GROUP))
+        make_hidden(3)
         w4_dealt.append(sbuf("w4_dealt", [2, 2 * GROUP], U8, AT_W4 + 3))
         nc.scalar.copy(w4_dealt[0][:].bitcast(U16).rearrange("p a (t m) -> p a t m", t=PACK),
                        w4[2][:].bitcast(U16).rearrange("p a (m t) -> p a t m", t=PACK))
-        turned_wgs = turn_wgs(1, banks[0])
+        turned_wgs = turn_wgs(1, next_bank())
         for t in range(PACK):
             dealt_factors(turned_wgs, 1, t)
             make_hidden(GROUP_TILES + t)
@@ -311,7 +338,7 @@ def tile_list_narrator_prefix_cache_kernel(
                               in_=w8_scales[:, 4 * q : 4 * q + 4, :].rearrange("a q c -> q a c").bitcast(I32))
 
         for c in range(LAST_TILE):
-            if c > 1:
+            if c > 2:
                 scatter(c)
             store_page(c)
 
@@ -398,7 +425,8 @@ def tile_list_narrator_prefix_cache_kernel(
         later_chunks = slice(BANK, T2)
         for k in range(CHUNKS):
             quantise_early(k)
-        store_codes(0, slice(0, T2))
+        for cols in page_halves:
+            store_codes(0, cols)
         store_scales(0)
         for n in range(BLOCKS):
             second_pass(n, 0, 0)
@@ -420,7 +448,7 @@ def tile_list_narrator_prefix_cache_kernel(
         store_codes(1, later_chunks)
         store_scales(1)
         for n in range(1, BLOCKS):
-            staged = sbuf(f"staged{n}", [BANK], F32, AT_TURNED + 16 - 2 * n)
+            staged = sbuf(f"staged{n}", [BANK], F32, (AT_TURNED + 12, AT_TURNED + 14, AT_WOVEN + 12)[n - 1])
             nc.scalar.copy(staged[:], bank_of(n, 1)[:])
             values = result[n // 2][:, n % 2, chunks[1]]
             nc.gpsimd.tensor_tensor(values, staged[:], values, ALU.add)

from contextlib import ExitStack

import concourse.mybir as mybir
from concourse.masks import make_identity

F32 = mybir.dt.float32
BF16 = mybir.dt.bfloat16
I32 = mybir.dt.int32
U32 = mybir.dt.uint32
U16 = mybir.dt.uint16
U8 = mybir.dt.uint8
FP8X4 = mybir.dt.float8_e4m3fn_x4
FP4X4 = mybir.dt.float4_e2m1fn_x4
ACT = mybir.ActivationFunctionType
ALU = mybir.AluOpType

P = 128
H, N, T, S, T2 = 1024, 512, 4096, 1024, 2048
PACK = 4
QUADRANTS = 4
LIST_ROWS = 16
BANK = 512
QUARTER = S // 4
GROUP = 512
PAGE_TILES = H // P
GROUP_TILES = GROUP // P
LAST_TILE = PAGE_TILES - 1
CHUNKS = T2 // BANK
BLOCKS = N // P
ALIGN = 64
KIB = 1024
FLOPS = 2 * (1024 + 512) * H * S + 2 * H * N * T2

AT_PAGE, AT_TABLE, AT_SCENE, AT_TURNED, AT_WOVEN, AT_FACTORS, AT_PICKED = 0, 64, 97, 113, 129, 145, 177
AT_WC, AT_W4, AT_WGS, AT_PICKED_SCALE, AT_WEIGHT_SCALE, AT_CODES, AT_SCALES = 185, 201, 206, 210, 212, 214, 222
AT_FIRST, AT_PAGE_SCALE, AT_SMALL, AT_PICKED_ROWS, AT_W4_ROWS = 224, 228, 232, 234, 235


def tile_list_narrator_prefix_cache_kernel(
    tc, tab_words, tab_scales, offs, w4_words, w4_scales, wc, scene, gain, page0, offs2, wgs,
    w8_words, w8_scales, bias, out_0, out_1, out_2, out_3,
):
    nc = tc.nc
    with ExitStack() as ctx:
        lists = ctx.enter_context(tc.tile_pool(name="lists", bufs=1))
        keep = ctx.enter_context(tc.tile_pool(name="keep", bufs=1))
        psum = ctx.enter_context(tc.psum_pool(name="psum", bufs=1))
        banks = [psum.tile([P, BANK], F32, name=f"bank{b}") for b in range(8)]
        fills = []

        def next_bank():
            fills.append(len(fills))
            return banks[fills[-1] % len(banks)]

        def sbuf(name, shape, dtype, at):
            return keep.tile([P] + shape, dtype, name=name, align_bytes=ALIGN, offset=int(at * KIB))

        halves = [slice(0, BANK), slice(BANK, S)]
        quarters = [slice(q * QUARTER, (q + 1) * QUARTER) for q in range(4)]
        chunks = [slice(k * BANK, (k + 1) * BANK) for k in range(CHUNKS)]

        def entries(offsets, cols):
            return offsets[:, cols.start // LIST_ROWS : cols.stop // LIST_ROWS]

        def plane_rows(plane, q, first=0):
            return plane[32 * q + first : 32 * q + first + 4].bitcast(I32)

        tab_scale_rows = sbuf("tab_scale_rows", [T], U8, AT_PICKED)
        picked_scale = [sbuf(f"picked_scale{i}", [2, BANK], U8, AT_PICKED_SCALE + i) for i in range(2)]
        weight_scale = sbuf("weight_scale", [2, H], U8, AT_WEIGHT_SCALE)
        ident = sbuf("ident", [P], F32, AT_SMALL)
        gain_rows = sbuf("gain_rows", [P], F32, AT_SMALL + 0.5)
        gain_cols = sbuf("gain_cols", [GROUP_TILES], F32, AT_SMALL + 1)
        gain_dealt = sbuf("gain_dealt", [PACK], F32, AT_SMALL + 1.0625)
        w4_scale_rows = sbuf("w4_scale_rows", [GROUP], U8, AT_W4_ROWS)
        w4_scale_dealt = sbuf("w4_scale_dealt", [GROUP], U8, AT_W4_ROWS + 0.5)
        for plane in (tab_scale_rows, weight_scale, picked_scale[0], picked_scale[1], w4_scale_rows):
            nc.vector.memset(plane[:].bitcast(I32), 0)
        for q in range(QUADRANTS):
            nc.gpsimd.dma_start(out=plane_rows(weight_scale[:, :, 0:GROUP], q),
                                in_=w4_scales[:, 4 * q : 4 * q + 4, 0:GROUP].rearrange("a q c -> q a c").bitcast(I32))
        nc.gpsimd.memset(gain_rows[:], 0.0)
        nc.scalar.dma_start(out=gain_rows[0:GROUP_TILES, :], in_=gain[0:GROUP].rearrange("(c p) -> c p", p=P))
        nc.scalar.dma_start(out=gain_dealt[:], in_=gain[GROUP:].rearrange("(p t) -> p t", t=PACK))
        make_identity(nc, ident[:])

        picks = lists.tile([P, S // LIST_ROWS], U16)
        slots = lists.tile([P, S // LIST_ROWS], U16)
        wc_rows = wc.rearrange("(p j) c -> p j c", j=PACK)
        weight_pieces = [slice(0, 2 * P), slice(2 * P, GROUP), slice(GROUP, H)]
        scene_rows = scene.rearrange("(p j) s -> p j s", j=PACK)
        scene_pieces = [halves[0]] + quarters[2:]
        scene_raw = [sbuf(f"scene_raw{i}", [PACK, cols.stop - cols.start], F32, AT_SCENE + cols.start / 64)
                     for i, cols in enumerate(scene_pieces)]
        wc_raw = [sbuf(f"wc_raw{i}", [PACK, cols.stop - cols.start], F32, AT_WC + cols.start / 64)
                  for i, cols in enumerate(weight_pieces)]
        tab = [sbuf(f"tab{a}", [T], I32, AT_TABLE + 16 * a) for a in range(2)]
        w4 = [sbuf(f"w4_{i}", [2, 2 * (cols.stop - cols.start)], U8, AT_W4 + (0, 3, 1)[i])
              for i, cols in enumerate(weight_pieces)]
        wgs_sb = [sbuf(f"wgs_sb{i}", [BANK], F32, AT_WGS + 2 * i) for i in range(2)]
        page = [sbuf(f"page{c}", [T2], F32, AT_PAGE + 8 * c) for c in range(PAGE_TILES)]

        def rows_of_tile(matrix, c):
            if c < GROUP_TILES:
                return matrix[c * P : (c + 1) * P, :]
            return matrix[GROUP:, :].rearrange("(p t) s -> t p s", t=PACK)[c - GROUP_TILES]

        def load_page(c):
            nc.sync.dma_start(out=page[c][:], in_=rows_of_tile(page0, c))

        def load_table(a, cols):
            nc.sync.dma_start(out=tab[a][:, cols], in_=tab_words[a].rearrange("p t i -> p (t i)").bitcast(I32)[:, cols])

        def load_wc(i):
            nc.sync.dma_start(out=wc_raw[i][:], in_=wc_rows[:, :, weight_pieces[i]])

        def load_scene(i):
            nc.sync.dma_start(out=scene_raw[i][:], in_=scene_rows[:, :, scene_pieces[i]])

        def load_wgs(i):
            nc.sync.dma_start(out=wgs_sb[i][:], in_=wgs[:, halves[i]])

        def load_w4(i):
            cols = weight_pieces[i]
            columns = w4_words.rearrange("a p c -> p a c")[:, :, 2 * cols.start : 2 * cols.stop]
            nc.sync.dma_start(out=w4[i][:].bitcast(I32), in_=columns.bitcast(I32))

        picked_rows = sbuf("picked_rows", [S], U8, AT_PICKED_ROWS)

        def move_scales(planes, rows):
            for q in (0, 2, 1, 3):
                nc.sync.dma_start(out=plane_rows(planes, q), in_=rows[32 * q : 32 * (q + 1) : 4].bitcast(I32))

        nc.sync.dma_start(picks[:], offs)
        load_wgs(0)
        load_table(0, slice(0, T // 4))
        nc.sync.dma_start(out=tab_scale_rows[0:P:4].bitcast(I32), in_=tab_scales.rearrange("a b t -> b a t").bitcast(I32))
        load_table(0, slice(T // 4, T))
        for i in range(2):
            nc.vector.tensor_copy(picked_rows[:, halves[i]], tab_scale_rows[:].indirect(entries(picks, halves[i])))
        load_scene(0)
        move_scales(picked_scale[0], picked_rows[:, halves[0]])
        load_wc(0)
        nc.sync.dma_start(out=w4_scale_rows[0:P:4].bitcast(I32), in_=w4_scales[:, :, GROUP:].rearrange("a b c -> b a c").bitcast(I32))
        nc.vector.tensor_copy(w4_scale_dealt[:].rearrange("p (t m) -> p t m", t=PACK),
                              w4_scale_rows[:].rearrange("p (m t) -> p t m", t=PACK))
        load_table(1, slice(0, T))
        load_w4(0)
        nc.sync.dma_start(slots[:], offs2)
        load_page(0)
        load_page(1)
        load_scene(1)
        load_scene(2)
        move_scales(picked_scale[1], picked_rows[:, halves[1]])
        load_wgs(1)
        load_wc(1)
        load_w4(1)
        load_page(2)
        load_wc(2)
        load_w4(2)
        load_page(3)
        move_scales(weight_scale[:, :, GROUP:], w4_scale_dealt)
        for c in range(GROUP_TILES, PAGE_TILES):
            load_page(c)

        bank = next_bank()
        nc.tensor.transpose(bank[:, 0:P], gain_rows[:], ident[:])
        nc.scalar.copy(gain_cols[:], bank[:, 0:GROUP_TILES])

        def times_gain(out, in_, column):
            nc.scalar.activation(out, in_, ACT.Copy, scale=column)

        factors = [sbuf(f"factors{c}", [S], F32, AT_FACTORS + 4 * c) for c in range(PAGE_TILES)]

        def natural_factors(c, cols):
            i = cols.start // BANK
            times_gain(factors[c][:, cols], wgs_sb[i][:, cols.start - i * BANK : cols.stop - i * BANK], gain_cols[:, c : c + 1])

        def turn_wgs(i, bank):
            turned_wgs = [sbuf(f"wgs_turned{i}{pair}", [2, PACK, QUADRANTS, 32], F32, AT_TURNED + 4 * (2 * i + pair)) for pair in range(2)]
            for b in range(4):
                nc.tensor.transpose(bank[:, b * P : (b + 1) * P], wgs_sb[i][:, b * P : (b + 1) * P], ident[:])
            for pair in range(2):
                rows = bank[:, 2 * pair * P : 2 * (pair + 1) * P].rearrange("j (b q t) -> j b t q", b=2, t=PACK)
                nc.scalar.copy(turned_wgs[pair][:], rows.unsqueeze(3).to_broadcast([P, 2, PACK, QUADRANTS, 32]))
            return turned_wgs

        def dealt_factors(turned_wgs, i, t):
            bank = next_bank()
            for b in range(4):
                block = turned_wgs[b // 2][:, b % 2, t].rearrange("j r q -> j (r q)")
                nc.tensor.transpose(bank[:, b * P : (b + 1) * P], block, ident[:])
            times_gain(factors[GROUP_TILES + t][:, halves[i]], bank[:], gain_dealt[:, t : t + 1])

        picked = sbuf("picked", [2, S], U32, AT_PICKED)
        nc.vector.tensor_copy(picked[:, 0, :], tab[0][:].bitcast(U32).indirect(picks[:]))

        def weave(woven, raw, copy):
            copy(woven.rearrange("p (c i) j -> p c j i", i=4), raw.rearrange("p j (c i) -> p c j i", i=4))

        def quantise(codes, scale, woven):
            nc.vector.quantize_mx(out=codes.bitcast(FP8X4), scales=scale, in_=woven[:].rearrange("p c j -> p (c j)"))

        def quantised(name, woven, first):
            width = woven.shape[1]
            codes = sbuf(name + "_codes", [width], U32, AT_CODES + first / 256)
            scale = sbuf(name + "_scale", [width], U8, AT_SCALES + first / 1024)
            quantise(codes[:], scale[:], woven)
            return codes, scale

        scene_q = sbuf("scene_codes", [S], U32, AT_CODES), sbuf("scene_scale", [S], U8, AT_SCALES)

        def quantise_scene(i, copy):
            cols = scene_pieces[i]
            woven = sbuf(f"scene_woven{i}", [cols.stop - cols.start, PACK], BF16, AT_WOVEN + 4 * min(i, 1))
            weave(woven[:], scene_raw[i][:], copy)
            quantise(scene_q[0][:, cols], scene_q[1][:, cols], woven)

        def woven_wc(i):
            cols = weight_pieces[i]
            return sbuf(f"wc_woven{i}", [cols.stop - cols.start, PACK], BF16, AT_WOVEN + 8 + cols.start / 128)

        def quantised_wc(i):
            woven = woven_wc(i)
            weave(woven[:], wc_raw[i][:], nc.scalar.copy)
            return quantised(f"wc{i}", woven, S + weight_pieces[i].start)

        quantise_scene(0, nc.vector.tensor_copy)
        wc_q = [quantised_wc(0)]
        for c in range(GROUP_TILES):
            natural_factors(c, halves[0])
        turned_wgs = turn_wgs(0, next_bank())
        for t in range(PACK):
            dealt_factors(turned_wgs, 0, t)
        for cols in quarters[:2] + halves[1:]:
            nc.vector.tensor_copy(picked[:, 1, cols], tab[1][:].bitcast(U32).indirect(entries(picks, cols)))

        def mx_pass(out, stationary, moving, start, stop):
            nc.tensor.matmul_mx(out=out, lhsT=stationary[0], lhsT_scale=stationary[1], rhs=moving[0], rhs_scale=moving[1],
                                start=start, stop=stop)

        def columns_of(operand, cols):
            return operand[0][:, cols].bitcast(FP8X4), operand[1][:, cols]

        w4_dealt = []

        def w4_operand(a, c):
            words, at = (w4_dealt[0], c * P - GROUP) if c >= GROUP_TILES else (w4[c // 2], c % 2 * P)
            return words[:, a, 2 * at : 2 * (at + P)].bitcast(FP4X4), weight_scale[:, a, c * P : (c + 1) * P]

        def wc_operand(c):
            piece = min(c // 2, 2)
            at = c * P - weight_pieces[piece].start
            return columns_of(wc_q[piece], slice(at, at + P))

        def table_passes(c, cols, sums, opening):
            i = cols.start // BANK
            within = slice(cols.start - i * BANK, cols.stop - i * BANK)
            for a in range(2):
                mx_pass(sums, w4_operand(a, c), (picked[:, a, cols].bitcast(FP8X4), picked_scale[i][:, a, within]),
                        opening and a == 0, not opening and a == 1)

        def scene_pass(c, cols, sums, opening):
            mx_pass(sums, wc_operand(c), columns_of(scene_q, cols), opening, not opening)

        def gelu_of_sums(c, cols, out, scene_first):
            sums = next_bank()[:, 0 : cols.stop - cols.start]
            if scene_first:
                scene_pass(c, cols, sums, True)
            table_passes(c, cols, sums, not scene_first)
            if not scene_first:
                scene_pass(c, cols, sums, False)
            nc.scalar.activation(out, sums, ACT.Gelu_apprx_tanh)

        hidden_at = {2: AT_SCENE, 3: AT_WC + 8, 4: AT_SCENE + 4, 5: AT_SCENE + 8, 6: AT_SCENE + 12, 7: AT_WC + 12}
        hidden = {}

        def make_hidden(c):
            hidden.update({c: sbuf(f"hidden{c}", [S], F32, hidden_at[c])})
            for cols in halves:
                gelu_of_sums(c, cols, hidden[c][:, cols], c > 2)

        def store_page(c):
            nc.sync.dma_start(out=rows_of_tile(out_1, c), in_=page[c][:])

        def scatter(c):
            nc.vector.tensor_tensor(page[c][:].indirect(slots[:]), hidden[c][:], factors[c][:], ALU.mult)

        def scatter_piece(c, cols, values):
            nc.vector.tensor_tensor(page[c][:].indirect(entries(slots, cols)), values, factors[c][:, cols], ALU.mult)

        def quarter_piece(c, q, at):
            values = sbuf(f"hidden{c}_{q}", [QUARTER], F32, at)
            gelu_of_sums(c, quarters[q], values[:], q < 2)
            scatter_piece(c, quarters[q], values[:])

        first = sbuf("hidden0_first", [BANK], F32, AT_FIRST)
        for cols in quarters[:2]:
            gelu_of_sums(0, cols, first[:, cols], True)
        scatter_piece(0, halves[0], first[:])
        quarter_piece(1, 0, AT_FIRST + 2)
        quantise_scene(1, nc.scalar.copy)
        quarter_piece(1, 1, AT_SCENE + 8)
        quantise_scene(2, nc.scalar.copy)
        natural_factors(0, quarters[2])
        quarter_piece(0, 2, AT_FIRST + 3)
        natural_factors(1, halves[1])
        quarter_piece(1, 2, AT_WOVEN + 6)
        wc_q.append(quantised_wc(1))
        natural_factors(0, quarters[3])
        for c in range(2):
            quarter_piece(c, 3, AT_WC + 4 + c)
        natural_factors(2, halves[1])
        make_hidden(2)
        natural_factors(3, halves[1])
        woven = woven_wc(2)
        nc.scalar.copy(woven[:].rearrange("p (t m) j -> p m j t", t=PACK), wc_raw[2][:].rearrange("p j (m t) -> p m j t", t=PACK))
        scatter(2)
        wc_q.append(quantised("wc2", woven, S + GROUP))
        make_hidden(3)
        w4_dealt.append(sbuf("w4_dealt", [2, 2 * GROUP], U8, AT_W4 + 3))
        nc.scalar.copy(w4_dealt[0][:].bitcast(U16).rearrange("p a (t m) -> p a t m", t=PACK),
                       w4[2][:].bitcast(U16).rearrange("p a (m t) -> p a t m", t=PACK))
        turned_wgs = turn_wgs(1, next_bank())
        for t in range(PACK):
            dealt_factors(turned_wgs, 1, t)
            make_hidden(GROUP_TILES + t)

        result = [sbuf(f"result{a}", [2, T2], F32, AT_TABLE + 1 + 16 * a) for a in range(2)]
        bias_rows = bias.rearrange("(n p) t -> p n t", p=P)
        out_rows = out_0.rearrange("(n p) t -> p n t", p=P)
        for a in range(2):
            nc.sync.dma_start(out=result[a][:], in_=bias_rows[:, 2 * a : 2 * a + 2, :])
        w8 = sbuf("w8", [2, N], I32, AT_FIRST)
        nc.sync.dma_start(out=w8[:], in_=w8_words.rearrange("a p c i -> p a (c i)").bitcast(I32))
        for q in range(QUADRANTS):
            nc.sync.dma_start(out=plane_rows(weight_scale[:, :, 0:N], q, 4),
                              in_=w8_scales[:, 4 * q : 4 * q + 4, :].rearrange("a q c -> q a c").bitcast(I32))

        for c in range(LAST_TILE):
            if c > 2:
                scatter(c)
            store_page(c)

        turned = sbuf("turned", [CHUNKS, 4, 2, 2 * P], BF16, AT_TURNED)
        for c in range(GROUP_TILES):
            for k in range(CHUNKS):
                bank = next_bank()
                for b in range(4):
                    nc.tensor.transpose(bank[:, b * P : (b + 1) * P], page[c][:, k * BANK + b * P : k * BANK + (b + 1) * P], ident[:])
                nc.scalar.copy(
                    turned[:, k, :, :, 64 * c : 64 * (c + 1)].rearrange("s b u (p e) -> s b u p e", e=2),
                    bank[:].rearrange("s (b p u e) -> s b u p e", b=4, u=2, e=2))

        def turn_back(k):
            words = turned[:, k].rearrange("s b u w -> s (b u w)").bitcast(F32)
            woven = sbuf(f"woven_page0{k}", [BANK, PACK], BF16, AT_WOVEN + 4 * k)
            woven_pairs = woven[:].rearrange("p s j -> p (s j)").bitcast(F32)
            for two_blocks in range(2):
                bank = next_bank()
                for bu in range(4):
                    at = (4 * two_blocks + bu) * P
                    nc.tensor.transpose(bank[:, bu * P : (bu + 1) * P], words[:, at : at + P], ident[:])
                nc.scalar.copy(
                    woven_pairs[:, two_blocks * BANK : (two_blocks + 1) * BANK].rearrange("p (b s u) -> p b s u", b=2, u=2),
                    bank[:].rearrange("p (b u s) -> p b s u", b=2, u=2))
            return woven

        woven_group0 = [turn_back(k) for k in range(CHUNKS)]
        pairs = [sbuf(f"pairs{k}", [2, BANK, 2], BF16, AT_TURNED + 4 * k) for k in range(CHUNKS)]

        def round_chunk(c, k):
            t = c - GROUP_TILES
            nc.scalar.copy(pairs[k][:, t // 2, :, t % 2], page[c][:, chunks[k]])

        for c in range(GROUP_TILES, LAST_TILE):
            for k in range(CHUNKS):
                round_chunk(c, k)
        scatter(LAST_TILE)
        store_page(LAST_TILE)

        page_codes = [sbuf(f"page_codes{g}", [T2], I32, at) for g, at in enumerate((AT_FACTORS, AT_PICKED))]
        page_scale = [sbuf(f"page_scale{g}", [T2], U8, AT_PAGE_SCALE + 2 * g) for g in range(2)]
        page_halves = [slice(0, T2 // 2), slice(T2 // 2, T2)]

        def store_codes(g, cols):
            nc.sync.dma_start(out=out_2[g].rearrange("p m t -> p (m t)").bitcast(I32)[:, cols], in_=page_codes[g][:, cols])

        def store_scales(g):
            for r in range(4):
                nc.sync.dma_start(out=out_3[g, r : 16 : 4, :].bitcast(I32), in_=page_scale[g][r : P : 32].bitcast(I32))

        def quantise_early(k):
            quantise(page_codes[0][:, chunks[k]], page_scale[0][:, chunks[k]], woven_group0[k])

        def quantise_late(k):
            round_chunk(LAST_TILE, k)
            woven = sbuf(f"woven_page1{k}", [BANK, PACK], BF16, AT_WOVEN + 4 * k)
            words = woven[:].rearrange("p s j -> p (s j)").bitcast(U32).rearrange("p (s u) -> p s u", u=2)
            nc.scalar.copy(words, pairs[k][:].rearrange("p u s e -> p u (s e)").bitcast(U32).rearrange("p u s -> p s u"))
            quantise(page_codes[1][:, chunks[k]], page_scale[1][:, chunks[k]], woven)

        sums = [(n, k) for k in (0, 1) for n in range(BLOCKS)] + [(n, k) for n in range(BLOCKS) for k in (2, 3)]

        def bank_of(n, k):
            return banks[sums.index((n, k)) % len(banks)]

        def second_pass(n, k, g):
            mx_pass(bank_of(n, k)[:],
                    (w8[:, g, n * P : (n + 1) * P].bitcast(FP8X4), weight_scale[4:P, g, n * P : (n + 1) * P]),
                    (page_codes[g][:, chunks[k]].bitcast(FP8X4), page_scale[g][:, chunks[k]]), g == 0, g == 1)

        def add_bias(n, k):
            values = result[n // 2][:, n % 2, chunks[k]]
            nc.vector.tensor_tensor(values, bank_of(n, k)[:], values, ALU.add)

        def finish(n, k):
            for g in range(2):
                second_pass(n, k, g)
            add_bias(n, k)

        def store_result(n, cols):
            nc.sync.dma_start(out=out_rows[:, n, cols], in_=result[n // 2][:, n % 2, cols])

        later_chunks = slice(BANK, T2)
        for k in range(CHUNKS):
            quantise_early(k)
        for cols in page_halves:
            store_codes(0, cols)
        store_scales(0)
        for n in range(BLOCKS):
            second_pass(n, 0, 0)
        quantise_late(0)
        store_codes(1, chunks[0])
        for n in range(BLOCKS):
            second_pass(n, 0, 1)
        for n in range(BLOCKS):
            add_bias(n, 0)
            store_result(n, chunks[0])
            if n == 0:
                quantise_late(1)
        for n in range(BLOCKS):
            for g in range(2):
                second_pass(n, 1, g)
        quantise_late(2)
        add_bias(0, 1)
        quantise_late(3)
        store_codes(1, later_chunks)
        store_scales(1)
        for n in range(1, BLOCKS):
            staged = sbuf(f"staged{n}", [BANK], F32, (AT_TURNED + 12, AT_TURNED + 14, AT_WOVEN + 12)[n - 1])
            nc.scalar.copy(staged[:], bank_of(n, 1)[:])
            values = result[n // 2][:, n % 2, chunks[1]]
            nc.gpsimd.tensor_tensor(values, staged[:], values, ALU.add)
        for n, k in sums[2 * BLOCKS :]:
            finish(n, k)
            if (n, k) == sums[-2]:
                store_result(n, slice(BANK, T2 - BANK))
            elif (n, k) == sums[-1]:
                store_result(n, chunks[k])
            elif k == CHUNKS - 1:
                store_result(n, later_chunks)
